import numpy as np
import ml_dtypes


def mxq(x, axis, fmt="e4m3"):
    dtype, down = {"e4m3": (ml_dtypes.float8_e4m3fn, 7), "e5m2": (ml_dtypes.float8_e5m2, 14)}[fmt]
    v = np.moveaxis(np.asarray(x, np.float32).astype(ml_dtypes.bfloat16).astype(np.float64), axis, -1)
    blocks = v.reshape(v.shape[:-1] + (-1, 32))
    amax = np.abs(blocks).max(-1, keepdims=True)
    byte = np.maximum(np.where(amax > 0, np.frexp(amax)[1] - 1 + 127, 0) - down, 1)
    scale = np.exp2(byte - 127.0)
    codes = (blocks / scale).astype(np.float32).astype(dtype).astype(np.float64)
    return np.moveaxis((codes * scale).reshape(v.shape), -1, axis)


WIDE = False


def mx_kscale(k):
    if not WIDE:
        return np.ones(k)
    levels = np.array([10, -10, 5, -5, 0])
    if k % 512:
        return np.exp2(np.random.permutation(np.resize(levels, k // 32))).repeat(32)
    a = np.empty((k // 512, 16))
    for p in range(k // 512):
        a[p, :8] = np.random.permutation(np.resize(levels, 8))
        for g in range(8):
            far = levels[np.abs(levels - a[p, g]) >= 10]
            a[p, g + 8] = far[np.random.randint(len(far))]
    return np.exp2(a.ravel()).repeat(32)


def f64(x):
    return np.asarray(x).astype(np.float64)


def striped(idx):
    return np.tile(idx.reshape(-1, 16).T, (8, 1)).astype(np.uint16)


def unstriped(offs):
    return offs[:16].T.reshape(-1).astype(np.int64)


E2M1 = np.array([0.0, 0.5, 1.0, 1.5, 2.0, 3.0, 4.0, 6.0, -0.0, -0.5, -1.0, -1.5, -2.0, -3.0, -4.0, -6.0])


def pack_weight(w, fmt):
    k, n = w.shape
    w = f64(np.asarray(w, np.float32).astype(ml_dtypes.bfloat16)).reshape(k // 32, 32, n)
    amax = np.abs(w).max(1)
    if fmt == "e4m3":
        byte = np.frexp(amax)[1] - 1 + 127 - 7
    else:
        mant, ex = np.frexp(amax / 6.0)
        byte = np.where(mant > 0.5, ex, ex - 1) + 127
    byte = np.clip(np.where(amax > 0, byte, 1), 1, 254)
    scaled = (w * np.exp2(127.0 - byte)[:, None, :]).reshape(k, n).astype(np.float32)
    by_word = np.ascontiguousarray(scaled.reshape(k // 512, 128, 4, n).transpose(0, 1, 3, 2))
    if fmt == "e4m3":
        words = by_word.astype(ml_dtypes.float8_e4m3fn).view(np.uint8)
    else:
        c = by_word.astype(ml_dtypes.float4_e2m1fn).view(np.uint8) & 0xF
        words = (c[..., 0::2] | (c[..., 1::2] << 4)).reshape(k // 512, 128, 2 * n)
    return np.ascontiguousarray(words), np.ascontiguousarray(byte.astype(np.uint8).reshape(k // 512, 16, n))


def unpack_weight(words, scales, fmt):
    g, _, n = scales.shape
    words = np.ascontiguousarray(words).reshape(g, 128, n, -1)
    if fmt == "e4m3":
        vals = words.view(ml_dtypes.float8_e4m3fn).astype(np.float64)
    else:
        nib = np.empty((g, 128, n, 4), np.uint8)
        nib[..., 0::2] = words & 0xF
        nib[..., 1::2] = words >> 4
        vals = E2M1[nib]
    vals = vals * np.repeat(np.exp2(scales.astype(np.float64) - 127.0), 8, axis=1)[..., None]
    return vals.transpose(0, 1, 3, 2).reshape(g * 512, n)


def sigmoid(v):
    return 1.0 / (1.0 + np.exp(-np.maximum(v, -700.0)))


K, T, E, C, H, N = 1024, 512, 8, 256, 512, 128
TOP = 4


def by_expert(wq, xq):
    return np.concatenate([wq[e].T @ xq[:, e * C:(e + 1) * C] for e in range(E)], axis=1)


def setup_inputs():
    n = np.random.standard_normal
    s = mx_kscale(K)[:, None]
    u = mx_kscale(H)
    deal = np.repeat(np.arange(E), C).reshape(TOP, T)[:, np.random.permutation(T)]
    deal = np.take_along_axis(deal, np.argsort(np.random.rand(TOP, T), axis=0), axis=0)
    for _ in range(8):
        s_, t_ = np.random.permutation(T).reshape(2, -1); r = np.random.randint(TOP, size=T // 2); x, y = deal[r, s_].copy(), deal[r, t_].copy()
        ok = ~((deal[:, s_] == y).any(0) | (deal[:, t_] == x).any(0)); deal[r[ok], s_[ok]] = y[ok]; deal[r[ok], t_[ok]] = x[ok]
    order = np.lexsort((np.random.rand(TOP * T), deal.reshape(-1)))
    slot_token = order % T; pos = np.empty(TOP * T, np.int64); pos[order] = np.arange(TOP * T); pos = pos.reshape(TOP, T)
    g = np.random.uniform(0.5, 1.5, (TOP, T)); g = g / g.sum(0)
    w1 = [pack_weight(m, "e2m1") for m in n((E, K, H)) / np.sqrt(K) / s[None]]
    w3 = [pack_weight(m, "e2m1") for m in n((E, K, H)) / np.sqrt(K) / s[None] * u[None, None, :]]
    w2 = [pack_weight(m, "e2m1") for m in n((E, H, N)) / np.sqrt(H) / u[None, :, None]]
    return {
        "xT": (n((K, T)) * s).astype(np.float32),
        "w1_words": np.stack([m[0] for m in w1]),
        "w1_scales": np.stack([m[1] for m in w1]),
        "w3_words": np.stack([m[0] for m in w3]),
        "w3_scales": np.stack([m[1] for m in w3]),
        "w2_words": np.stack([m[0] for m in w2]),
        "w2_scales": np.stack([m[1] for m in w2]),
        "gate": np.stack([np.tile(r, (N, 1)) for r in g]).astype(np.float32),
        "offs": striped(slot_token),
        "pos1": striped(pos[0]),
        "pos2": striped(pos[1]),
        "pos3": striped(pos[2]),
        "pos4": striped(pos[3]),
    }


def reference(xT, w1_words, w1_scales, w3_words, w3_scales, w2_words, w2_scales, gate, offs, pos1, pos2, pos3, pos4):
    idx = unstriped(offs)
    w1 = np.stack([unpack_weight(w1_words[e], w1_scales[e], "e2m1") for e in range(E)])
    w3 = np.stack([unpack_weight(w3_words[e], w3_scales[e], "e2m1") for e in range(E)])
    w2 = np.stack([unpack_weight(w2_words[e], w2_scales[e], "e2m1") for e in range(E)])
    xq = mxq(f64(xT)[:, idx], 0, "e4m3")
    h = sigmoid(by_expert(w1, xq))
    h = h * by_expert(w3, xq)
    y = by_expert(w2, mxq(h, 0, "e4m3"))
    return sum(f64(gate[r]) * y[:, unstriped(p)] for r, p in enumerate((pos1, pos2, pos3, pos4)))

@@ -1,0 +1,278 @@
+from contextlib import ExitStack
+
+import concourse.mybir as mybir
+from concourse.masks import make_identity
+
+F32 = mybir.dt.float32
+BF16 = mybir.dt.bfloat16
+I32 = mybir.dt.int32
+U32 = mybir.dt.uint32
+U16 = mybir.dt.uint16
+U8 = mybir.dt.uint8
+FP8X4 = mybir.dt.float8_e4m3fn_x4
+FP4X4 = mybir.dt.float4_e2m1fn_x4
+SIGMOID = mybir.ActivationFunctionType.Sigmoid
+MULT = mybir.AluOpType.mult
+ADD = mybir.AluOpType.add
+
+P = 128
+K, T, E, C, H, N, TOP = 1024, 512, 8, 256, 512, 128, 4
+SLOTS = E * C
+PASSES = K // 512
+FLOPS = 2 * SLOTS * (2 * K * H + H * N)
+
+RING = 3
+EARLY = 3
+PIECES = ((0,), (1, 2), (3, 4), (5, 6), (7,))
+AHEAD = 3
+WINDOW = 2 * T
+
+
+def tile_moe_tk_glu_sigmoid_kernel(
+    tc, xT, w1_words, w1_scales, w3_words, w3_scales, w2_words, w2_scales, gate, offs, pos1, pos2, pos3, pos4, out
+):
+    nc = tc.nc
+    with ExitStack() as ctx:
+        lists = ctx.enter_context(tc.tile_pool(name="lists", bufs=1))
+        keep = ctx.enter_context(tc.tile_pool(name="keep", bufs=1))
+        ring = ctx.enter_context(tc.tile_pool(name="ring", bufs=RING))
+        gathered = ctx.enter_context(tc.tile_pool(name="gathered", bufs=AHEAD))
+        gathered_0 = ctx.enter_context(tc.tile_pool(name="gathered_0", bufs=AHEAD - 1))
+        work = ctx.enter_context(tc.tile_pool(name="work", bufs=4))
+        psum = ctx.enter_context(tc.psum_pool(name="psum", bufs=3))
+        psum_2 = ctx.enter_context(tc.psum_pool(name="psum_2", bufs=1))
+
+        offs_t = lists.tile([P, SLOTS // 16], U16, name="offs_t")
+        pos_t = [lists.tile([P, T // 16], U16, name=f"pos{r}_t") for r in range(TOP)]
+
+        x_raw = [keep.tile([P, 4, T], F32, name=f"x_raw{s}", align_bytes=64) for s in range(PASSES)]
+        x_bf = [keep.tile([P, T, 4], BF16, name=f"x_bf{s}", align_bytes=64) for s in range(PASSES)]
+        shifted = keep.tile([P, AHEAD, 2 * C], U8, name="shifted", align_bytes=64)
+        x_codes = [keep.tile([P, WINDOW], U32, name=f"x_codes{s}", align_bytes=64) for s in range(PASSES)]
+        x_bytes = keep.tile([P, WINDOW], U8, name="x_bytes", align_bytes=64)
+        early_scales = [keep.tile([P, EARLY, PASSES, H], U8, name=f"early_scales{m}", align_bytes=64) for m in range(2)]
+        y_t = keep.tile([P, SLOTS], F32, name="y_t", align_bytes=64)
+        out_t = keep.tile([P, T], F32, name="out_t", align_bytes=64)
+        ident = keep.tile([P, P], F32, name="ident", align_bytes=64)
+        warm = keep.tile([P, 2], F32, name="warm", align_bytes=64)
+
+        nc.sync.dma_start(x_raw[0][:], xT[0:512, :].rearrange("(p j) w -> p j w", j=4))
+        nc.sync.dma_start(offs_t[:], offs)
+        nc.sync.dma_start(x_raw[1][:], xT[512:1024, :].rearrange("(p j) w -> p j w", j=4))
+
+        nc.vector.memset(warm[:], 0.0)
+        nc.scalar.activation(warm[:, 0:1], warm[:, 1:2], SIGMOID)
+        for t in early_scales:
+            nc.vector.memset(t[:].bitcast(I32), 0)
+        for t in x_codes:
+            nc.vector.memset(t[:, T:WINDOW].bitcast(I32), 0)
+        nc.gpsimd.memset(x_bytes[:], 0)
+        nc.gpsimd.memset(shifted[:].bitcast(I32), 0)
+        make_identity(nc, ident[:])
+
+        def load_scales(t, src, e0, e1, queue):
+            view = src.bitcast(I32).rearrange("e s q i -> q (e s) i")
+            for quad in range(4):
+                queue.dma_start(
+                    t[32 * quad : 32 * quad + 4].bitcast(I32).rearrange("q e s i -> q (e s) i"),
+                    view[4 * quad : 4 * quad + 4, e0 * PASSES : e1 * PASSES, :],
+                )
+
+        w_tiles = {}
+        gates = {}
+
+        def load_ring(i):
+            if i < E:
+                w = ring.tile([P, 2, PASSES, 2 * H], U8, name="w", align_bytes=64)
+                for m, src in enumerate((w1_words, w3_words)):
+                    nc.sync.dma_start(w[:, m].bitcast(I32), src.bitcast(I32)[i].rearrange("s p c -> p s c"))
+                w_tiles[i] = w
+            elif i < E + 2:
+                r = 2 * (i - E)
+                g = ring.tile([P, 2, T], F32, name="w", align_bytes=64)
+                nc.sync.dma_start(g[:], gate[r : r + 2].rearrange("r p t -> p r t"))
+                gates[r] = g[:, 0]
+                gates[r + 1] = g[:, 1]
+
+        for t, src in zip(early_scales, (w1_scales, w3_scales)):
+            load_scales(t, src, 0, EARLY, nc.sync)
+        load_ring(0)
+        load_ring(1)
+        load_ring(2)
+
+        def cast(s, a, b, engine_copy):
+            engine_copy(x_bf[s][:, a:b, :], x_raw[s][:, :, a:b].rearrange("p j w -> p w j"))
+
+        def quantize_tokens(s):
+            nc.vector.quantize_mx(
+                out=x_codes[s][:, 0:T].bitcast(FP8X4),
+                scales=x_bytes[4 * s : P, 0:T],
+                in_=x_bf[s][:].rearrange("p w j -> p (w j)"),
+            )
+
+        s_codes = {}
+        s_bytes = {}
+
+        def gather_bytes(i, queue):
+            experts = PIECES[i]
+            n = len(experts) * C
+            a = experts[0] * C
+            both = gathered.tile([P, n], U8, name="s_bytes", align_bytes=64)
+            nc.vector.tensor_copy(both[:], x_bytes[:].indirect(offs_t[:, a // 16 : (a + n) // 16]))
+            queue.dma_start(shifted[0 : P - 4, i % AHEAD, 0:n].bitcast(I32), both[4:P, :].bitcast(I32))
+            for x, e in enumerate(experts):
+                s_bytes[0, e] = both[:, x * C : (x + 1) * C]
+                s_bytes[1, e] = shifted[:, i % AHEAD, x * C : (x + 1) * C]
+
+        def gather_codes(s, i):
+            experts = PIECES[i]
+            n = len(experts) * C
+            a = experts[0] * C
+            codes = (gathered_0 if s == 0 else gathered).tile([P, n], U32, name=f"s_codes{s}", align_bytes=64)
+            nc.vector.tensor_copy(codes[:], x_codes[s][:].indirect(offs_t[:, a // 16 : (a + n) // 16]))
+            for x, e in enumerate(experts):
+                s_codes[s, e] = codes[:, x * C : (x + 1) * C]
+
+        cast(0, 320, 512, nc.scalar.copy)
+        cast(0, 0, 320, nc.vector.tensor_copy)
+        quantize_tokens(0)
+        gather_codes(0, 0)
+        cast(1, 208, 512, nc.scalar.copy)
+        cast(1, 0, 208, nc.vector.tensor_copy)
+        quantize_tokens(1)
+        gather_bytes(0, nc.scalar)
+        gather_codes(1, 0)
+        for i in range(1, AHEAD):
+            gather_bytes(i, nc.scalar if i == 1 else nc.sync)
+            if i < AHEAD - 1:
+                gather_codes(0, i)
+            gather_codes(1, i)
+
+        late_scales = []
+        for m, src in enumerate((w1_scales, w3_scales)):
+            t = keep.tile([P, E - EARLY, PASSES, H], U8, name=f"x_raw{m}", align_bytes=64)
+            nc.gpsimd.memset(t[:].bitcast(I32), 0)
+            load_scales(t, src, EARLY, E, nc.gpsimd)
+            late_scales.append(t)
+        w2_all = keep.tile([P, E, 3 * N], U8, name="x_bf1", align_bytes=64)
+        w2_t = w2_all[:].rearrange("p e c -> p (e c)")[:, 0 : E * 2 * N].rearrange("p (e c) -> p e c", e=E)
+        w2_s = w2_all[:].rearrange("p e c -> p (e c)")[:, E * 2 * N :].rearrange("p (e c) -> p e c", e=E)
+        nc.gpsimd.memset(w2_s.bitcast(I32), 0)
+        nc.sync.dma_start(w2_t.bitcast(I32), w2_words.bitcast(I32).rearrange("e s p c -> p (e s) c"))
+        for quad in range(4):
+            nc.sync.dma_start(
+                w2_s[32 * quad : 32 * quad + 4].bitcast(I32),
+                w2_scales.bitcast(I32).rearrange("e s q i -> q (e s) i")[4 * quad : 4 * quad + 4],
+            )
+
+        h_tiles = {}
+
+        def multiply_1(e, st):
+            slots = slice(st * P, (st + 1) * P)
+            banks = []
+            for m, name in enumerate(("bank_a", "bank_b")):
+                scales = early_scales[m][:, e] if e < EARLY else late_scales[m][:, e - EARLY]
+                bank = psum.tile([P, H], F32, name=name)
+                for s in range(PASSES):
+                    nc.tensor.matmul_mx(
+                        out=bank[:],
+                        lhsT=s_codes[s, e][:, slots].bitcast(FP8X4),
+                        lhsT_scale=s_bytes[s, e][:, slots],
+                        rhs=w_tiles[e][:, m, s, :].bitcast(FP4X4),
+                        rhs_scale=scales[:, s, :],
+                        start=(s == 0),
+                        stop=(s == PASSES - 1),
+                    )
+                banks.append(bank)
+            return banks
+
+        def activate(e, st, banks):
+            sig = work.tile([P, H], F32, name="sig")
+            nc.scalar.activation(sig[:], banks[0][:], SIGMOID)
+            h = work.tile([P, H], BF16, name="h", align_bytes=64)
+            nc.vector.tensor_tensor(h[:], banks[1][:], sig[:], MULT)
+            h_tiles[e, st] = h
+
+        def turn(e, tiles, engine_copy):
+            n = len(tiles) * P
+            turned = psum_2.tile([P, 2, n], F32, name="turned")
+            for x, st in enumerate(tiles):
+                words = h_tiles[e, st][:].bitcast(F32)
+                for u in range(2):
+                    nc.tensor.transpose(turned[:, u, x * P : (x + 1) * P], words[:, u::2], ident[:])
+            h_bf = work.tile([P, 4 * n], BF16, name="h_bf", align_bytes=64)
+            engine_copy(h_bf[:].bitcast(F32).rearrange("p (r u) -> p r u", u=2), turned[:].rearrange("p u r -> p r u"))
+            return h_bf
+
+        def quantize_hidden(h_bf):
+            n = h_bf.shape[1] // 4
+            h_codes = work.tile([P, n], U32, name="h_codes", align_bytes=64)
+            h_bytes = work.tile([P, n], U8, name="h_bytes", align_bytes=64)
+            nc.vector.quantize_mx(out=h_codes[:].bitcast(FP8X4), scales=h_bytes[:], in_=h_bf[:])
+            return h_codes, h_bytes
+
+        def multiply_2(e, target, h_codes, h_bytes):
+            nc.tensor.matmul_mx(
+                out=target,
+                lhsT=w2_t[:, e, :].bitcast(FP4X4),
+                lhsT_scale=w2_s[:, e, :],
+                rhs=h_codes[:].bitcast(FP8X4),
+                rhs_scale=h_bytes[:],
+                start=True,
+                stop=True,
+            )
+
+        quantized = {}
+        y_banks = {}
+
+        def second_layer(e):
+            if e % 2 == 0:
+                y_bank = psum_2.tile([P, 2 * C], F32, name="y_bank")
+                y_banks[e] = y_bank
+                multiply_2(e, y_bank[:, 0:C], *quantized[e])
+            else:
+                y_bank = y_banks[e - 1]
+                multiply_2(e, y_bank[:, C : 2 * C], *quantized[e])
+                nc.scalar.copy(y_t[:, (e - 1) * C : (e + 1) * C], y_bank[:])
+
+        last = E - 1
+        for e in range(E):
+            activate(e, 0, multiply_1(e, 0))
+            activate(e, 1, multiply_1(e, 1))
+            if e >= 2:
+                second_layer(e - 2)
+            if e >= 1:
+                h_bf = turn(e - 1, (0, 1), nc.scalar.copy)
+                quantized[e - 1] = quantize_hidden(h_bf)
+            load_ring(e + RING)
+            if e % 2 == 0:
+                i = e // 2 + AHEAD
+                if i - 1 < len(PIECES):
+                    gather_codes(0, i - 1)
+                if i < len(PIECES):
+                    gather_bytes(i, nc.sync)
+                    gather_codes(1, i)
+            if e == 3:
+                for r, src in enumerate((pos1, pos2, pos3, pos4)):
+                    nc.sync.dma_start(pos_t[r][:], src)
+
+        first = quantize_hidden(turn(last, (0,), nc.scalar.copy))
+        second_layer(last - 1)
+        y_bank = y_banks[last - 1]
+        multiply_2(last, y_bank[:, C : C + P], *first)
+        nc.scalar.copy(y_t[:, (last - 1) * C : last * C + P], y_bank[:, 0 : C + P])
+        second = quantize_hidden(turn(last, (1,), nc.vector.tensor_copy))
+        y_last = psum.tile([P, P], F32, name="bank_a")
+        multiply_2(last, y_last[:], *second)
+        nc.vector.tensor_copy(y_t[:, last * C + P :], y_last[:])
+
+        parts = keep.tile([P, TOP, T], F32, name="parts", align_bytes=64)
+        for r in range(TOP):
+            nc.vector.tensor_tensor(parts[:, r], y_t[:].indirect(pos_t[r][:]), gates[r], MULT)
+        pairs = keep.tile([P, 2, T], F32, name="pairs", align_bytes=64)
+        nc.vector.tensor_tensor(pairs[:], parts[:, 0:2], parts[:, 2:4], ADD)
+        half = T // 2
+        for hf in range(2):
+            cols = slice(hf * half, (hf + 1) * half)
+            nc.vector.tensor_tensor(out_t[:, cols], pairs[:, 0, cols], pairs[:, 1, cols], ADD)
+            nc.sync.dma_start(out[:, cols], out_t[:, cols])

@@ -21,11 +21,9 @@ SLOTS = E * C
 PASSES = K // 512
 FLOPS = 2 * SLOTS * (2 * K * H + H * N)
 
-RING = 3
-EARLY = 3
-PIECES = ((0,), (1, 2), (3, 4), (5, 6), (7,))
-AHEAD = 3
-WINDOW = 2 * T
+KB = 1024
+VECTOR_CAST = (344, 176)
+BYTE_PIECES = ((0, 1), (2, 3), (4, 5), (6, 7))
 
 
 def tile_moe_tk_glu_sigmoid_kernel(
@@ -34,23 +32,22 @@ def tile_moe_tk_glu_sigmoid_kernel(
     nc = tc.nc
     with ExitStack() as ctx:
         lists = ctx.enter_context(tc.tile_pool(name="lists", bufs=1))
+        places = ctx.enter_context(tc.tile_pool(name="places", bufs=1))
         keep = ctx.enter_context(tc.tile_pool(name="keep", bufs=1))
-        ring = ctx.enter_context(tc.tile_pool(name="ring", bufs=RING))
-        gathered = ctx.enter_context(tc.tile_pool(name="gathered", bufs=AHEAD))
-        gathered_0 = ctx.enter_context(tc.tile_pool(name="gathered_0", bufs=AHEAD - 1))
+        gathered = ctx.enter_context(tc.tile_pool(name="gathered", bufs=2))
         work = ctx.enter_context(tc.tile_pool(name="work", bufs=4))
-        psum = ctx.enter_context(tc.psum_pool(name="psum", bufs=3))
-        psum_2 = ctx.enter_context(tc.psum_pool(name="psum_2", bufs=1))
+        psum = ctx.enter_context(tc.psum_pool(name="psum", bufs=1))
+
+        def placed(shape, dtype, name, offset):
+            return places.tile(shape, dtype, name=name, align_bytes=64, offset=offset)
 
         offs_t = lists.tile([P, SLOTS // 16], U16, name="offs_t")
         pos_t = [lists.tile([P, T // 16], U16, name=f"pos{r}_t") for r in range(TOP)]
 
-        x_raw = [keep.tile([P, 4, T], F32, name=f"x_raw{s}", align_bytes=64) for s in range(PASSES)]
-        x_bf = [keep.tile([P, T, 4], BF16, name=f"x_bf{s}", align_bytes=64) for s in range(PASSES)]
-        shifted = keep.tile([P, AHEAD, 2 * C], U8, name="shifted", align_bytes=64)
-        x_codes = [keep.tile([P, WINDOW], U32, name=f"x_codes{s}", align_bytes=64) for s in range(PASSES)]
-        x_bytes = keep.tile([P, WINDOW], U8, name="x_bytes", align_bytes=64)
-        early_scales = [keep.tile([P, EARLY, PASSES, H], U8, name=f"early_scales{m}", align_bytes=64) for m in range(2)]
+        x_raw = [placed([P, 4, T], F32, f"x_raw{s}", 8 * KB * s) for s in range(PASSES)]
+        x_bf = [placed([P, T, 4], BF16, f"x_bf{s}", 16 * KB + 4 * KB * s) for s in range(PASSES)]
+        x_codes = [keep.tile([P, T], U32, name=f"x_codes{s}", align_bytes=64) for s in range(PASSES)]
+        x_bytes = keep.tile([P, 2 * T], U8, name="x_bytes", align_bytes=64)
         y_t = keep.tile([P, SLOTS], F32, name="y_t", align_bytes=64)
         out_t = keep.tile([P, T], F32, name="out_t", align_bytes=64)
         ident = keep.tile([P, P], F32, name="ident", align_bytes=64)
@@ -58,148 +55,147 @@ def tile_moe_tk_glu_sigmoid_kernel(
 
         nc.sync.dma_start(x_raw[0][:], xT[0:512, :].rearrange("(p j) w -> p j w", j=4))
         nc.sync.dma_start(offs_t[:], offs)
+        for r, src in enumerate((pos1, pos2, pos3, pos4)):
+            nc.sync.dma_start(pos_t[r][:], src)
         nc.sync.dma_start(x_raw[1][:], xT[512:1024, :].rearrange("(p j) w -> p j w", j=4))
 
+        w_scales = {}
+        w_tiles = {}
+
+        def load_scale_rows(t, view):
+            for r in range(4):
+                nc.sync.dma_start(t[r:P:32], view[r:16:4])
+
+        def load_scales(e0, e1, offsets, label, clear):
+            for m, src in enumerate((w1_scales, w3_scales)):
+                t = placed([P, (e1 - e0) * PASSES, H], U8, f"scales_{label}{m}", offsets[m])
+                if clear:
+                    nc.vector.memset(t[:].bitcast(I32), 0)
+                view = src.bitcast(I32).rearrange("e s q i -> q (e s) i")[:, e0 * PASSES : e1 * PASSES, :]
+                load_scale_rows(t[:].bitcast(I32), view)
+                for e in range(e0, e1):
+                    w_scales[m, e] = t[:, (e - e0) * PASSES : (e - e0 + 1) * PASSES, :]
+
+        def load_weights(e, offset):
+            w = placed([P, 2, PASSES, 2 * H], U8, f"w{e}", offset)
+            for m, src in enumerate((w1_words, w3_words)):
+                nc.sync.dma_start(w[:, m].bitcast(I32), src.bitcast(I32)[e].rearrange("s p c -> p s c"))
+            w_tiles[e] = w
+
+        first_weights = 30 * KB
+        w_places = {1: 38 * KB, 2: 17 * KB + 256, 3: first_weights + 3 * KB}
+        load_scales(0, 3, (24 * KB, 27 * KB), "a", True)
+        load_weights(0, first_weights)
+        load_weights(1, w_places[1])
+
+        nc.vector.memset(x_bytes[:].bitcast(I32), 0)
         nc.vector.memset(warm[:], 0.0)
         nc.scalar.activation(warm[:, 0:1], warm[:, 1:2], SIGMOID)
-        for t in early_scales:
-            nc.vector.memset(t[:].bitcast(I32), 0)
-        for t in x_codes:
-            nc.vector.memset(t[:, T:WINDOW].bitcast(I32), 0)
-        nc.gpsimd.memset(x_bytes[:], 0)
-        nc.gpsimd.memset(shifted[:].bitcast(I32), 0)
         make_identity(nc, ident[:])
 
-        def load_scales(t, src, e0, e1, queue):
-            view = src.bitcast(I32).rearrange("e s q i -> q (e s) i")
-            for quad in range(4):
-                queue.dma_start(
-                    t[32 * quad : 32 * quad + 4].bitcast(I32).rearrange("q e s i -> q (e s) i"),
-                    view[4 * quad : 4 * quad + 4, e0 * PASSES : e1 * PASSES, :],
-                )
-
-        w_tiles = {}
-        gates = {}
-
-        def load_ring(i):
-            if i < E:
-                w = ring.tile([P, 2, PASSES, 2 * H], U8, name="w", align_bytes=64)
-                for m, src in enumerate((w1_words, w3_words)):
-                    nc.sync.dma_start(w[:, m].bitcast(I32), src.bitcast(I32)[i].rearrange("s p c -> p s c"))
-                w_tiles[i] = w
-            elif i < E + 2:
-                r = 2 * (i - E)
-                g = ring.tile([P, 2, T], F32, name="w", align_bytes=64)
-                nc.sync.dma_start(g[:], gate[r : r + 2].rearrange("r p t -> p r t"))
-                gates[r] = g[:, 0]
-                gates[r + 1] = g[:, 1]
-
-        for t, src in zip(early_scales, (w1_scales, w3_scales)):
-            load_scales(t, src, 0, EARLY, nc.sync)
-        load_ring(0)
-        load_ring(1)
-        load_ring(2)
-
         def cast(s, a, b, engine_copy):
-            engine_copy(x_bf[s][:, a:b, :], x_raw[s][:, :, a:b].rearrange("p j w -> p w j"))
+            engine_copy(
+                x_bf[s][:, a:b, :].rearrange("p (c i) j -> p c j i", i=4),
+                x_raw[s][:, :, a:b].rearrange("p j (c i) -> p c j i", i=4),
+            )
 
         def quantize_tokens(s):
+            cast(s, VECTOR_CAST[s], T, nc.scalar.copy)
+            cast(s, 0, VECTOR_CAST[s], nc.vector.tensor_copy)
             nc.vector.quantize_mx(
-                out=x_codes[s][:, 0:T].bitcast(FP8X4),
-                scales=x_bytes[4 * s : P, 0:T],
+                out=x_codes[s][:].bitcast(FP8X4),
+                scales=x_bytes[4 * (1 - s) : P, 0:T],
                 in_=x_bf[s][:].rearrange("p w j -> p (w j)"),
             )
 
         s_codes = {}
         s_bytes = {}
 
-        def gather_bytes(i, queue):
-            experts = PIECES[i]
+        def gather_bytes(experts, name):
             n = len(experts) * C
             a = experts[0] * C
-            both = gathered.tile([P, n], U8, name="s_bytes", align_bytes=64)
+            both = gathered.tile([P, n], U8, name=name, align_bytes=64)
             nc.vector.tensor_copy(both[:], x_bytes[:].indirect(offs_t[:, a // 16 : (a + n) // 16]))
-            queue.dma_start(shifted[0 : P - 4, i % AHEAD, 0:n].bitcast(I32), both[4:P, :].bitcast(I32))
             for x, e in enumerate(experts):
-                s_bytes[0, e] = both[:, x * C : (x + 1) * C]
-                s_bytes[1, e] = shifted[:, i % AHEAD, x * C : (x + 1) * C]
+                s_bytes[1, e] = both[:, x * C : (x + 1) * C]
+            return both
 
-        def gather_codes(s, i):
-            experts = PIECES[i]
+        def shift_bytes(experts, source, queue):
             n = len(experts) * C
             a = experts[0] * C
-            codes = (gathered_0 if s == 0 else gathered).tile([P, n], U32, name=f"s_codes{s}", align_bytes=64)
-            nc.vector.tensor_copy(codes[:], x_codes[s][:].indirect(offs_t[:, a // 16 : (a + n) // 16]))
-            for x, e in enumerate(experts):
-                s_codes[s, e] = codes[:, x * C : (x + 1) * C]
+            queue.dma_start(shifted[0 : P - 4, a : a + n].bitcast(I32), source[4:P].bitcast(I32))
+            for e in experts:
+                s_bytes[0, e] = shifted[:, e * C : (e + 1) * C]
 
-        cast(0, 320, 512, nc.scalar.copy)
-        cast(0, 0, 320, nc.vector.tensor_copy)
+        def gather_codes(s, e):
+            codes = gathered.tile([P, C], U32, name=f"s_codes{s}", align_bytes=64)
+            nc.vector.tensor_copy(codes[:], x_codes[s][:].indirect(offs_t[:, e * C // 16 : (e + 1) * C // 16]))
+            for st in range(2):
+                s_codes[s, e, st] = codes[:, st * P : (st + 1) * P]
+
+        def gather_first_codes(st, offset):
+            codes = placed([P, P], U32, f"first_codes{st}", offset)
+            nc.vector.tensor_copy(codes[:], x_codes[0][:].indirect(offs_t[:, st * P // 16 : (st + 1) * P // 16]))
+            s_codes[0, 0, st] = codes[:]
+
         quantize_tokens(0)
-        gather_codes(0, 0)
-        cast(1, 208, 512, nc.scalar.copy)
-        cast(1, 0, 208, nc.vector.tensor_copy)
+        shifted = placed([P, SLOTS], U8, "shifted", 0)
+        shift_bytes((0,), gather_bytes((0,), "first_bytes"), nc.gpsimd)
+        gather_first_codes(0, 17 * KB + 256)
+        gather_first_codes(1, 7 * KB - 256)
+        gather_codes(0, 1)
         quantize_tokens(1)
-        gather_bytes(0, nc.scalar)
+        shift_bytes((1,), gather_bytes(BYTE_PIECES[0], "s_bytes")[:, C:], nc.gpsimd)
         gather_codes(1, 0)
-        for i in range(1, AHEAD):
-            gather_bytes(i, nc.scalar if i == 1 else nc.sync)
-            if i < AHEAD - 1:
-                gather_codes(0, i)
-            gather_codes(1, i)
-
-        late_scales = []
-        for m, src in enumerate((w1_scales, w3_scales)):
-            t = keep.tile([P, E - EARLY, PASSES, H], U8, name=f"x_raw{m}", align_bytes=64)
-            nc.gpsimd.memset(t[:].bitcast(I32), 0)
-            load_scales(t, src, EARLY, E, nc.gpsimd)
-            late_scales.append(t)
-        w2_all = keep.tile([P, E, 3 * N], U8, name="x_bf1", align_bytes=64)
-        w2_t = w2_all[:].rearrange("p e c -> p (e c)")[:, 0 : E * 2 * N].rearrange("p (e c) -> p e c", e=E)
-        w2_s = w2_all[:].rearrange("p e c -> p (e c)")[:, E * 2 * N :].rearrange("p (e c) -> p e c", e=E)
-        nc.gpsimd.memset(w2_s.bitcast(I32), 0)
-        nc.sync.dma_start(w2_t.bitcast(I32), w2_words.bitcast(I32).rearrange("e s p c -> p (e s) c"))
-        for quad in range(4):
-            nc.sync.dma_start(
-                w2_s[32 * quad : 32 * quad + 4].bitcast(I32),
-                w2_scales.bitcast(I32).rearrange("e s q i -> q (e s) i")[4 * quad : 4 * quad + 4],
-            )
+        gather_codes(1, 1)
+        shift_bytes(BYTE_PIECES[1], gather_bytes(BYTE_PIECES[1], "s_bytes"), nc.gpsimd)
 
         h_tiles = {}
 
-        def multiply_1(e, st):
+        def first_banks(e, st):
+            k = 2 * e + st
+            return [psum.tile([P, H], F32, name=f"bank_a{k % 3}"), psum.tile([P, H], F32, name=f"bank_b{k % 4}")]
+
+        def multiply_1(e, st, m, s, bank, opens):
             slots = slice(st * P, (st + 1) * P)
-            banks = []
-            for m, name in enumerate(("bank_a", "bank_b")):
-                scales = early_scales[m][:, e] if e < EARLY else late_scales[m][:, e - EARLY]
-                bank = psum.tile([P, H], F32, name=name)
-                for s in range(PASSES):
-                    nc.tensor.matmul_mx(
-                        out=bank[:],
-                        lhsT=s_codes[s, e][:, slots].bitcast(FP8X4),
-                        lhsT_scale=s_bytes[s, e][:, slots],
-                        rhs=w_tiles[e][:, m, s, :].bitcast(FP4X4),
-                        rhs_scale=scales[:, s, :],
-                        start=(s == 0),
-                        stop=(s == PASSES - 1),
-                    )
-                banks.append(bank)
-            return banks
+            nc.tensor.matmul_mx(
+                out=bank[:],
+                lhsT=s_codes[s, e, st].bitcast(FP8X4),
+                lhsT_scale=s_bytes[s, e][:, slots],
+                rhs=w_tiles[e][:, m, s, :].bitcast(FP4X4),
+                rhs_scale=w_scales[m, e][:, s, :],
+                start=opens,
+                stop=not opens,
+            )
+
+        def first_layer(e):
+            banks = [first_banks(e, st) for st in range(2)]
+            opening = 0 if e == 0 else 1
+            if e < 2:
+                for st in range(2):
+                    for m in range(2):
+                        multiply_1(e, st, m, opening, banks[st][m], True)
+            for st in range(2):
+                for m in range(2):
+                    if e >= 2:
+                        multiply_1(e, st, m, opening, banks[st][m], True)
+                    multiply_1(e, st, m, 1 - opening, banks[st][m], False)
+                activate(e, st, banks[st])
 
         def activate(e, st, banks):
-            sig = work.tile([P, H], F32, name="sig")
-            nc.scalar.activation(sig[:], banks[0][:], SIGMOID)
-            h = work.tile([P, H], BF16, name="h", align_bytes=64)
-            nc.vector.tensor_tensor(h[:], banks[1][:], sig[:], MULT)
+            sig = work.tile([P, 2, P, 2], F32, name="sig", align_bytes=64)
+            nc.scalar.activation(sig[:], banks[0][:].rearrange("s (p u d) -> s u p d", u=2, d=2), SIGMOID)
+            h = work.tile([P, 2, P, 2], BF16, name="h", align_bytes=64)
+            nc.vector.tensor_tensor(h[:], banks[1][:].rearrange("s (p u d) -> s u p d", u=2, d=2), sig[:], MULT)
             h_tiles[e, st] = h
 
         def turn(e, tiles, engine_copy):
             n = len(tiles) * P
-            turned = psum_2.tile([P, 2, n], F32, name="turned")
+            turned = psum.tile([P, 2, n], F32, name=f"bank_a{(2 * e + 2 + tiles[0]) % 3}")
             for x, st in enumerate(tiles):
-                words = h_tiles[e, st][:].bitcast(F32)
+                words = h_tiles[e, st][:].rearrange("s u p d -> s (u p d)").bitcast(F32)
                 for u in range(2):
-                    nc.tensor.transpose(turned[:, u, x * P : (x + 1) * P], words[:, u::2], ident[:])
+                    nc.tensor.transpose(turned[:, u, x * P : (x + 1) * P], words[:, u * P : (u + 1) * P], ident[:])
             h_bf = work.tile([P, 4 * n], BF16, name="h_bf", align_bytes=64)
             engine_copy(h_bf[:].bitcast(F32).rearrange("p (r u) -> p r u", u=2), turned[:].rearrange("p u r -> p r u"))
             return h_bf
@@ -211,11 +207,21 @@ def tile_moe_tk_glu_sigmoid_kernel(
             nc.vector.quantize_mx(out=h_codes[:].bitcast(FP8X4), scales=h_bytes[:], in_=h_bf[:])
             return h_codes, h_bytes
 
+        second = {}
+
+        def load_second():
+            w2_s = placed([P, E, N], U8, "w2_s", first_weights)
+            w2_t = placed([P, E, 2 * N], U8, "w2_t", first_weights + KB)
+            load_scale_rows(w2_s[:].bitcast(I32), w2_scales.bitcast(I32).rearrange("e s q i -> q (e s) i"))
+            nc.sync.dma_start(w2_t[:].bitcast(I32), w2_words.bitcast(I32).rearrange("e s p c -> p (e s) c"))
+            second["s"] = w2_s
+            second["t"] = w2_t
+
         def multiply_2(e, target, h_codes, h_bytes):
             nc.tensor.matmul_mx(
                 out=target,
-                lhsT=w2_t[:, e, :].bitcast(FP4X4),
-                lhsT_scale=w2_s[:, e, :],
+                lhsT=second["t"][:, e, :].bitcast(FP4X4),
+                lhsT_scale=second["s"][:, e, :],
                 rhs=h_codes[:].bitcast(FP8X4),
                 rhs_scale=h_bytes[:],
                 start=True,
@@ -227,7 +233,7 @@ def tile_moe_tk_glu_sigmoid_kernel(
 
         def second_layer(e):
             if e % 2 == 0:
-                y_bank = psum_2.tile([P, 2 * C], F32, name="y_bank")
+                y_bank = psum.tile([P, 2 * C], F32, name="y_bank")
                 y_banks[e] = y_bank
                 multiply_2(e, y_bank[:, 0:C], *quantized[e])
             else:
@@ -237,38 +243,42 @@ def tile_moe_tk_glu_sigmoid_kernel(
 
         last = E - 1
         for e in range(E):
-            activate(e, 0, multiply_1(e, 0))
-            activate(e, 1, multiply_1(e, 1))
+            first_layer(e)
             if e >= 2:
                 second_layer(e - 2)
             if e >= 1:
-                h_bf = turn(e - 1, (0, 1), nc.scalar.copy)
-                quantized[e - 1] = quantize_hidden(h_bf)
-            load_ring(e + RING)
-            if e % 2 == 0:
-                i = e // 2 + AHEAD
-                if i - 1 < len(PIECES):
-                    gather_codes(0, i - 1)
-                if i < len(PIECES):
-                    gather_bytes(i, nc.sync)
-                    gather_codes(1, i)
-            if e == 3:
-                for r, src in enumerate((pos1, pos2, pos3, pos4)):
-                    nc.sync.dma_start(pos_t[r][:], src)
+                quantized[e - 1] = quantize_hidden(turn(e - 1, (0, 1), nc.scalar.copy))
+            if e % 2 == 1 and (e + 3) // 2 < len(BYTE_PIECES):
+                piece = BYTE_PIECES[(e + 3) // 2]
+                shift_bytes(piece, gather_bytes(piece, "s_bytes"), nc.gpsimd)
+            if e + 2 < E:
+                gather_codes(1, e + 2)
+                gather_codes(0, e + 2)
+            if e == 0:
+                load_weights(2, w_places[2])
+                load_scales(3, 8, (7 * KB, 2 * KB), "b", False)
+                load_second()
+                load_weights(3, w_places[3])
+            if 1 <= e <= 4:
+                w_places[e + 3] = w_places[e]
+                load_weights(e + 3, w_places[e])
+            if e == 5:
+                gates = placed([P, TOP, T], F32, "gates", w_places[5] + 3 * KB)
+                nc.sync.dma_start(gates[:], gate.rearrange("r p t -> p r t"))
 
         first = quantize_hidden(turn(last, (0,), nc.scalar.copy))
         second_layer(last - 1)
         y_bank = y_banks[last - 1]
         multiply_2(last, y_bank[:, C : C + P], *first)
         nc.scalar.copy(y_t[:, (last - 1) * C : last * C + P], y_bank[:, 0 : C + P])
-        second = quantize_hidden(turn(last, (1,), nc.vector.tensor_copy))
-        y_last = psum.tile([P, P], F32, name="bank_a")
-        multiply_2(last, y_last[:], *second)
+        final = quantize_hidden(turn(last, (1,), nc.vector.tensor_copy))
+        y_last = psum.tile([P, P], F32, name="bank_b0")
+        multiply_2(last, y_last[:], *final)
         nc.vector.tensor_copy(y_t[:, last * C + P :], y_last[:])
 
         parts = keep.tile([P, TOP, T], F32, name="parts", align_bytes=64)
         for r in range(TOP):
-            nc.vector.tensor_tensor(parts[:, r], y_t[:].indirect(pos_t[r][:]), gates[r], MULT)
+            nc.vector.tensor_tensor(parts[:, r], y_t[:].indirect(pos_t[r][:]), gates[:, r], MULT)
         pairs = keep.tile([P, 2, T], F32, name="pairs", align_bytes=64)
         nc.vector.tensor_tensor(pairs[:], parts[:, 0:2], parts[:, 2:4], ADD)
         half = T // 2

@@ -12,6 +12,7 @@ U8 = mybir.dt.uint8
 FP8X4 = mybir.dt.float8_e4m3fn_x4
 FP4X4 = mybir.dt.float4_e2m1fn_x4
 SIGMOID = mybir.ActivationFunctionType.Sigmoid
+COPY = mybir.ActivationFunctionType.Copy
 MULT = mybir.AluOpType.mult
 ADD = mybir.AluOpType.add
 
@@ -22,7 +23,8 @@ PASSES = K // 512
 FLOPS = 2 * SLOTS * (2 * K * H + H * N)
 
 KB = 1024
-VECTOR_CAST = (344, 176)
+BLOCKS = T // P
+VECTOR_CAST = (176, 176, 176)
 BYTE_PIECES = ((0, 1), (2, 3), (4, 5), (6, 7))
 
 
@@ -44,8 +46,9 @@ def tile_moe_tk_glu_sigmoid_kernel(
         offs_t = lists.tile([P, SLOTS // 16], U16, name="offs_t")
         pos_t = [lists.tile([P, T // 16], U16, name=f"pos{r}_t") for r in range(TOP)]
 
-        x_raw = [placed([P, 4, T], F32, f"x_raw{s}", 8 * KB * s) for s in range(PASSES)]
-        x_bf = [placed([P, T, 4], BF16, f"x_bf{s}", 16 * KB + 4 * KB * s) for s in range(PASSES)]
+        x_pieces = ((0, 0, T // 2), (0, T // 2, T), (1, 0, T))
+        x_raw = [placed([P, 4, b - a], F32, f"x_raw{s}_{a}", 8 * KB * s + 16 * a) for s, a, b in x_pieces]
+        x_bf = [placed([P, T, 4], BF16, f"x_bf{s}", 48 * KB + 4 * KB * s) for s in range(PASSES)]
         x_codes = [keep.tile([P, T], U32, name=f"x_codes{s}", align_bytes=64) for s in range(PASSES)]
         x_bytes = keep.tile([P, 2 * T], U8, name="x_bytes", align_bytes=64)
         y_t = keep.tile([P, SLOTS], F32, name="y_t", align_bytes=64)
@@ -53,59 +56,69 @@ def tile_moe_tk_glu_sigmoid_kernel(
         ident = keep.tile([P, P], F32, name="ident", align_bytes=64)
         warm = keep.tile([P, 2], F32, name="warm", align_bytes=64)
 
-        nc.sync.dma_start(x_raw[0][:], xT[0:512, :].rearrange("(p j) w -> p j w", j=4))
+        def load_tokens(i):
+            s, a, b = x_pieces[i]
+            nc.sync.dma_start(x_raw[i][:], xT[512 * s : 512 * (s + 1), a:b].rearrange("(p j) w -> p j w", j=4))
+
+        load_tokens(0)
+        load_tokens(1)
         nc.sync.dma_start(offs_t[:], offs)
         for r, src in enumerate((pos1, pos2, pos3, pos4)):
             nc.sync.dma_start(pos_t[r][:], src)
-        nc.sync.dma_start(x_raw[1][:], xT[512:1024, :].rearrange("(p j) w -> p j w", j=4))
+        load_tokens(2)
 
         w_scales = {}
         w_tiles = {}
 
-        def load_scale_rows(t, view):
+        def load_scale_rows(t, view, queues):
             for r in range(4):
-                nc.sync.dma_start(t[r:P:32], view[r:16:4])
+                queues[r].dma_start(t[r:P:32], view[r:16:4])
 
-        def load_scales(e0, e1, offsets, label, clear):
+        def load_scales(e0, e1, tiles, queues):
             for m, src in enumerate((w1_scales, w3_scales)):
-                t = placed([P, (e1 - e0) * PASSES, H], U8, f"scales_{label}{m}", offsets[m])
-                if clear:
-                    nc.vector.memset(t[:].bitcast(I32), 0)
+                t = tiles[m].rearrange("p (g i) -> p g i", i=H)
                 view = src.bitcast(I32).rearrange("e s q i -> q (e s) i")[:, e0 * PASSES : e1 * PASSES, :]
-                load_scale_rows(t[:].bitcast(I32), view)
+                load_scale_rows(t.bitcast(I32), view, queues[4 * m : 4 * m + 4])
                 for e in range(e0, e1):
                     w_scales[m, e] = t[:, (e - e0) * PASSES : (e - e0 + 1) * PASSES, :]
 
-        def load_weights(e, offset):
-            w = placed([P, 2, PASSES, 2 * H], U8, f"w{e}", offset)
+        def load_weights(e0, e1, room):
+            w = room.rearrange("p (m e s c) -> p m e s c", m=2, e=e1 - e0, s=PASSES)
             for m, src in enumerate((w1_words, w3_words)):
-                nc.sync.dma_start(w[:, m].bitcast(I32), src.bitcast(I32)[e].rearrange("s p c -> p s c"))
-            w_tiles[e] = w
+                nc.sync.dma_start(
+                    w[:, m].rearrange("p e s c -> p (e s) c").bitcast(I32),
+                    src.bitcast(I32)[e0:e1].rearrange("e s p c -> p (e s) c"),
+                )
+            for e in range(e0, e1):
+                w_tiles[e] = w[:, :, e - e0]
 
-        first_weights = 30 * KB
-        w_places = {1: 38 * KB, 2: 17 * KB + 256, 3: first_weights + 3 * KB}
-        load_scales(0, 3, (24 * KB, 27 * KB), "a", True)
-        load_weights(0, first_weights)
-        load_weights(1, w_places[1])
+        first_scales = [keep.tile([P, 2 * KB], U8, name=f"first_scales{m}", align_bytes=64) for m in range(2)]
+        for t in first_scales:
+            nc.vector.memset(t[:].bitcast(I32), 0)
+        load_scales(0, 2, [t[:] for t in first_scales], [nc.gpsimd] * 2 + [nc.sync] * 6)
+        first_weights = placed([P, 4 * KB], U8, "first_weights", 56 * KB)
+        load_weights(0, 1, first_weights[:])
 
         nc.vector.memset(x_bytes[:].bitcast(I32), 0)
         nc.vector.memset(warm[:], 0.0)
         nc.scalar.activation(warm[:, 0:1], warm[:, 1:2], SIGMOID)
         make_identity(nc, ident[:])
 
-        def cast(s, a, b, engine_copy):
+        def cast(i, a, b, engine_copy):
+            s, first = x_pieces[i][0:2]
             engine_copy(
-                x_bf[s][:, a:b, :].rearrange("p (c i) j -> p c j i", i=4),
-                x_raw[s][:, :, a:b].rearrange("p j (c i) -> p c j i", i=4),
+                x_bf[s][:, first + a : first + b, :].rearrange("p (c i) j -> p c j i", i=4),
+                x_raw[i][:, :, a:b].rearrange("p j (c i) -> p c j i", i=4),
             )
 
-        def quantize_tokens(s):
-            cast(s, VECTOR_CAST[s], T, nc.scalar.copy)
-            cast(s, 0, VECTOR_CAST[s], nc.vector.tensor_copy)
+        def quantize_tokens(i):
+            s, a, b = x_pieces[i]
+            cast(i, VECTOR_CAST[i], b - a, nc.scalar.copy)
+            cast(i, 0, VECTOR_CAST[i], nc.vector.tensor_copy)
             nc.vector.quantize_mx(
-                out=x_codes[s][:].bitcast(FP8X4),
-                scales=x_bytes[4 * (1 - s) : P, 0:T],
-                in_=x_bf[s][:].rearrange("p w j -> p (w j)"),
+                out=x_codes[s][:, a:b].bitcast(FP8X4),
+                scales=x_bytes[4 * (1 - s) : P, a:b],
+                in_=x_bf[s][:, a:b].rearrange("p w j -> p (w j)"),
             )
 
         s_codes = {}
@@ -133,22 +146,32 @@ def tile_moe_tk_glu_sigmoid_kernel(
             for st in range(2):
                 s_codes[s, e, st] = codes[:, st * P : (st + 1) * P]
 
-        def gather_first_codes(st, offset):
-            codes = placed([P, P], U32, f"first_codes{st}", offset)
-            nc.vector.tensor_copy(codes[:], x_codes[0][:].indirect(offs_t[:, st * P // 16 : (st + 1) * P // 16]))
-            s_codes[0, 0, st] = codes[:]
-
         quantize_tokens(0)
+        quantize_tokens(1)
         shifted = placed([P, SLOTS], U8, "shifted", 0)
         shift_bytes((0,), gather_bytes((0,), "first_bytes"), nc.gpsimd)
-        gather_first_codes(0, 17 * KB + 256)
-        gather_first_codes(1, 7 * KB - 256)
+        gather_codes(0, 0)
         gather_codes(0, 1)
-        quantize_tokens(1)
+        quantize_tokens(2)
         shift_bytes((1,), gather_bytes(BYTE_PIECES[0], "s_bytes")[:, C:], nc.gpsimd)
         gather_codes(1, 0)
         gather_codes(1, 1)
         shift_bytes(BYTE_PIECES[1], gather_bytes(BYTE_PIECES[1], "s_bytes"), nc.gpsimd)
+
+        late = placed([P, 30 * KB], U8, "late", 15 * KB + 256)
+
+        def late_weights(e0, e1):
+            load_weights(e0, e1, late[:, (4 * e0 - 2) * KB : (4 * e1 - 2) * KB])
+
+        late_weights(1, 2)
+        load_scales(2, E, [placed([P, 6 * KB], U8, f"late_scales{m}", (2 + 6 * m) * KB + 256)[:] for m in range(2)], [nc.sync] * 8)
+        late_weights(2, 4)
+        w2_s = placed([P, E, N], U8, "w2_s", 14 * KB + 256)[:]
+        w2_t = late[:, 0 : 2 * KB].rearrange("p (e n) -> p e n", e=E)
+        load_scale_rows(w2_s.bitcast(I32), w2_scales.bitcast(I32).rearrange("e s q i -> q (e s) i"), [nc.sync] * 4)
+        nc.sync.dma_start(w2_t.bitcast(I32), w2_words.bitcast(I32).rearrange("e s p c -> p (e s) c"))
+        late_weights(4, 6)
+        late_weights(6, 8)
 
         h_tiles = {}
 
@@ -172,8 +195,8 @@ def tile_moe_tk_glu_sigmoid_kernel(
             banks = [first_banks(e, st) for st in range(2)]
             opening = 0 if e == 0 else 1
             if e < 2:
-                for st in range(2):
-                    for m in range(2):
+                for m in range(2):
+                    for st in range(2):
                         multiply_1(e, st, m, opening, banks[st][m], True)
             for st in range(2):
                 for m in range(2):
@@ -185,13 +208,13 @@ def tile_moe_tk_glu_sigmoid_kernel(
         def activate(e, st, banks):
             sig = work.tile([P, 2, P, 2], F32, name="sig", align_bytes=64)
             nc.scalar.activation(sig[:], banks[0][:].rearrange("s (p u d) -> s u p d", u=2, d=2), SIGMOID)
-            h = work.tile([P, 2, P, 2], BF16, name="h", align_bytes=64)
+            h = work.tile([P, 2, P, 2], BF16, name="h", align_bytes=64, bufs=6)
             nc.vector.tensor_tensor(h[:], banks[1][:].rearrange("s (p u d) -> s u p d", u=2, d=2), sig[:], MULT)
             h_tiles[e, st] = h
 
-        def turn(e, tiles, engine_copy):
+        def turn(e, tiles, k, engine_copy):
             n = len(tiles) * P
-            turned = psum.tile([P, 2, n], F32, name=f"bank_a{(2 * e + 2 + tiles[0]) % 3}")
+            turned = psum.tile([P, 2, n], F32, name=f"bank_a{k % 3}")
             for x, st in enumerate(tiles):
                 words = h_tiles[e, st][:].rearrange("s u p d -> s (u p d)").bitcast(F32)
                 for u in range(2):
@@ -207,21 +230,11 @@ def tile_moe_tk_glu_sigmoid_kernel(
             nc.vector.quantize_mx(out=h_codes[:].bitcast(FP8X4), scales=h_bytes[:], in_=h_bf[:])
             return h_codes, h_bytes
 
-        second = {}
-
-        def load_second():
-            w2_s = placed([P, E, N], U8, "w2_s", first_weights)
-            w2_t = placed([P, E, 2 * N], U8, "w2_t", first_weights + KB)
-            load_scale_rows(w2_s[:].bitcast(I32), w2_scales.bitcast(I32).rearrange("e s q i -> q (e s) i"))
-            nc.sync.dma_start(w2_t[:].bitcast(I32), w2_words.bitcast(I32).rearrange("e s p c -> p (e s) c"))
-            second["s"] = w2_s
-            second["t"] = w2_t
-
         def multiply_2(e, target, h_codes, h_bytes):
             nc.tensor.matmul_mx(
                 out=target,
-                lhsT=second["t"][:, e, :].bitcast(FP4X4),
-                lhsT_scale=second["s"][:, e, :],
+                lhsT=w2_t[:, e, :].bitcast(FP4X4),
+                lhsT_scale=w2_s[:, e, :],
                 rhs=h_codes[:].bitcast(FP8X4),
                 rhs_scale=h_bytes[:],
                 start=True,
@@ -244,10 +257,15 @@ def tile_moe_tk_glu_sigmoid_kernel(
         last = E - 1
         for e in range(E):
             first_layer(e)
-            if e >= 2:
+            if e >= 3 and e % 2 == 1:
+                second_layer(e - 3)
                 second_layer(e - 2)
-            if e >= 1:
-                quantized[e - 1] = quantize_hidden(turn(e - 1, (0, 1), nc.scalar.copy))
+            if e >= 2 and e % 2 == 0:
+                pair = [turn(e - 2 + x, (0, 1), 2 * e + x, nc.scalar.copy) for x in range(2)]
+                for x in range(2):
+                    quantized[e - 2 + x] = quantize_hidden(pair[x])
+            if e == last:
+                quantized[e - 1] = quantize_hidden(turn(e - 1, (0, 1), 2 * e, nc.scalar.copy))
             if e % 2 == 1 and (e + 3) // 2 < len(BYTE_PIECES):
                 piece = BYTE_PIECES[(e + 3) // 2]
                 shift_bytes(piece, gather_bytes(piece, "s_bytes"), nc.gpsimd)
@@ -255,34 +273,42 @@ def tile_moe_tk_glu_sigmoid_kernel(
                 gather_codes(1, e + 2)
                 gather_codes(0, e + 2)
             if e == 0:
-                load_weights(2, w_places[2])
-                load_scales(3, 8, (7 * KB, 2 * KB), "b", False)
-                load_second()
-                load_weights(3, w_places[3])
-            if 1 <= e <= 4:
-                w_places[e + 3] = w_places[e]
-                load_weights(e + 3, w_places[e])
-            if e == 5:
-                gates = placed([P, TOP, T], F32, "gates", w_places[5] + 3 * KB)
-                nc.sync.dma_start(gates[:], gate.rearrange("r p t -> p r t"))
+                last_gate = placed([P, T], F32, "last_gate", 56 * KB)
+                nc.sync.dma_start(last_gate[:], gate[TOP - 1])
+                gate_cols = placed([P, TOP - 1, 8], F32, "gate_cols", 58 * KB)
+                with nc.allow_non_contiguous_dma(reason="one gate a token, tokens on the partitions"):
+                    for r in range(TOP - 1):
+                        nc.sync.dma_start(gate_cols[:, r, 0:BLOCKS], gate[r, 0].rearrange("(b t) -> t b", t=P))
 
-        first = quantize_hidden(turn(last, (0,), nc.scalar.copy))
+        first = quantize_hidden(turn(last, (0,), 2 * last + 2, nc.scalar.copy))
         second_layer(last - 1)
         y_bank = y_banks[last - 1]
         multiply_2(last, y_bank[:, C : C + P], *first)
         nc.scalar.copy(y_t[:, (last - 1) * C : last * C + P], y_bank[:, 0 : C + P])
-        final = quantize_hidden(turn(last, (1,), nc.vector.tensor_copy))
+        final = quantize_hidden(turn(last, (1,), 2 * last + 1, nc.vector.tensor_copy))
         y_last = psum.tile([P, P], F32, name="bank_b0")
         multiply_2(last, y_last[:], *final)
         nc.vector.tensor_copy(y_t[:, last * C + P :], y_last[:])
 
-        parts = keep.tile([P, TOP, T], F32, name="parts", align_bytes=64)
-        for r in range(TOP):
-            nc.vector.tensor_tensor(parts[:, r], y_t[:].indirect(pos_t[r][:]), gates[:, r], MULT)
-        pairs = keep.tile([P, 2, T], F32, name="pairs", align_bytes=64)
-        nc.vector.tensor_tensor(pairs[:], parts[:, 0:2], parts[:, 2:4], ADD)
-        half = T // 2
-        for hf in range(2):
-            cols = slice(hf * half, (hf + 1) * half)
-            nc.vector.tensor_tensor(out_t[:, cols], pairs[:, 0, cols], pairs[:, 1, cols], ADD)
-            nc.sync.dma_start(out[:, cols], out_t[:, cols])
+        sums = [psum.tile([P, P], F32, name=f"bank_b{b}") for b in range(BLOCKS)]
+        for r in range(TOP - 1):
+            picked = keep.tile([P, T], F32, name=f"picked{r}", align_bytes=64)
+            nc.vector.tensor_copy(picked[:], y_t[:].indirect(pos_t[r][:]))
+            by_token = psum.tile([P, BLOCKS, N], F32, name=f"bank_a{r}")
+            weighted = keep.tile([P, BLOCKS, N], F32, name=f"weighted{r}", align_bytes=64)
+            for b in range(BLOCKS):
+                nc.tensor.transpose(by_token[:, b], picked[:, b * P : (b + 1) * P], ident[:])
+            for b in range(BLOCKS):
+                nc.scalar.activation(weighted[:, b], by_token[:, b], COPY, scale=gate_cols[:, r, b : b + 1])
+            for b in range(BLOCKS):
+                nc.tensor.matmul(
+                    sums[b][:], weighted[:, b], ident[:], start=(r == 0), stop=(r == TOP - 2), is_transpose=True
+                )
+        part = keep.tile([P, T], F32, name="part", align_bytes=64)
+        nc.vector.tensor_tensor(part[:], y_t[:].indirect(pos_t[TOP - 1][:]), last_gate[:], MULT)
+        for b in range(BLOCKS):
+            cols = slice(b * P, (b + 1) * P)
+            nc.vector.tensor_tensor(out_t[:, cols], sums[b][:], part[:, cols], ADD)
+            if b % 2 == 1:
+                pair = slice((b - 1) * P, (b + 1) * P)
+                nc.sync.dma_start(out[:, pair], out_t[:, pair])

@@ -47,8 +47,8 @@ def tile_moe_tk_glu_sigmoid_kernel(
         pos_t = [lists.tile([P, T // 16], U16, name=f"pos{r}_t") for r in range(TOP)]
 
         x_pieces = ((0, 0, T // 2), (0, T // 2, T), (1, 0, T))
-        x_raw = [placed([P, 4, b - a], F32, f"x_raw{s}_{a}", 8 * KB * s + 16 * a) for s, a, b in x_pieces]
-        x_bf = [placed([P, T, 4], BF16, f"x_bf{s}", 48 * KB + 4 * KB * s) for s in range(PASSES)]
+        x_raw = [placed([P, 4, b - a], F32, f"x_raw{s}_{a}", 8 * KB * (s + 1) + 16 * a) for s, a, b in x_pieces]
+        x_bf = [placed([P, T, 4], BF16, f"x_bf{s}", 28 * KB - 4 * KB * s) for s in range(PASSES)]
         x_codes = [keep.tile([P, T], U32, name=f"x_codes{s}", align_bytes=64) for s in range(PASSES)]
         x_bytes = keep.tile([P, 2 * T], U8, name="x_bytes", align_bytes=64)
         y_t = keep.tile([P, SLOTS], F32, name="y_t", align_bytes=64)
@@ -70,15 +70,15 @@ def tile_moe_tk_glu_sigmoid_kernel(
         w_scales = {}
         w_tiles = {}
 
-        def load_scale_rows(t, view, queues):
+        def load_scale_rows(t, view):
             for r in range(4):
-                queues[r].dma_start(t[r:P:32], view[r:16:4])
+                nc.sync.dma_start(t[r:P:32], view[r:16:4])
 
-        def load_scales(e0, e1, tiles, queues):
+        def load_scales(e0, e1, tiles):
             for m, src in enumerate((w1_scales, w3_scales)):
                 t = tiles[m].rearrange("p (g i) -> p g i", i=H)
                 view = src.bitcast(I32).rearrange("e s q i -> q (e s) i")[:, e0 * PASSES : e1 * PASSES, :]
-                load_scale_rows(t.bitcast(I32), view, queues[4 * m : 4 * m + 4])
+                load_scale_rows(t.bitcast(I32), view)
                 for e in range(e0, e1):
                     w_scales[m, e] = t[:, (e - e0) * PASSES : (e - e0 + 1) * PASSES, :]
 
@@ -92,11 +92,11 @@ def tile_moe_tk_glu_sigmoid_kernel(
             for e in range(e0, e1):
                 w_tiles[e] = w[:, :, e - e0]
 
-        first_scales = [keep.tile([P, 2 * KB], U8, name=f"first_scales{m}", align_bytes=64) for m in range(2)]
+        first_scales = [keep.tile([P, 3 * KB], U8, name=f"first_scales{m}", align_bytes=64) for m in range(2)]
         for t in first_scales:
             nc.vector.memset(t[:].bitcast(I32), 0)
-        load_scales(0, 2, [t[:] for t in first_scales], [nc.gpsimd] * 2 + [nc.sync] * 6)
-        first_weights = placed([P, 4 * KB], U8, "first_weights", 56 * KB)
+        load_scales(0, 3, [t[:] for t in first_scales])
+        first_weights = placed([P, 4 * KB], U8, "first_weights", 40 * KB)
         load_weights(0, 1, first_weights[:])
 
         nc.vector.memset(x_bytes[:].bitcast(I32), 0)
@@ -146,32 +146,24 @@ def tile_moe_tk_glu_sigmoid_kernel(
             for st in range(2):
                 s_codes[s, e, st] = codes[:, st * P : (st + 1) * P]
 
+        def gather_first_codes(st, offset):
+            codes = placed([P, P], U32, f"first_codes{st}", offset)
+            nc.vector.tensor_copy(codes[:], x_codes[1][:].indirect(offs_t[:, st * P // 16 : (st + 1) * P // 16]))
+            s_codes[1, 0, st] = codes[:]
+
         quantize_tokens(0)
         quantize_tokens(1)
-        shifted = placed([P, SLOTS], U8, "shifted", 0)
-        shift_bytes((0,), gather_bytes((0,), "first_bytes"), nc.gpsimd)
+        shifted = placed([P, SLOTS], U8, "shifted", 8 * KB)
+        shift_bytes((0,), gather_bytes((0,), "first_bytes"), nc.sync)
         gather_codes(0, 0)
         gather_codes(0, 1)
         quantize_tokens(2)
-        shift_bytes((1,), gather_bytes(BYTE_PIECES[0], "s_bytes")[:, C:], nc.gpsimd)
-        gather_codes(1, 0)
+        load_weights(1, 2, placed([P, 4 * KB], U8, "second_weights", 20 * KB)[:])
+        shift_bytes((1,), gather_bytes(BYTE_PIECES[0], "s_bytes")[:, C:], nc.sync)
+        gather_first_codes(0, 32 * KB)
+        gather_first_codes(1, 15 * KB - 256)
         gather_codes(1, 1)
-        shift_bytes(BYTE_PIECES[1], gather_bytes(BYTE_PIECES[1], "s_bytes"), nc.gpsimd)
-
-        late = placed([P, 30 * KB], U8, "late", 15 * KB + 256)
-
-        def late_weights(e0, e1):
-            load_weights(e0, e1, late[:, (4 * e0 - 2) * KB : (4 * e1 - 2) * KB])
-
-        late_weights(1, 2)
-        load_scales(2, E, [placed([P, 6 * KB], U8, f"late_scales{m}", (2 + 6 * m) * KB + 256)[:] for m in range(2)], [nc.sync] * 8)
-        late_weights(2, 4)
-        w2_s = placed([P, E, N], U8, "w2_s", 14 * KB + 256)[:]
-        w2_t = late[:, 0 : 2 * KB].rearrange("p (e n) -> p e n", e=E)
-        load_scale_rows(w2_s.bitcast(I32), w2_scales.bitcast(I32).rearrange("e s q i -> q (e s) i"), [nc.sync] * 4)
-        nc.sync.dma_start(w2_t.bitcast(I32), w2_words.bitcast(I32).rearrange("e s p c -> p (e s) c"))
-        late_weights(4, 6)
-        late_weights(6, 8)
+        shift_bytes(BYTE_PIECES[1], gather_bytes(BYTE_PIECES[1], "s_bytes"), nc.sync)
 
         h_tiles = {}
 
@@ -230,11 +222,21 @@ def tile_moe_tk_glu_sigmoid_kernel(
             nc.vector.quantize_mx(out=h_codes[:].bitcast(FP8X4), scales=h_bytes[:], in_=h_bf[:])
             return h_codes, h_bytes
 
+        second = {}
+
+        def load_second():
+            w2_s = placed([P, E, N], U8, "w2_s", 40 * KB)[:]
+            w2_t = placed([P, E, 2 * N], U8, "w2_t", 41 * KB)[:]
+            load_scale_rows(w2_s.bitcast(I32), w2_scales.bitcast(I32).rearrange("e s q i -> q (e s) i"))
+            nc.sync.dma_start(w2_t.bitcast(I32), w2_words.bitcast(I32).rearrange("e s p c -> p (e s) c"))
+            second["s"] = w2_s
+            second["t"] = w2_t
+
         def multiply_2(e, target, h_codes, h_bytes):
             nc.tensor.matmul_mx(
                 out=target,
-                lhsT=w2_t[:, e, :].bitcast(FP4X4),
-                lhsT_scale=w2_s[:, e, :],
+                lhsT=second["t"][:, e, :].bitcast(FP4X4),
+                lhsT_scale=second["s"][:, e, :],
                 rhs=h_codes[:].bitcast(FP8X4),
                 rhs_scale=h_bytes[:],
                 start=True,
@@ -268,14 +270,22 @@ def tile_moe_tk_glu_sigmoid_kernel(
                 quantized[e - 1] = quantize_hidden(turn(e - 1, (0, 1), 2 * e, nc.scalar.copy))
             if e % 2 == 1 and (e + 3) // 2 < len(BYTE_PIECES):
                 piece = BYTE_PIECES[(e + 3) // 2]
-                shift_bytes(piece, gather_bytes(piece, "s_bytes"), nc.gpsimd)
+                shift_bytes(piece, gather_bytes(piece, "s_bytes"), nc.sync)
             if e + 2 < E:
                 gather_codes(1, e + 2)
                 gather_codes(0, e + 2)
             if e == 0:
-                last_gate = placed([P, T], F32, "last_gate", 56 * KB)
+                load_weights(2, 4, placed([P, 8 * KB], U8, "third_weights", 32 * KB)[:])
+                load_scales(3, E, [placed([P, 5 * KB], U8, f"late_scales{m}", (10 + 5 * m) * KB)[:] for m in range(2)])
+                load_second()
+            if e == 1:
+                load_weights(4, 6, placed([P, 8 * KB], U8, "fourth_weights", 20 * KB)[:])
+            if e == 3:
+                load_weights(6, 8, placed([P, 8 * KB], U8, "fifth_weights", 32 * KB)[:])
+            if e == 5:
+                last_gate = placed([P, T], F32, "last_gate", 20 * KB)
                 nc.sync.dma_start(last_gate[:], gate[TOP - 1])
-                gate_cols = placed([P, TOP - 1, 8], F32, "gate_cols", 58 * KB)
+                gate_cols = placed([P, TOP - 1, 8], F32, "gate_cols", 22 * KB)
                 with nc.allow_non_contiguous_dma(reason="one gate a token, tokens on the partitions"):
                     for r in range(TOP - 1):
                         nc.sync.dma_start(gate_cols[:, r, 0:BLOCKS], gate[r, 0].rearrange("(b t) -> t b", t=P))

@@ -54,7 +54,6 @@ def tile_moe_tk_glu_sigmoid_kernel(
         y_t = keep.tile([P, SLOTS], F32, name="y_t", align_bytes=64)
         out_t = keep.tile([P, T], F32, name="out_t", align_bytes=64)
         ident = keep.tile([P, P], F32, name="ident", align_bytes=64)
-        warm = keep.tile([P, 2], F32, name="warm", align_bytes=64)
 
         def load_tokens(i):
             s, a, b = x_pieces[i]
@@ -74,34 +73,31 @@ def tile_moe_tk_glu_sigmoid_kernel(
             for r in range(4):
                 nc.sync.dma_start(t[r:P:32], view[r:16:4])
 
-        def load_scales(e0, e1, tiles):
-            for m, src in enumerate((w1_scales, w3_scales)):
-                t = tiles[m].rearrange("p (g i) -> p g i", i=H)
-                view = src.bitcast(I32).rearrange("e s q i -> q (e s) i")[:, e0 * PASSES : e1 * PASSES, :]
-                load_scale_rows(t.bitcast(I32), view)
-                for e in range(e0, e1):
-                    w_scales[m, e] = t[:, (e - e0) * PASSES : (e - e0 + 1) * PASSES, :]
+        def load_scales(m, e0, e1, room):
+            t = room.rearrange("p (g i) -> p g i", i=H)
+            view = (w1_scales, w3_scales)[m].bitcast(I32).rearrange("e s q i -> q (e s) i")
+            load_scale_rows(t.bitcast(I32), view[:, e0 * PASSES : e1 * PASSES, :])
+            for e in range(e0, e1):
+                w_scales[m, e] = t[:, (e - e0) * PASSES : (e - e0 + 1) * PASSES, :]
+
+        def load_words(m, e0, e1, room):
+            w = room.rearrange("p (g c) -> p g c", c=2 * H)
+            view = (w1_words, w3_words)[m].bitcast(I32)[e0:e1].rearrange("e s p c -> p (e s) c")
+            nc.sync.dma_start(w.bitcast(I32), view)
+            for e in range(e0, e1):
+                w_tiles[m, e] = w[:, (e - e0) * PASSES : (e - e0 + 1) * PASSES, :]
 
         def load_weights(e0, e1, room):
-            w = room.rearrange("p (m e s c) -> p m e s c", m=2, e=e1 - e0, s=PASSES)
-            for m, src in enumerate((w1_words, w3_words)):
-                nc.sync.dma_start(
-                    w[:, m].rearrange("p e s c -> p (e s) c").bitcast(I32),
-                    src.bitcast(I32)[e0:e1].rearrange("e s p c -> p (e s) c"),
-                )
-            for e in range(e0, e1):
-                w_tiles[e] = w[:, :, e - e0]
+            size = (e1 - e0) * 2 * KB
+            for m in range(2):
+                load_words(m, e0, e1, room[:, m * size : (m + 1) * size])
 
-        first_scales = [keep.tile([P, 3 * KB], U8, name=f"first_scales{m}", align_bytes=64) for m in range(2)]
-        for t in first_scales:
-            nc.vector.memset(t[:].bitcast(I32), 0)
-        load_scales(0, 3, [t[:] for t in first_scales])
-        first_weights = placed([P, 4 * KB], U8, "first_weights", 40 * KB)
-        load_weights(0, 1, first_weights[:])
+        first_scales = keep.tile([P, 3 * KB], U8, name="first_scales", align_bytes=64)
+        nc.vector.memset(first_scales[:].bitcast(I32), 0)
+        load_words(0, 0, 1, placed([P, 2 * KB], U8, "first_words", 40 * KB)[:])
+        load_scales(0, 0, 3, first_scales[:])
 
         nc.vector.memset(x_bytes[:].bitcast(I32), 0)
-        nc.vector.memset(warm[:], 0.0)
-        nc.scalar.activation(warm[:, 0:1], warm[:, 1:2], SIGMOID)
         make_identity(nc, ident[:])
 
         def cast(i, a, b, engine_copy):
@@ -158,10 +154,12 @@ def tile_moe_tk_glu_sigmoid_kernel(
         gather_codes(0, 0)
         gather_codes(0, 1)
         quantize_tokens(2)
+        load_words(1, 0, 1, placed([P, 2 * KB], U8, "second_words", 18 * KB)[:])
+        load_scales(1, 0, 3, placed([P, 3 * KB], U8, "second_scales", 15 * KB)[:])
         load_weights(1, 2, placed([P, 4 * KB], U8, "second_weights", 20 * KB)[:])
         shift_bytes((1,), gather_bytes(BYTE_PIECES[0], "s_bytes")[:, C:], nc.sync)
-        gather_first_codes(0, 32 * KB)
-        gather_first_codes(1, 15 * KB - 256)
+        gather_first_codes(0, 32 * KB - 256)
+        gather_first_codes(1, 10 * KB)
         gather_codes(1, 1)
         shift_bytes(BYTE_PIECES[1], gather_bytes(BYTE_PIECES[1], "s_bytes"), nc.sync)
 
@@ -177,7 +175,7 @@ def tile_moe_tk_glu_sigmoid_kernel(
                 out=bank[:],
                 lhsT=s_codes[s, e, st].bitcast(FP8X4),
                 lhsT_scale=s_bytes[s, e][:, slots],
-                rhs=w_tiles[e][:, m, s, :].bitcast(FP4X4),
+                rhs=w_tiles[m, e][:, s, :].bitcast(FP4X4),
                 rhs_scale=w_scales[m, e][:, s, :],
                 start=opens,
                 stop=not opens,
@@ -204,15 +202,18 @@ def tile_moe_tk_glu_sigmoid_kernel(
             nc.vector.tensor_tensor(h[:], banks[1][:].rearrange("s (p u d) -> s u p d", u=2, d=2), sig[:], MULT)
             h_tiles[e, st] = h
 
-        def turn(e, tiles, k, engine_copy):
+        def turn(e, tiles, k, engine_copy, h_bf):
             n = len(tiles) * P
             turned = psum.tile([P, 2, n], F32, name=f"bank_a{k % 3}")
             for x, st in enumerate(tiles):
                 words = h_tiles[e, st][:].rearrange("s u p d -> s (u p d)").bitcast(F32)
                 for u in range(2):
                     nc.tensor.transpose(turned[:, u, x * P : (x + 1) * P], words[:, u * P : (u + 1) * P], ident[:])
-            h_bf = work.tile([P, 4 * n], BF16, name="h_bf", align_bytes=64)
-            engine_copy(h_bf[:].bitcast(F32).rearrange("p (r u) -> p r u", u=2), turned[:].rearrange("p u r -> p r u"))
+            engine_copy(h_bf.bitcast(F32).rearrange("p (r u) -> p r u", u=2), turned[:].rearrange("p u r -> p r u"))
+
+        def turn_alone(e, tiles, k, engine_copy):
+            h_bf = work.tile([P, 4 * P * len(tiles)], BF16, name="h_bf", align_bytes=64)
+            turn(e, tiles, k, engine_copy, h_bf[:])
             return h_bf
 
         def quantize_hidden(h_bf):
@@ -220,7 +221,7 @@ def tile_moe_tk_glu_sigmoid_kernel(
             h_codes = work.tile([P, n], U32, name="h_codes", align_bytes=64)
             h_bytes = work.tile([P, n], U8, name="h_bytes", align_bytes=64)
             nc.vector.quantize_mx(out=h_codes[:].bitcast(FP8X4), scales=h_bytes[:], in_=h_bf[:])
-            return h_codes, h_bytes
+            return h_codes[:], h_bytes[:]
 
         second = {}
 
@@ -237,8 +238,8 @@ def tile_moe_tk_glu_sigmoid_kernel(
                 out=target,
                 lhsT=second["t"][:, e, :].bitcast(FP4X4),
                 lhsT_scale=second["s"][:, e, :],
-                rhs=h_codes[:].bitcast(FP8X4),
-                rhs_scale=h_bytes[:],
+                rhs=h_codes.bitcast(FP8X4),
+                rhs_scale=h_bytes,
                 start=True,
                 stop=True,
             )
@@ -259,15 +260,19 @@ def tile_moe_tk_glu_sigmoid_kernel(
         last = E - 1
         for e in range(E):
             first_layer(e)
-            if e >= 3 and e % 2 == 1:
-                second_layer(e - 3)
-                second_layer(e - 2)
+            if e in (4, 6, 7):
+                done = e - 4 + e % 2
+                second_layer(done)
+                second_layer(done + 1)
             if e >= 2 and e % 2 == 0:
-                pair = [turn(e - 2 + x, (0, 1), 2 * e + x, nc.scalar.copy) for x in range(2)]
+                h_bf = work.tile([P, 8 * C], BF16, name="h_bf", align_bytes=64)
                 for x in range(2):
-                    quantized[e - 2 + x] = quantize_hidden(pair[x])
+                    turn(e - 2 + x, (0, 1), 2 * e + x, nc.scalar.copy, h_bf[:, 4 * C * x : 4 * C * (x + 1)])
+                h_codes, h_bytes = quantize_hidden(h_bf)
+                for x in range(2):
+                    quantized[e - 2 + x] = (h_codes[:, x * C : (x + 1) * C], h_bytes[:, x * C : (x + 1) * C])
             if e == last:
-                quantized[e - 1] = quantize_hidden(turn(e - 1, (0, 1), 2 * e, nc.scalar.copy))
+                quantized[e - 1] = quantize_hidden(turn_alone(e - 1, (0, 1), 2 * e, nc.scalar.copy))
             if e % 2 == 1 and (e + 3) // 2 < len(BYTE_PIECES):
                 piece = BYTE_PIECES[(e + 3) // 2]
                 shift_bytes(piece, gather_bytes(piece, "s_bytes"), nc.sync)
@@ -276,26 +281,27 @@ def tile_moe_tk_glu_sigmoid_kernel(
                 gather_codes(0, e + 2)
             if e == 0:
                 load_weights(2, 4, placed([P, 8 * KB], U8, "third_weights", 32 * KB)[:])
-                load_scales(3, E, [placed([P, 5 * KB], U8, f"late_scales{m}", (10 + 5 * m) * KB)[:] for m in range(2)])
+                load_scales(0, 3, E, placed([P, 5 * KB], U8, "late_scales0", 27 * KB)[:])
+                load_scales(1, 3, E, placed([P, 5 * KB], U8, "late_scales1", 10 * KB)[:])
                 load_second()
             if e == 1:
-                load_weights(4, 6, placed([P, 8 * KB], U8, "fourth_weights", 20 * KB)[:])
+                load_weights(4, 6, placed([P, 8 * KB], U8, "fourth_weights", 18 * KB)[:])
             if e == 3:
                 load_weights(6, 8, placed([P, 8 * KB], U8, "fifth_weights", 32 * KB)[:])
             if e == 5:
-                last_gate = placed([P, T], F32, "last_gate", 20 * KB)
+                last_gate = placed([P, T], F32, "last_gate", 18 * KB)
                 nc.sync.dma_start(last_gate[:], gate[TOP - 1])
-                gate_cols = placed([P, TOP - 1, 8], F32, "gate_cols", 22 * KB)
+                gate_cols = placed([P, TOP - 1, 8], F32, "gate_cols", 20 * KB)
                 with nc.allow_non_contiguous_dma(reason="one gate a token, tokens on the partitions"):
                     for r in range(TOP - 1):
                         nc.sync.dma_start(gate_cols[:, r, 0:BLOCKS], gate[r, 0].rearrange("(b t) -> t b", t=P))
 
-        first = quantize_hidden(turn(last, (0,), 2 * last + 2, nc.scalar.copy))
+        first = quantize_hidden(turn_alone(last, (0,), 2 * last + 2, nc.scalar.copy))
         second_layer(last - 1)
         y_bank = y_banks[last - 1]
         multiply_2(last, y_bank[:, C : C + P], *first)
         nc.scalar.copy(y_t[:, (last - 1) * C : last * C + P], y_bank[:, 0 : C + P])
-        final = quantize_hidden(turn(last, (1,), 2 * last + 1, nc.vector.tensor_copy))
+        final = quantize_hidden(turn_alone(last, (1,), 2 * last + 1, nc.vector.tensor_copy))
         y_last = psum.tile([P, P], F32, name="bank_b0")
         multiply_2(last, y_last[:], *final)
         nc.vector.tensor_copy(y_t[:, last * C + P :], y_last[:])

@@ -12,7 +12,6 @@ U8 = mybir.dt.uint8
 FP8X4 = mybir.dt.float8_e4m3fn_x4
 FP4X4 = mybir.dt.float4_e2m1fn_x4
 SIGMOID = mybir.ActivationFunctionType.Sigmoid
-COPY = mybir.ActivationFunctionType.Copy
 MULT = mybir.AluOpType.mult
 ADD = mybir.AluOpType.add
 
@@ -23,7 +22,6 @@ PASSES = K // 512
 FLOPS = 2 * SLOTS * (2 * K * H + H * N)
 
 KB = 1024
-BLOCKS = T // P
 VECTOR_CAST = (176, 176, 176)
 BYTE_PIECES = ((0, 1), (2, 3), (4, 5), (6, 7))
 
@@ -150,7 +148,12 @@ def tile_moe_tk_glu_sigmoid_kernel(
         quantize_tokens(0)
         quantize_tokens(1)
         shifted = placed([P, SLOTS], U8, "shifted", 8 * KB)
-        shift_bytes((0,), gather_bytes((0,), "first_bytes"), nc.sync)
+        first_bytes = gather_bytes((0,), "first_bytes")
+        for row, rows in ((0, 64), (64, 32), (96, 4)):
+            nc.sync.dma_start(
+                shifted[row : row + rows, 0:C].bitcast(I32), first_bytes[row + 4 : row + 4 + rows].bitcast(I32)
+            )
+        s_bytes[0, 0] = shifted[:, 0:C]
         gather_codes(0, 0)
         gather_codes(0, 1)
         quantize_tokens(2)
@@ -289,12 +292,8 @@ def tile_moe_tk_glu_sigmoid_kernel(
             if e == 3:
                 load_weights(6, 8, placed([P, 8 * KB], U8, "fifth_weights", 32 * KB)[:])
             if e == 5:
-                last_gate = placed([P, T], F32, "last_gate", 18 * KB)
-                nc.sync.dma_start(last_gate[:], gate[TOP - 1])
-                gate_cols = placed([P, TOP - 1, 8], F32, "gate_cols", 20 * KB)
-                with nc.allow_non_contiguous_dma(reason="one gate a token, tokens on the partitions"):
-                    for r in range(TOP - 1):
-                        nc.sync.dma_start(gate_cols[:, r, 0:BLOCKS], gate[r, 0].rearrange("(b t) -> t b", t=P))
+                gates = placed([P, TOP, T], F32, "gates", 18 * KB)
+                nc.sync.dma_start(gates[:], gate.rearrange("r p t -> p r t"))
 
         first = quantize_hidden(turn_alone(last, (0,), 2 * last + 2, nc.scalar.copy))
         second_layer(last - 1)
@@ -306,25 +305,13 @@ def tile_moe_tk_glu_sigmoid_kernel(
         multiply_2(last, y_last[:], *final)
         nc.vector.tensor_copy(y_t[:, last * C + P :], y_last[:])
 
-        sums = [psum.tile([P, P], F32, name=f"bank_b{b}") for b in range(BLOCKS)]
-        for r in range(TOP - 1):
-            picked = keep.tile([P, T], F32, name=f"picked{r}", align_bytes=64)
-            nc.vector.tensor_copy(picked[:], y_t[:].indirect(pos_t[r][:]))
-            by_token = psum.tile([P, BLOCKS, N], F32, name=f"bank_a{r}")
-            weighted = keep.tile([P, BLOCKS, N], F32, name=f"weighted{r}", align_bytes=64)
-            for b in range(BLOCKS):
-                nc.tensor.transpose(by_token[:, b], picked[:, b * P : (b + 1) * P], ident[:])
-            for b in range(BLOCKS):
-                nc.scalar.activation(weighted[:, b], by_token[:, b], COPY, scale=gate_cols[:, r, b : b + 1])
-            for b in range(BLOCKS):
-                nc.tensor.matmul(
-                    sums[b][:], weighted[:, b], ident[:], start=(r == 0), stop=(r == TOP - 2), is_transpose=True
-                )
-        part = keep.tile([P, T], F32, name="part", align_bytes=64)
-        nc.vector.tensor_tensor(part[:], y_t[:].indirect(pos_t[TOP - 1][:]), last_gate[:], MULT)
-        for b in range(BLOCKS):
-            cols = slice(b * P, (b + 1) * P)
-            nc.vector.tensor_tensor(out_t[:, cols], sums[b][:], part[:, cols], ADD)
-            if b % 2 == 1:
-                pair = slice((b - 1) * P, (b + 1) * P)
-                nc.sync.dma_start(out[:, pair], out_t[:, pair])
+        parts = keep.tile([P, TOP, T], F32, name="parts", align_bytes=64)
+        for r in range(TOP):
+            nc.vector.tensor_tensor(parts[:, r], y_t[:].indirect(pos_t[r][:]), gates[:, r], MULT)
+        pairs = keep.tile([P, 2, T], F32, name="pairs", align_bytes=64)
+        nc.vector.tensor_tensor(pairs[:], parts[:, 0:2], parts[:, 2:4], ADD)
+        half = T // 2
+        for hf in range(2):
+            cols = slice(hf * half, (hf + 1) * half)
+            nc.vector.tensor_tensor(out_t[:, cols], pairs[:, 0, cols], pairs[:, 1, cols], ADD)
+            nc.sync.dma_start(out[:, cols], out_t[:, cols])

@@ -19,11 +19,32 @@ P = 128
 K, T, E, C, H, N, TOP = 1024, 512, 8, 256, 512, 128, 4
 SLOTS = E * C
 PASSES = K // 512
+LAST = E - 1
 FLOPS = 2 * SLOTS * (2 * K * H + H * N)
 
+X_PIECES = ((0, 0, T // 2), (0, T // 2, T), (1, 0, T // 2), (1, T // 2, T))
+VECTOR_CAST = (176, 176, 0, 176)
+EARLY = 3
+SHIFT_ROWS = ((0, 64), (64, 4), (96, 4))
+A_BANKS = 3
+B_BANKS = 4
+
 KB = 1024
-VECTOR_CAST = (176, 176, 176)
-BYTE_PIECES = ((0, 1), (2, 3), (4, 5), (6, 7))
+AT_X_RAW = 8 * KB
+AT_X_BF = (28 * KB, 24 * KB)
+AT_SHIFTED = 8 * KB
+AT_W1_FIRST = 40 * KB
+AT_W3_FIRST_SCALES = 15 * KB
+AT_W3_FIRST = 18 * KB
+AT_EXPERT_1 = 20 * KB
+AT_FIRST_CODES = (32 * KB - 256, 10 * KB)
+AT_EXPERTS_2_3 = 32 * KB
+AT_LATE_SCALES = (27 * KB, 10 * KB)
+AT_W2_SCALES = 40 * KB
+AT_W2 = 41 * KB
+AT_EXPERTS_4_5 = 18 * KB
+AT_EXPERTS_6_7 = 32 * KB
+AT_GATES = 18 * KB
 
 
 def tile_moe_tk_glu_sigmoid_kernel(
@@ -44,9 +65,8 @@ def tile_moe_tk_glu_sigmoid_kernel(
         offs_t = lists.tile([P, SLOTS // 16], U16, name="offs_t")
         pos_t = [lists.tile([P, T // 16], U16, name=f"pos{r}_t") for r in range(TOP)]
 
-        x_pieces = ((0, 0, T // 2), (0, T // 2, T), (1, 0, T))
-        x_raw = [placed([P, 4, b - a], F32, f"x_raw{s}_{a}", 8 * KB * (s + 1) + 16 * a) for s, a, b in x_pieces]
-        x_bf = [placed([P, T, 4], BF16, f"x_bf{s}", 28 * KB - 4 * KB * s) for s in range(PASSES)]
+        x_raw = [placed([P, 4, T // 2], F32, f"x_raw{i}", AT_X_RAW + 4 * KB * i) for i in range(len(X_PIECES))]
+        x_bf = [placed([P, T, 4], BF16, f"x_bf{s}", AT_X_BF[s]) for s in range(PASSES)]
         x_codes = [keep.tile([P, T], U32, name=f"x_codes{s}", align_bytes=64) for s in range(PASSES)]
         x_bytes = keep.tile([P, 2 * T], U8, name="x_bytes", align_bytes=64)
         y_t = keep.tile([P, SLOTS], F32, name="y_t", align_bytes=64)
@@ -54,7 +74,7 @@ def tile_moe_tk_glu_sigmoid_kernel(
         ident = keep.tile([P, P], F32, name="ident", align_bytes=64)
 
         def load_tokens(i):
-            s, a, b = x_pieces[i]
+            s, a, b = X_PIECES[i]
             nc.sync.dma_start(x_raw[i][:], xT[512 * s : 512 * (s + 1), a:b].rearrange("(p j) w -> p j w", j=4))
 
         load_tokens(0)
@@ -63,140 +83,129 @@ def tile_moe_tk_glu_sigmoid_kernel(
         for r, src in enumerate((pos1, pos2, pos3, pos4)):
             nc.sync.dma_start(pos_t[r][:], src)
         load_tokens(2)
+        load_tokens(3)
 
         w_scales = {}
-        w_tiles = {}
+        w_words = {}
 
-        def load_scale_rows(t, view):
+        def load_scale_rows(plane, rows):
             for r in range(4):
-                nc.sync.dma_start(t[r:P:32], view[r:16:4])
+                nc.sync.dma_start(plane[r:P:32], rows[r:16:4])
 
         def load_scales(m, e0, e1, room):
-            t = room.rearrange("p (g i) -> p g i", i=H)
-            view = (w1_scales, w3_scales)[m].bitcast(I32).rearrange("e s q i -> q (e s) i")
-            load_scale_rows(t.bitcast(I32), view[:, e0 * PASSES : e1 * PASSES, :])
+            planes = room.rearrange("p (g i) -> p g i", i=H)
+            rows = (w1_scales, w3_scales)[m].bitcast(I32).rearrange("e s q i -> q (e s) i")
+            load_scale_rows(planes.bitcast(I32), rows[:, e0 * PASSES : e1 * PASSES, :])
             for e in range(e0, e1):
-                w_scales[m, e] = t[:, (e - e0) * PASSES : (e - e0 + 1) * PASSES, :]
+                w_scales[m, e] = planes[:, (e - e0) * PASSES : (e - e0 + 1) * PASSES, :]
 
         def load_words(m, e0, e1, room):
-            w = room.rearrange("p (g c) -> p g c", c=2 * H)
-            view = (w1_words, w3_words)[m].bitcast(I32)[e0:e1].rearrange("e s p c -> p (e s) c")
-            nc.sync.dma_start(w.bitcast(I32), view)
+            words = room.rearrange("p (g c) -> p g c", c=2 * H)
+            src = (w1_words, w3_words)[m].bitcast(I32)[e0:e1].rearrange("e s p c -> p (e s) c")
+            nc.sync.dma_start(words.bitcast(I32), src)
             for e in range(e0, e1):
-                w_tiles[m, e] = w[:, (e - e0) * PASSES : (e - e0 + 1) * PASSES, :]
+                w_words[m, e] = words[:, (e - e0) * PASSES : (e - e0 + 1) * PASSES, :]
 
-        def load_weights(e0, e1, room):
-            size = (e1 - e0) * 2 * KB
+        def load_weights(e0, e1, name, offset):
+            size = (e1 - e0) * PASSES * 2 * H
+            room = placed([P, 2 * size], U8, name, offset)
             for m in range(2):
                 load_words(m, e0, e1, room[:, m * size : (m + 1) * size])
 
-        first_scales = keep.tile([P, 3 * KB], U8, name="first_scales", align_bytes=64)
+        first_scales = keep.tile([P, EARLY * PASSES * H], U8, name="first_scales", align_bytes=64)
         nc.vector.memset(first_scales[:].bitcast(I32), 0)
-        load_words(0, 0, 1, placed([P, 2 * KB], U8, "first_words", 40 * KB)[:])
-        load_scales(0, 0, 3, first_scales[:])
+        load_words(0, 0, 1, placed([P, PASSES * 2 * H], U8, "w1_first", AT_W1_FIRST)[:])
+        load_scales(0, 0, EARLY, first_scales[:])
 
         nc.vector.memset(x_bytes[:].bitcast(I32), 0)
         make_identity(nc, ident[:])
 
         def cast(i, a, b, engine_copy):
-            s, first = x_pieces[i][0:2]
+            s, first = X_PIECES[i][0:2]
             engine_copy(
                 x_bf[s][:, first + a : first + b, :].rearrange("p (c i) j -> p c j i", i=4),
                 x_raw[i][:, :, a:b].rearrange("p j (c i) -> p c j i", i=4),
             )
 
         def quantize_tokens(i):
-            s, a, b = x_pieces[i]
+            s, a, b = X_PIECES[i]
             cast(i, VECTOR_CAST[i], b - a, nc.scalar.copy)
-            cast(i, 0, VECTOR_CAST[i], nc.vector.tensor_copy)
+            if VECTOR_CAST[i]:
+                cast(i, 0, VECTOR_CAST[i], nc.vector.tensor_copy)
             nc.vector.quantize_mx(
                 out=x_codes[s][:, a:b].bitcast(FP8X4),
                 scales=x_bytes[4 * (1 - s) : P, a:b],
                 in_=x_bf[s][:, a:b].rearrange("p w j -> p (w j)"),
             )
 
-        s_codes = {}
-        s_bytes = {}
+        slot_codes = {}
+        slot_bytes = {}
 
-        def gather_bytes(experts, name):
-            n = len(experts) * C
-            a = experts[0] * C
-            both = gathered.tile([P, n], U8, name=name, align_bytes=64)
-            nc.vector.tensor_copy(both[:], x_bytes[:].indirect(offs_t[:, a // 16 : (a + n) // 16]))
-            for x, e in enumerate(experts):
-                s_bytes[1, e] = both[:, x * C : (x + 1) * C]
+        def entries(first, count):
+            return offs_t[:, first // 16 : (first + count) // 16]
+
+        def gather_bytes(e0, e1, name):
+            both = gathered.tile([P, (e1 - e0) * C], U8, name=name, align_bytes=64)
+            nc.vector.tensor_copy(both[:], x_bytes[:].indirect(entries(e0 * C, (e1 - e0) * C)))
+            for e in range(e0, e1):
+                slot_bytes[1, e] = both[:, (e - e0) * C : (e - e0 + 1) * C]
             return both
 
-        def shift_bytes(experts, source, queue):
-            n = len(experts) * C
-            a = experts[0] * C
-            queue.dma_start(shifted[0 : P - 4, a : a + n].bitcast(I32), source[4:P].bitcast(I32))
-            for e in experts:
-                s_bytes[0, e] = shifted[:, e * C : (e + 1) * C]
+        def shift_bytes(e0, e1, both):
+            for row, rows in SHIFT_ROWS:
+                nc.sync.dma_start(
+                    shifted[row : row + rows, e0 * C : e1 * C].bitcast(I32),
+                    both[row + 4 : row + 4 + rows].bitcast(I32),
+                )
+            for e in range(e0, e1):
+                slot_bytes[0, e] = shifted[:, e * C : (e + 1) * C]
 
         def gather_codes(s, e):
-            codes = gathered.tile([P, C], U32, name=f"s_codes{s}", align_bytes=64)
-            nc.vector.tensor_copy(codes[:], x_codes[s][:].indirect(offs_t[:, e * C // 16 : (e + 1) * C // 16]))
+            codes = gathered.tile([P, C], U32, name=f"slot_codes{s}", align_bytes=64)
+            nc.vector.tensor_copy(codes[:], x_codes[s][:].indirect(entries(e * C, C)))
             for st in range(2):
-                s_codes[s, e, st] = codes[:, st * P : (st + 1) * P]
+                slot_codes[s, e, st] = codes[:, st * P : (st + 1) * P]
 
-        def gather_first_codes(st, offset):
-            codes = placed([P, P], U32, f"first_codes{st}", offset)
-            nc.vector.tensor_copy(codes[:], x_codes[1][:].indirect(offs_t[:, st * P // 16 : (st + 1) * P // 16]))
-            s_codes[1, 0, st] = codes[:]
+        def gather_first_codes(st):
+            codes = placed([P, P], U32, f"first_codes{st}", AT_FIRST_CODES[st])
+            nc.vector.tensor_copy(codes[:], x_codes[1][:].indirect(entries(st * P, P)))
+            slot_codes[1, 0, st] = codes[:]
 
         quantize_tokens(0)
         quantize_tokens(1)
-        shifted = placed([P, SLOTS], U8, "shifted", 8 * KB)
-        first_bytes = gather_bytes((0,), "first_bytes")
-        for row, rows in ((0, 64), (64, 32), (96, 4)):
-            nc.sync.dma_start(
-                shifted[row : row + rows, 0:C].bitcast(I32), first_bytes[row + 4 : row + 4 + rows].bitcast(I32)
-            )
-        s_bytes[0, 0] = shifted[:, 0:C]
+        shifted = placed([P, SLOTS], U8, "shifted", AT_SHIFTED)
+        shift_bytes(0, 1, gather_bytes(0, 1, "first_bytes"))
         gather_codes(0, 0)
         gather_codes(0, 1)
         quantize_tokens(2)
-        load_words(1, 0, 1, placed([P, 2 * KB], U8, "second_words", 18 * KB)[:])
-        load_scales(1, 0, 3, placed([P, 3 * KB], U8, "second_scales", 15 * KB)[:])
-        load_weights(1, 2, placed([P, 4 * KB], U8, "second_weights", 20 * KB)[:])
-        shift_bytes((1,), gather_bytes(BYTE_PIECES[0], "s_bytes")[:, C:], nc.sync)
-        gather_first_codes(0, 32 * KB - 256)
-        gather_first_codes(1, 10 * KB)
+        quantize_tokens(3)
+        load_words(1, 0, 1, placed([P, PASSES * 2 * H], U8, "w3_first", AT_W3_FIRST)[:])
+        load_scales(1, 0, EARLY, placed([P, EARLY * PASSES * H], U8, "w3_first_scales", AT_W3_FIRST_SCALES)[:])
+        load_weights(1, 2, "expert_1", AT_EXPERT_1)
+        shift_bytes(1, 2, gather_bytes(0, 2, "slot_bytes")[:, C:])
+        gather_first_codes(0)
+        gather_first_codes(1)
         gather_codes(1, 1)
-        shift_bytes(BYTE_PIECES[1], gather_bytes(BYTE_PIECES[1], "s_bytes"), nc.sync)
+        shift_bytes(2, 4, gather_bytes(2, 4, "slot_bytes"))
 
         h_tiles = {}
 
-        def first_banks(e, st):
-            k = 2 * e + st
-            return [psum.tile([P, H], F32, name=f"bank_a{k % 3}"), psum.tile([P, H], F32, name=f"bank_b{k % 4}")]
+        def a_bank(shape, count):
+            return psum.tile(shape, F32, name=f"bank_a{count % A_BANKS}")
+
+        def b_bank(shape, count):
+            return psum.tile(shape, F32, name=f"bank_b{count % B_BANKS}")
 
         def multiply_1(e, st, m, s, bank, opens):
-            slots = slice(st * P, (st + 1) * P)
             nc.tensor.matmul_mx(
                 out=bank[:],
-                lhsT=s_codes[s, e, st].bitcast(FP8X4),
-                lhsT_scale=s_bytes[s, e][:, slots],
-                rhs=w_tiles[m, e][:, s, :].bitcast(FP4X4),
+                lhsT=slot_codes[s, e, st].bitcast(FP8X4),
+                lhsT_scale=slot_bytes[s, e][:, st * P : (st + 1) * P],
+                rhs=w_words[m, e][:, s, :].bitcast(FP4X4),
                 rhs_scale=w_scales[m, e][:, s, :],
                 start=opens,
                 stop=not opens,
             )
-
-        def first_layer(e):
-            banks = [first_banks(e, st) for st in range(2)]
-            opening = 0 if e == 0 else 1
-            if e < 2:
-                for m in range(2):
-                    for st in range(2):
-                        multiply_1(e, st, m, opening, banks[st][m], True)
-            for st in range(2):
-                for m in range(2):
-                    if e >= 2:
-                        multiply_1(e, st, m, opening, banks[st][m], True)
-                    multiply_1(e, st, m, 1 - opening, banks[st][m], False)
-                activate(e, st, banks[st])
 
         def activate(e, st, banks):
             sig = work.tile([P, 2, P, 2], F32, name="sig", align_bytes=64)
@@ -205,19 +214,29 @@ def tile_moe_tk_glu_sigmoid_kernel(
             nc.vector.tensor_tensor(h[:], banks[1][:].rearrange("s (p u d) -> s u p d", u=2, d=2), sig[:], MULT)
             h_tiles[e, st] = h
 
-        def turn(e, tiles, k, engine_copy, h_bf):
+        def first_layer(e):
+            banks = [(a_bank([P, H], 2 * e + st), b_bank([P, H], 2 * e + st)) for st in range(2)]
+            opening = 0 if e == 0 else 1
+            opens_all = e < 2
+            if opens_all:
+                for m in range(2):
+                    for st in range(2):
+                        multiply_1(e, st, m, opening, banks[st][m], True)
+            for st in range(2):
+                for m in range(2):
+                    if not opens_all:
+                        multiply_1(e, st, m, opening, banks[st][m], True)
+                    multiply_1(e, st, m, 1 - opening, banks[st][m], False)
+                activate(e, st, banks[st])
+
+        def turn(e, tiles, count, h_bf):
             n = len(tiles) * P
-            turned = psum.tile([P, 2, n], F32, name=f"bank_a{k % 3}")
+            turned = a_bank([P, 2, n], count)
             for x, st in enumerate(tiles):
                 words = h_tiles[e, st][:].rearrange("s u p d -> s (u p d)").bitcast(F32)
                 for u in range(2):
                     nc.tensor.transpose(turned[:, u, x * P : (x + 1) * P], words[:, u * P : (u + 1) * P], ident[:])
-            engine_copy(h_bf.bitcast(F32).rearrange("p (r u) -> p r u", u=2), turned[:].rearrange("p u r -> p r u"))
-
-        def turn_alone(e, tiles, k, engine_copy):
-            h_bf = work.tile([P, 4 * P * len(tiles)], BF16, name="h_bf", align_bytes=64)
-            turn(e, tiles, k, engine_copy, h_bf[:])
-            return h_bf
+            nc.scalar.copy(h_bf.bitcast(F32).rearrange("p (r u) -> p r u", u=2), turned[:].rearrange("p u r -> p r u"))
 
         def quantize_hidden(h_bf):
             n = h_bf.shape[1] // 4
@@ -226,92 +245,95 @@ def tile_moe_tk_glu_sigmoid_kernel(
             nc.vector.quantize_mx(out=h_codes[:].bitcast(FP8X4), scales=h_bytes[:], in_=h_bf[:])
             return h_codes[:], h_bytes[:]
 
-        second = {}
+        def turn_and_quantize(e, tiles, count):
+            h_bf = work.tile([P, 4 * P * len(tiles)], BF16, name="h_bf", align_bytes=64)
+            turn(e, tiles, count, h_bf[:])
+            return quantize_hidden(h_bf)
 
-        def load_second():
-            w2_s = placed([P, E, N], U8, "w2_s", 40 * KB)[:]
-            w2_t = placed([P, E, 2 * N], U8, "w2_t", 41 * KB)[:]
-            load_scale_rows(w2_s.bitcast(I32), w2_scales.bitcast(I32).rearrange("e s q i -> q (e s) i"))
-            nc.sync.dma_start(w2_t.bitcast(I32), w2_words.bitcast(I32).rearrange("e s p c -> p (e s) c"))
-            second["s"] = w2_s
-            second["t"] = w2_t
+        hidden = {}
+
+        def turn_and_quantize_pair(e):
+            h_bf = work.tile([P, 8 * C], BF16, name="h_bf", align_bytes=64)
+            for x in range(2):
+                turn(e + x, (0, 1), 2 * (e + 2) + x, h_bf[:, 4 * C * x : 4 * C * (x + 1)])
+            h_codes, h_bytes = quantize_hidden(h_bf)
+            for x in range(2):
+                hidden[e + x] = (h_codes[:, x * C : (x + 1) * C], h_bytes[:, x * C : (x + 1) * C])
+
+        w2 = {}
+
+        def load_w2():
+            w2["scales"] = placed([P, E, N], U8, "w2_planes", AT_W2_SCALES)[:]
+            w2["words"] = placed([P, E, 2 * N], U8, "w2_codes", AT_W2)[:]
+            load_scale_rows(w2["scales"].bitcast(I32), w2_scales.bitcast(I32).rearrange("e s q i -> q (e s) i"))
+            nc.sync.dma_start(w2["words"].bitcast(I32), w2_words.bitcast(I32).rearrange("e s p c -> p (e s) c"))
 
         def multiply_2(e, target, h_codes, h_bytes):
             nc.tensor.matmul_mx(
                 out=target,
-                lhsT=second["t"][:, e, :].bitcast(FP4X4),
-                lhsT_scale=second["s"][:, e, :],
+                lhsT=w2["words"][:, e, :].bitcast(FP4X4),
+                lhsT_scale=w2["scales"][:, e, :],
                 rhs=h_codes.bitcast(FP8X4),
                 rhs_scale=h_bytes,
                 start=True,
                 stop=True,
             )
 
-        quantized = {}
-        y_banks = {}
+        def second_layer_pair(e, engine_copy):
+            y_bank = psum.tile([P, 2 * C], F32, name="y_bank")
+            for x in range(2):
+                multiply_2(e + x, y_bank[:, x * C : (x + 1) * C], *hidden[e + x])
+            engine_copy(y_t[:, e * C : (e + 2) * C], y_bank[:])
 
-        def second_layer(e):
-            if e % 2 == 0:
-                y_bank = psum.tile([P, 2 * C], F32, name="y_bank")
-                y_banks[e] = y_bank
-                multiply_2(e, y_bank[:, 0:C], *quantized[e])
-            else:
-                y_bank = y_banks[e - 1]
-                multiply_2(e, y_bank[:, C : 2 * C], *quantized[e])
-                nc.scalar.copy(y_t[:, (e - 1) * C : (e + 1) * C], y_bank[:])
-
-        last = E - 1
         for e in range(E):
             first_layer(e)
-            if e in (4, 6, 7):
-                done = e - 4 + e % 2
-                second_layer(done)
-                second_layer(done + 1)
-            if e >= 2 and e % 2 == 0:
-                h_bf = work.tile([P, 8 * C], BF16, name="h_bf", align_bytes=64)
-                for x in range(2):
-                    turn(e - 2 + x, (0, 1), 2 * e + x, nc.scalar.copy, h_bf[:, 4 * C * x : 4 * C * (x + 1)])
-                h_codes, h_bytes = quantize_hidden(h_bf)
-                for x in range(2):
-                    quantized[e - 2 + x] = (h_codes[:, x * C : (x + 1) * C], h_bytes[:, x * C : (x + 1) * C])
-            if e == last:
-                quantized[e - 1] = quantize_hidden(turn_alone(e - 1, (0, 1), 2 * e, nc.scalar.copy))
-            if e % 2 == 1 and (e + 3) // 2 < len(BYTE_PIECES):
-                piece = BYTE_PIECES[(e + 3) // 2]
-                shift_bytes(piece, gather_bytes(piece, "s_bytes"), nc.sync)
+            if e == LAST:
+                second_layer_pair(e - 3, nc.vector.tensor_copy)
+                hidden[e - 1] = turn_and_quantize(e - 1, (0, 1), 2 * e)
+            elif e % 2 == 0:
+                if e >= 4:
+                    second_layer_pair(e - 4, nc.scalar.copy)
+                if e >= 2:
+                    turn_and_quantize_pair(e - 2)
+            elif e + 3 < E:
+                shift_bytes(e + 3, e + 5, gather_bytes(e + 3, e + 5, "slot_bytes"))
             if e + 2 < E:
                 gather_codes(1, e + 2)
                 gather_codes(0, e + 2)
             if e == 0:
-                load_weights(2, 4, placed([P, 8 * KB], U8, "third_weights", 32 * KB)[:])
-                load_scales(0, 3, E, placed([P, 5 * KB], U8, "late_scales0", 27 * KB)[:])
-                load_scales(1, 3, E, placed([P, 5 * KB], U8, "late_scales1", 10 * KB)[:])
-                load_second()
+                load_weights(2, 4, "experts_2_3", AT_EXPERTS_2_3)
+                for m in range(2):
+                    room = placed([P, (E - EARLY) * PASSES * H], U8, f"late_scales{m}", AT_LATE_SCALES[m])
+                    load_scales(m, EARLY, E, room[:])
+                load_w2()
             if e == 1:
-                load_weights(4, 6, placed([P, 8 * KB], U8, "fourth_weights", 18 * KB)[:])
+                load_weights(4, 6, "experts_4_5", AT_EXPERTS_4_5)
             if e == 3:
-                load_weights(6, 8, placed([P, 8 * KB], U8, "fifth_weights", 32 * KB)[:])
+                load_weights(6, 8, "experts_6_7", AT_EXPERTS_6_7)
             if e == 5:
-                gates = placed([P, TOP, T], F32, "gates", 18 * KB)
+                gates = placed([P, TOP, T], F32, "gates", AT_GATES)
                 nc.sync.dma_start(gates[:], gate.rearrange("r p t -> p r t"))
 
-        first = quantize_hidden(turn_alone(last, (0,), 2 * last + 2, nc.scalar.copy))
-        second_layer(last - 1)
-        y_bank = y_banks[last - 1]
-        multiply_2(last, y_bank[:, C : C + P], *first)
-        nc.scalar.copy(y_t[:, (last - 1) * C : last * C + P], y_bank[:, 0 : C + P])
-        final = quantize_hidden(turn_alone(last, (1,), 2 * last + 1, nc.vector.tensor_copy))
-        y_last = psum.tile([P, P], F32, name="bank_b0")
-        multiply_2(last, y_last[:], *final)
-        nc.vector.tensor_copy(y_t[:, last * C + P :], y_last[:])
+        last_hidden = turn_and_quantize(LAST, (0,), 2 * LAST + 2)
+        y_before = b_bank([P, C + P], 2 * LAST - 1)
+        multiply_2(LAST - 1, y_before[:, 0:C], *hidden[LAST - 1])
+        multiply_2(LAST, y_before[:, C:], *last_hidden)
+        nc.vector.tensor_copy(y_t[:, (LAST - 1) * C : LAST * C + P], y_before[:])
+        last_hidden = turn_and_quantize(LAST, (1,), 2 * LAST + 1)
+        y_last = b_bank([P, P], 2 * LAST - 2)
+        multiply_2(LAST, y_last[:], *last_hidden)
+        nc.scalar.copy(y_t[:, LAST * C + P :], y_last[:])
 
         parts = keep.tile([P, TOP, T], F32, name="parts", align_bytes=64)
+        two = keep.tile([P, T], F32, name="two", align_bytes=64)
+        three = keep.tile([P, T], F32, name="three", align_bytes=64)
+        halves = (slice(0, T // 2), slice(T // 2, T))
         for r in range(TOP):
+            if r == TOP - 1:
+                nc.vector.tensor_tensor(two[:], parts[:, 0], parts[:, 1], ADD)
             nc.vector.tensor_tensor(parts[:, r], y_t[:].indirect(pos_t[r][:]), gates[:, r], MULT)
-        pairs = keep.tile([P, 2, T], F32, name="pairs", align_bytes=64)
-        nc.vector.tensor_tensor(pairs[:], parts[:, 0:2], parts[:, 2:4], ADD)
-        half = T // 2
-        for hf in range(2):
-            cols = slice(hf * half, (hf + 1) * half)
-            nc.vector.tensor_tensor(out_t[:, cols], pairs[:, 0, cols], pairs[:, 1, cols], ADD)
+        for cols in halves:
+            nc.vector.tensor_tensor(three[:, cols], two[:, cols], parts[:, 2, cols], ADD)
+        for cols in halves:
+            nc.vector.tensor_tensor(out_t[:, cols], three[:, cols], parts[:, 3, cols], ADD)
             nc.sync.dma_start(out[:, cols], out_t[:, cols])

@@ -23,28 +23,38 @@ LAST = E - 1
 FLOPS = 2 * SLOTS * (2 * K * H + H * N)
 
 X_PIECES = ((0, 0, T // 2), (0, T // 2, T), (1, 0, T // 2), (1, T // 2, T))
-VECTOR_CAST = (176, 176, 0, 176)
+VECTOR_CAST = (176, 176, 0, 192)
 EARLY = 3
 SHIFT_ROWS = ((0, 64), (64, 4), (96, 4))
 A_BANKS = 3
 B_BANKS = 4
+CODES_PLACE = {2: 2, 3: 0, 4: 1, 5: 2, 6: 1, 7: 2}
+GATHER_AFTER = {1: 4, 2: 5, 4: 6, 5: 7}
+WARM_UPS = 4
 
 KB = 1024
-AT_X_RAW = 8 * KB
-AT_X_BF = (28 * KB, 24 * KB)
-AT_SHIFTED = 8 * KB
-AT_W1_FIRST = 40 * KB
-AT_W3_FIRST_SCALES = 15 * KB
-AT_W3_FIRST = 18 * KB
-AT_EXPERT_1 = 20 * KB
-AT_FIRST_CODES = (32 * KB - 256, 10 * KB)
-AT_EXPERTS_2_3 = 32 * KB
-AT_LATE_SCALES = (27 * KB, 10 * KB)
-AT_W2_SCALES = 40 * KB
-AT_W2 = 41 * KB
-AT_EXPERTS_4_5 = 18 * KB
-AT_EXPERTS_6_7 = 32 * KB
-AT_GATES = 18 * KB
+AT_X_RAW = (0, 4 * KB, 35 * KB, 12 * KB)
+AT_X_BF = (8 * KB, 16 * KB)
+AT_SHIFTED = 36 * KB
+AT_FIRST_WORDS = {
+    (0, 1): 62 * KB,
+    (1, 1): 4 * KB,
+    (0, 0): 34 * KB,
+    (1, 0): 38 * KB,
+}
+AT_W3_FIRST_SCALES = 0
+AT_FIRST_TILE = 56 * KB
+AT_EXPERT_2 = 56 * KB + 256
+AT_EXPERT_3 = 62 * KB
+AT_LATE_SCALES = (12 * KB, 4 * KB)
+AT_FIRST_CODES = {(0, 0): 47 * KB, (0, 1): 48 * KB, (1, 0): 42 * KB, (1, 1): 16 * KB}
+AT_CODES = (17 * KB, 48 * KB + 512, 19 * KB)
+AT_BYTES = (45 * KB, 46 * KB, 48 * KB, 46 * KB)
+AT_EXPERTS_4_5 = 28 * KB
+AT_W2_SCALES = 38 * KB
+AT_W2 = 39 * KB
+AT_EXPERTS_6_7 = 62 * KB
+AT_GATES = 28 * KB
 
 
 def tile_moe_tk_glu_sigmoid_kernel(
@@ -55,7 +65,6 @@ def tile_moe_tk_glu_sigmoid_kernel(
         lists = ctx.enter_context(tc.tile_pool(name="lists", bufs=1))
         places = ctx.enter_context(tc.tile_pool(name="places", bufs=1))
         keep = ctx.enter_context(tc.tile_pool(name="keep", bufs=1))
-        gathered = ctx.enter_context(tc.tile_pool(name="gathered", bufs=2))
         work = ctx.enter_context(tc.tile_pool(name="work", bufs=4))
         psum = ctx.enter_context(tc.psum_pool(name="psum", bufs=1))
 
@@ -65,7 +74,7 @@ def tile_moe_tk_glu_sigmoid_kernel(
         offs_t = lists.tile([P, SLOTS // 16], U16, name="offs_t")
         pos_t = [lists.tile([P, T // 16], U16, name=f"pos{r}_t") for r in range(TOP)]
 
-        x_raw = [placed([P, 4, T // 2], F32, f"x_raw{i}", AT_X_RAW + 4 * KB * i) for i in range(len(X_PIECES))]
+        x_raw = [placed([P, 4, T // 2], F32, f"x_raw{i}", AT_X_RAW[i]) for i in range(len(X_PIECES))]
         x_bf = [placed([P, T, 4], BF16, f"x_bf{s}", AT_X_BF[s]) for s in range(PASSES)]
         x_codes = [keep.tile([P, T], U32, name=f"x_codes{s}", align_bytes=64) for s in range(PASSES)]
         x_bytes = keep.tile([P, 2 * T], U8, name="x_bytes", align_bytes=64)
@@ -104,7 +113,15 @@ def tile_moe_tk_glu_sigmoid_kernel(
             src = (w1_words, w3_words)[m].bitcast(I32)[e0:e1].rearrange("e s p c -> p (e s) c")
             nc.sync.dma_start(words.bitcast(I32), src)
             for e in range(e0, e1):
-                w_words[m, e] = words[:, (e - e0) * PASSES : (e - e0 + 1) * PASSES, :]
+                for s in range(PASSES):
+                    w_words[m, e, s] = words[:, (e - e0) * PASSES + s, :]
+
+        def load_first_words(m, s):
+            words = placed([P, 2, 2 * H], U8, f"first_words{m}{s}", AT_FIRST_WORDS[m, s])[:]
+            src = (w1_words, w3_words)[m].bitcast(I32)[0:2, s].rearrange("e p c -> p e c")
+            nc.sync.dma_start(words.bitcast(I32), src)
+            for e in range(2):
+                w_words[m, e, s] = words[:, e, :]
 
         def load_weights(e0, e1, name, offset):
             size = (e1 - e0) * PASSES * 2 * H
@@ -114,7 +131,7 @@ def tile_moe_tk_glu_sigmoid_kernel(
 
         first_scales = keep.tile([P, EARLY * PASSES * H], U8, name="first_scales", align_bytes=64)
         nc.vector.memset(first_scales[:].bitcast(I32), 0)
-        load_words(0, 0, 1, placed([P, PASSES * 2 * H], U8, "w1_first", AT_W1_FIRST)[:])
+        load_first_words(0, 1)
         load_scales(0, 0, EARLY, first_scales[:])
 
         nc.vector.memset(x_bytes[:].bitcast(I32), 0)
@@ -144,54 +161,65 @@ def tile_moe_tk_glu_sigmoid_kernel(
         def entries(first, count):
             return offs_t[:, first // 16 : (first + count) // 16]
 
-        def gather_bytes(e0, e1, name):
-            both = gathered.tile([P, (e1 - e0) * C], U8, name=name, align_bytes=64)
-            nc.vector.tensor_copy(both[:], x_bytes[:].indirect(entries(e0 * C, (e1 - e0) * C)))
-            for e in range(e0, e1):
-                slot_bytes[1, e] = both[:, (e - e0) * C : (e - e0 + 1) * C]
-            return both
-
-        def shift_bytes(e0, e1, both):
-            for row, rows in SHIFT_ROWS:
-                nc.sync.dma_start(
-                    shifted[row : row + rows, e0 * C : e1 * C].bitcast(I32),
-                    both[row + 4 : row + 4 + rows].bitcast(I32),
-                )
-            for e in range(e0, e1):
-                slot_bytes[0, e] = shifted[:, e * C : (e + 1) * C]
-
-        def gather_codes(s, e):
-            codes = gathered.tile([P, C], U32, name=f"slot_codes{s}", align_bytes=64)
-            nc.vector.tensor_copy(codes[:], x_codes[s][:].indirect(entries(e * C, C)))
-            for st in range(2):
-                slot_codes[s, e, st] = codes[:, st * P : (st + 1) * P]
-
-        def gather_first_codes(st):
-            codes = placed([P, P], U32, f"first_codes{st}", AT_FIRST_CODES[st])
+        def gather_first_tile(st, offset):
+            codes = placed([P, P], U32, f"first_tile{st}", offset)
             nc.vector.tensor_copy(codes[:], x_codes[1][:].indirect(entries(st * P, P)))
             slot_codes[1, 0, st] = codes[:]
 
+        def gather_bytes(e0):
+            both = placed([P, 2 * C], U8, f"slot_bytes{e0}", AT_BYTES[e0 // 2])
+            if e0 == 0:
+                nc.vector.tensor_copy(both[:, :C], x_bytes[:].indirect(entries(0, C)))
+                gather_first_tile(0, AT_FIRST_TILE)
+                nc.vector.tensor_copy(both[:, C:], x_bytes[:].indirect(entries(C, C)))
+            else:
+                nc.vector.tensor_copy(both[:], x_bytes[:].indirect(entries(e0 * C, 2 * C)))
+            for row, rows in SHIFT_ROWS:
+                nc.sync.dma_start(
+                    shifted[row : row + rows, e0 * C : (e0 + 2) * C].bitcast(I32),
+                    both[row + 4 : row + 4 + rows].bitcast(I32),
+                )
+            for x in range(2):
+                slot_bytes[0, e0 + x] = shifted[:, (e0 + x) * C : (e0 + x + 1) * C]
+                slot_bytes[1, e0 + x] = both[:, x * C : (x + 1) * C]
+
+        def gather_codes(s, e, codes):
+            nc.vector.tensor_copy(codes, x_codes[s][:].indirect(entries(e * C, C)))
+            for st in range(2):
+                slot_codes[s, e, st] = codes[:, st * P : (st + 1) * P]
+
+        def gather_first_codes(s, e):
+            gather_codes(s, e, placed([P, C], U32, f"first_codes{s}{e}", AT_FIRST_CODES[s, e])[:])
+
+        def expert_codes(e):
+            return placed([P, PASSES * C], U32, f"slot_codes{e}", AT_CODES[CODES_PLACE[e]])
+
+        def gather_expert(e):
+            codes = expert_codes(e)
+            gather_codes(1, e, codes[:, C:])
+            gather_codes(0, e, codes[:, :C])
+
         quantize_tokens(0)
         quantize_tokens(1)
-        shifted = placed([P, SLOTS], U8, "shifted", AT_SHIFTED)
-        shift_bytes(0, 1, gather_bytes(0, 1, "first_bytes"))
-        gather_codes(0, 0)
-        gather_codes(0, 1)
-        quantize_tokens(2)
-        quantize_tokens(3)
-        load_words(1, 0, 1, placed([P, PASSES * 2 * H], U8, "w3_first", AT_W3_FIRST)[:])
+        load_first_words(1, 1)
         load_scales(1, 0, EARLY, placed([P, EARLY * PASSES * H], U8, "w3_first_scales", AT_W3_FIRST_SCALES)[:])
-        load_weights(1, 2, "expert_1", AT_EXPERT_1)
-        shift_bytes(1, 2, gather_bytes(0, 2, "slot_bytes")[:, C:])
-        gather_first_codes(0)
-        gather_first_codes(1)
-        gather_codes(1, 1)
-        shift_bytes(2, 4, gather_bytes(2, 4, "slot_bytes"))
+        gather_first_codes(0, 0)
+        gather_first_codes(0, 1)
+        quantize_tokens(2)
+        load_first_words(0, 0)
+        load_first_words(1, 0)
+        quantize_tokens(3)
+        shifted = placed([P, SLOTS], U8, "shifted", AT_SHIFTED)
+        gather_bytes(0)
+        gather_first_tile(1, AT_FIRST_CODES[1, 0])
+        gather_first_codes(1, 1)
 
         h_tiles = {}
 
         def a_bank(shape, count):
-            return psum.tile(shape, F32, name=f"bank_a{count % A_BANKS}")
+            if count == A_BANKS:
+                return psum.tile(shape, F32, name="y_bank")
+            return psum.tile(shape, F32, name=f"bank_a{(count - (count > A_BANKS)) % A_BANKS}")
 
         def b_bank(shape, count):
             return psum.tile(shape, F32, name=f"bank_b{count % B_BANKS}")
@@ -201,7 +229,7 @@ def tile_moe_tk_glu_sigmoid_kernel(
                 out=bank[:],
                 lhsT=slot_codes[s, e, st].bitcast(FP8X4),
                 lhsT_scale=slot_bytes[s, e][:, st * P : (st + 1) * P],
-                rhs=w_words[m, e][:, s, :].bitcast(FP4X4),
+                rhs=w_words[m, e, s].bitcast(FP4X4),
                 rhs_scale=w_scales[m, e][:, s, :],
                 start=opens,
                 stop=not opens,
@@ -214,20 +242,24 @@ def tile_moe_tk_glu_sigmoid_kernel(
             nc.vector.tensor_tensor(h[:], banks[1][:].rearrange("s (p u d) -> s u p d", u=2, d=2), sig[:], MULT)
             h_tiles[e, st] = h
 
-        def first_layer(e):
-            banks = [(a_bank([P, H], 2 * e + st), b_bank([P, H], 2 * e + st)) for st in range(2)]
-            opening = 0 if e == 0 else 1
-            opens_all = e < 2
-            if opens_all:
-                for m in range(2):
-                    for st in range(2):
-                        multiply_1(e, st, m, opening, banks[st][m], True)
+        banks = {}
+
+        def open_sums(e):
+            for st in range(2):
+                banks[e, st] = (a_bank([P, H], 2 * e + st), b_bank([P, H], 2 * e + st))
             for st in range(2):
                 for m in range(2):
-                    if not opens_all:
-                        multiply_1(e, st, m, opening, banks[st][m], True)
-                    multiply_1(e, st, m, 1 - opening, banks[st][m], False)
-                activate(e, st, banks[st])
+                    multiply_1(e, st, m, 1, banks[e, st][m], True)
+
+        def first_layer(e):
+            for st in range(2):
+                if e >= 2:
+                    banks[e, st] = (a_bank([P, H], 2 * e + st), b_bank([P, H], 2 * e + st))
+                for m in range(2):
+                    if e >= 2:
+                        multiply_1(e, st, m, 1, banks[e, st][m], True)
+                    multiply_1(e, st, m, 0, banks[e, st][m], False)
+                activate(e, st, banks[e, st])
 
         def turn(e, tiles, count, h_bf):
             n = len(tiles) * P
@@ -285,29 +317,46 @@ def tile_moe_tk_glu_sigmoid_kernel(
                 multiply_2(e + x, y_bank[:, x * C : (x + 1) * C], *hidden[e + x])
             engine_copy(y_t[:, e * C : (e + 2) * C], y_bank[:])
 
+        warm = psum.tile([P, H], F32, name="y_bank")
+        for x in range(WARM_UPS):
+            nc.tensor.matmul_mx(
+                out=warm[:],
+                lhsT=slot_codes[0, 0, 0].bitcast(FP8X4),
+                lhsT_scale=w_scales[0, 0][:, 1, :P],
+                rhs=w_words[0, 0, 1].bitcast(FP4X4),
+                rhs_scale=w_scales[0, 0][:, 1, :],
+                start=True,
+                stop=True,
+            )
+        open_sums(0)
+        load_weights(2, 3, "expert_2", AT_EXPERT_2)
+        gather_bytes(2)
+        gather_expert(2)
+        gather_expert(3)
+        open_sums(1)
+        load_weights(3, 4, "expert_3", AT_EXPERT_3)
+        for m in range(2):
+            room = placed([P, (E - EARLY) * PASSES * H], U8, f"late_scales{m}", AT_LATE_SCALES[m])
+            load_scales(m, EARLY, E, room[:])
         for e in range(E):
             first_layer(e)
             if e == LAST:
-                second_layer_pair(e - 3, nc.vector.tensor_copy)
+                second_layer_pair(e - 3, nc.scalar.copy)
                 hidden[e - 1] = turn_and_quantize(e - 1, (0, 1), 2 * e)
             elif e % 2 == 0:
                 if e >= 4:
                     second_layer_pair(e - 4, nc.scalar.copy)
                 if e >= 2:
                     turn_and_quantize_pair(e - 2)
-            elif e + 3 < E:
-                shift_bytes(e + 3, e + 5, gather_bytes(e + 3, e + 5, "slot_bytes"))
-            if e + 2 < E:
-                gather_codes(1, e + 2)
-                gather_codes(0, e + 2)
-            if e == 0:
-                load_weights(2, 4, "experts_2_3", AT_EXPERTS_2_3)
-                for m in range(2):
-                    room = placed([P, (E - EARLY) * PASSES * H], U8, f"late_scales{m}", AT_LATE_SCALES[m])
-                    load_scales(m, EARLY, E, room[:])
-                load_w2()
+            if e == 1:
+                gather_bytes(4)
+            if e == 3:
+                gather_bytes(6)
+            if e in GATHER_AFTER:
+                gather_expert(GATHER_AFTER[e])
             if e == 1:
                 load_weights(4, 6, "experts_4_5", AT_EXPERTS_4_5)
+                load_w2()
             if e == 3:
                 load_weights(6, 8, "experts_6_7", AT_EXPERTS_6_7)
             if e == 5:
@@ -324,16 +373,31 @@ def tile_moe_tk_glu_sigmoid_kernel(
         multiply_2(LAST, y_last[:], *last_hidden)
         nc.scalar.copy(y_t[:, LAST * C + P :], y_last[:])
 
-        parts = keep.tile([P, TOP, T], F32, name="parts", align_bytes=64)
-        two = keep.tile([P, T], F32, name="two", align_bytes=64)
-        three = keep.tile([P, T], F32, name="three", align_bytes=64)
+        parts = [keep.tile([P, T], F32, name=f"part{r}", align_bytes=64) for r in range(TOP)]
         halves = (slice(0, T // 2), slice(T // 2, T))
-        for r in range(TOP):
-            if r == TOP - 1:
-                nc.vector.tensor_tensor(two[:], parts[:, 0], parts[:, 1], ADD)
-            nc.vector.tensor_tensor(parts[:, r], y_t[:].indirect(pos_t[r][:]), gates[:, r], MULT)
+
+        def gather_part(r, cols):
+            picks = pos_t[r][:, cols.start // 16 : cols.stop // 16]
+            nc.vector.tensor_tensor(parts[r][:, cols], y_t[:].indirect(picks), gates[:, r, cols], MULT)
+
+        backs = []
+        for half, cols in enumerate(halves):
+            sums = [b_bank([P, P], 2 * half + x) for x in range(2)]
+            for r in range(TOP - 1):
+                gather_part(r, cols)
+                for x in range(2):
+                    first = cols.start + x * P
+                    nc.tensor.matmul(
+                        sums[x][:], parts[r][:, first : first + P], ident[:], start=r == 0, stop=r == TOP - 2, is_transpose=True
+                    )
+            back = a_bank([P, T // 2], half)
+            for x in range(2):
+                by_token = work.tile([P, P], F32, name="by_token", align_bytes=64)
+                nc.scalar.copy(by_token[:], sums[x][:])
+                nc.tensor.transpose(back[:, x * P : (x + 1) * P], by_token[:], ident[:])
+            backs.append(back)
         for cols in halves:
-            nc.vector.tensor_tensor(three[:, cols], two[:, cols], parts[:, 2, cols], ADD)
-        for cols in halves:
-            nc.vector.tensor_tensor(out_t[:, cols], three[:, cols], parts[:, 3, cols], ADD)
+            gather_part(TOP - 1, cols)
+        for back, cols in zip(backs, halves):
+            nc.vector.tensor_tensor(out_t[:, cols], back[:], parts[TOP - 1][:, cols], ADD)
             nc.sync.dma_start(out[:, cols], out_t[:, cols])

@@ -11,6 +11,7 @@ U16 = mybir.dt.uint16
 U8 = mybir.dt.uint8
 FP8X4 = mybir.dt.float8_e4m3fn_x4
 FP4X4 = mybir.dt.float4_e2m1fn_x4
+COPY = mybir.ActivationFunctionType.Copy
 SIGMOID = mybir.ActivationFunctionType.Sigmoid
 MULT = mybir.AluOpType.mult
 ADD = mybir.AluOpType.add
@@ -30,24 +31,25 @@ A_BANKS = 3
 B_BANKS = 4
 CODES_PLACE = {2: 2, 3: 0, 4: 1, 5: 2, 6: 1, 7: 2}
 GATHER_AFTER = {1: 4, 2: 5, 4: 6, 5: 7}
-WARM_UPS = 4
+WARM_UPS = 2
 
 KB = 1024
 AT_X_RAW = (0, 4 * KB, 35 * KB, 12 * KB)
 AT_X_BF = (8 * KB, 16 * KB)
 AT_SHIFTED = 36 * KB
 AT_FIRST_WORDS = {
-    (0, 1): 62 * KB,
-    (1, 1): 4 * KB,
-    (0, 0): 34 * KB,
-    (1, 0): 38 * KB,
+    (0, 0): 62 * KB,
+    (1, 0): 4 * KB,
+    (0, 1): 34 * KB,
+    (1, 1): 38 * KB,
 }
+AT_EARLY_BYTES = 44 * KB
+AT_EARLY_SHIFTED = 6 * KB
 AT_W3_FIRST_SCALES = 0
-AT_FIRST_TILE = 56 * KB
 AT_EXPERT_2 = 56 * KB + 256
 AT_EXPERT_3 = 62 * KB
 AT_LATE_SCALES = (12 * KB, 4 * KB)
-AT_FIRST_CODES = {(0, 0): 47 * KB, (0, 1): 48 * KB, (1, 0): 42 * KB, (1, 1): 16 * KB}
+AT_FIRST_CODES = {(0, 0): 56 * KB, (0, 1): 48 * KB, (1, 0): 42 * KB, (1, 1): 16 * KB}
 AT_CODES = (17 * KB, 48 * KB + 512, 19 * KB)
 AT_BYTES = (45 * KB, 46 * KB, 48 * KB, 46 * KB)
 AT_EXPERTS_4_5 = 28 * KB
@@ -116,12 +118,8 @@ def tile_moe_tk_glu_sigmoid_kernel(
                 for s in range(PASSES):
                     w_words[m, e, s] = words[:, (e - e0) * PASSES + s, :]
 
-        def load_first_words(m, s):
-            words = placed([P, 2, 2 * H], U8, f"first_words{m}{s}", AT_FIRST_WORDS[m, s])[:]
-            src = (w1_words, w3_words)[m].bitcast(I32)[0:2, s].rearrange("e p c -> p e c")
-            nc.sync.dma_start(words.bitcast(I32), src)
-            for e in range(2):
-                w_words[m, e, s] = words[:, e, :]
+        def load_first_words(m, e):
+            load_words(m, e, e + 1, placed([P, PASSES * 2 * H], U8, f"first_words{m}{e}", AT_FIRST_WORDS[m, e])[:])
 
         def load_weights(e0, e1, name, offset):
             size = (e1 - e0) * PASSES * 2 * H
@@ -131,7 +129,7 @@ def tile_moe_tk_glu_sigmoid_kernel(
 
         first_scales = keep.tile([P, EARLY * PASSES * H], U8, name="first_scales", align_bytes=64)
         nc.vector.memset(first_scales[:].bitcast(I32), 0)
-        load_first_words(0, 1)
+        load_first_words(0, 0)
         load_scales(0, 0, EARLY, first_scales[:])
 
         nc.vector.memset(x_bytes[:].bitcast(I32), 0)
@@ -161,26 +159,25 @@ def tile_moe_tk_glu_sigmoid_kernel(
         def entries(first, count):
             return offs_t[:, first // 16 : (first + count) // 16]
 
-        def gather_first_tile(st, offset):
-            codes = placed([P, P], U32, f"first_tile{st}", offset)
-            nc.vector.tensor_copy(codes[:], x_codes[1][:].indirect(entries(st * P, P)))
-            slot_codes[1, 0, st] = codes[:]
+        def shift(target, source):
+            for row, rows in SHIFT_ROWS:
+                nc.sync.dma_start(target[row : row + rows].bitcast(I32), source[row + 4 : row + 4 + rows].bitcast(I32))
+
+        def gather_early_bytes():
+            early = placed([P, C], U8, "early_bytes", AT_EARLY_BYTES)
+            nc.vector.tensor_copy(early[:], x_bytes[:].indirect(entries(0, C)))
+            moved = placed([P, C], U8, "early_shifted", AT_EARLY_SHIFTED)
+            shift(moved[:], early[:])
+            slot_bytes[0, 0] = moved[:]
 
         def gather_bytes(e0):
             both = placed([P, 2 * C], U8, f"slot_bytes{e0}", AT_BYTES[e0 // 2])
-            if e0 == 0:
-                nc.vector.tensor_copy(both[:, :C], x_bytes[:].indirect(entries(0, C)))
-                gather_first_tile(0, AT_FIRST_TILE)
-                nc.vector.tensor_copy(both[:, C:], x_bytes[:].indirect(entries(C, C)))
-            else:
-                nc.vector.tensor_copy(both[:], x_bytes[:].indirect(entries(e0 * C, 2 * C)))
-            for row, rows in SHIFT_ROWS:
-                nc.sync.dma_start(
-                    shifted[row : row + rows, e0 * C : (e0 + 2) * C].bitcast(I32),
-                    both[row + 4 : row + 4 + rows].bitcast(I32),
-                )
+            nc.vector.tensor_copy(both[:], x_bytes[:].indirect(entries(e0 * C, 2 * C)))
+            skip = 1 if e0 == 0 else 0
+            shift(shifted[:, (e0 + skip) * C : (e0 + 2) * C], both[:, skip * C :])
             for x in range(2):
-                slot_bytes[0, e0 + x] = shifted[:, (e0 + x) * C : (e0 + x + 1) * C]
+                if x >= skip:
+                    slot_bytes[0, e0 + x] = shifted[:, (e0 + x) * C : (e0 + x + 1) * C]
                 slot_bytes[1, e0 + x] = both[:, x * C : (x + 1) * C]
 
         def gather_codes(s, e, codes):
@@ -201,17 +198,19 @@ def tile_moe_tk_glu_sigmoid_kernel(
 
         quantize_tokens(0)
         quantize_tokens(1)
-        load_first_words(1, 1)
+        gather_early_bytes()
+        load_first_words(1, 0)
         load_scales(1, 0, EARLY, placed([P, EARLY * PASSES * H], U8, "w3_first_scales", AT_W3_FIRST_SCALES)[:])
         gather_first_codes(0, 0)
         gather_first_codes(0, 1)
         quantize_tokens(2)
-        load_first_words(0, 0)
-        load_first_words(1, 0)
+        load_first_words(0, 1)
+        load_first_words(1, 1)
         quantize_tokens(3)
         shifted = placed([P, SLOTS], U8, "shifted", AT_SHIFTED)
         gather_bytes(0)
-        gather_first_tile(1, AT_FIRST_CODES[1, 0])
+        gather_first_codes(1, 0)
+        gather_bytes(2)
         gather_first_codes(1, 1)
 
         h_tiles = {}
@@ -247,9 +246,9 @@ def tile_moe_tk_glu_sigmoid_kernel(
         def open_sums(e):
             for st in range(2):
                 banks[e, st] = (a_bank([P, H], 2 * e + st), b_bank([P, H], 2 * e + st))
-            for st in range(2):
-                for m in range(2):
-                    multiply_1(e, st, m, 1, banks[e, st][m], True)
+            for m in range(2):
+                for st in range(2):
+                    multiply_1(e, st, m, e, banks[e, st][m], True)
 
         def first_layer(e):
             for st in range(2):
@@ -258,7 +257,7 @@ def tile_moe_tk_glu_sigmoid_kernel(
                 for m in range(2):
                     if e >= 2:
                         multiply_1(e, st, m, 1, banks[e, st][m], True)
-                    multiply_1(e, st, m, 0, banks[e, st][m], False)
+                    multiply_1(e, st, m, 1 if e == 0 else 0, banks[e, st][m], False)
                 activate(e, st, banks[e, st])
 
         def turn(e, tiles, count, h_bf):
@@ -330,7 +329,7 @@ def tile_moe_tk_glu_sigmoid_kernel(
             )
         open_sums(0)
         load_weights(2, 3, "expert_2", AT_EXPERT_2)
-        gather_bytes(2)
+        first_layer(0)
         gather_expert(2)
         gather_expert(3)
         open_sums(1)
@@ -338,10 +337,10 @@ def tile_moe_tk_glu_sigmoid_kernel(
         for m in range(2):
             room = placed([P, (E - EARLY) * PASSES * H], U8, f"late_scales{m}", AT_LATE_SCALES[m])
             load_scales(m, EARLY, E, room[:])
-        for e in range(E):
+        for e in range(1, E):
             first_layer(e)
             if e == LAST:
-                second_layer_pair(e - 3, nc.scalar.copy)
+                second_layer_pair(e - 3, nc.vector.tensor_copy)
                 hidden[e - 1] = turn_and_quantize(e - 1, (0, 1), 2 * e)
             elif e % 2 == 0:
                 if e >= 4:
@@ -360,8 +359,14 @@ def tile_moe_tk_glu_sigmoid_kernel(
             if e == 3:
                 load_weights(6, 8, "experts_6_7", AT_EXPERTS_6_7)
             if e == 5:
-                gates = placed([P, TOP, T], F32, "gates", AT_GATES)
-                nc.sync.dma_start(gates[:], gate.rearrange("r p t -> p r t"))
+                last_gate = placed([P, T], F32, "last_gate", AT_GATES)
+                nc.sync.dma_start(last_gate[:], gate[TOP - 1])
+                gates = placed([P, TOP - 1, T // 2], F32, "gates", AT_GATES + 2 * KB)
+                nc.sync.dma_start(gates[:], gate[: TOP - 1, :, T // 2 :].rearrange("r p t -> p r t"))
+                gate_cols = [placed([P, 2], F32, f"gate_cols{r}", AT_GATES + 6 * KB + 64 * r) for r in range(TOP - 1)]
+                with nc.allow_non_contiguous_dma(reason="one gate a partition"):
+                    for r in range(TOP - 1):
+                        nc.sync.dma_start(gate_cols[r][:], gate[r, 0, : T // 2].rearrange("(x p) -> p x", p=P))
 
         last_hidden = turn_and_quantize(LAST, (0,), 2 * LAST + 2)
         y_before = b_bank([P, C + P], 2 * LAST - 1)
@@ -376,12 +381,29 @@ def tile_moe_tk_glu_sigmoid_kernel(
         parts = [keep.tile([P, T], F32, name=f"part{r}", align_bytes=64) for r in range(TOP)]
         halves = (slice(0, T // 2), slice(T // 2, T))
 
-        def gather_part(r, cols):
-            picks = pos_t[r][:, cols.start // 16 : cols.stop // 16]
-            nc.vector.tensor_tensor(parts[r][:, cols], y_t[:].indirect(picks), gates[:, r, cols], MULT)
+        def picked(r, cols):
+            return y_t[:].indirect(pos_t[r][:, cols.start // 16 : cols.stop // 16])
 
-        backs = []
-        for half, cols in enumerate(halves):
+        def gather_part(r, cols):
+            weights = last_gate[:, cols] if r == TOP - 1 else gates[:, r, :]
+            nc.vector.tensor_tensor(parts[r][:, cols], picked(r, cols), weights, MULT)
+
+        backs = [a_bank([P, T // 2], 0)]
+        weighted = {}
+        for r in range(TOP - 1):
+            nc.vector.tensor_copy(parts[r][:, halves[0]], picked(r, halves[0]))
+            turned = a_bank([P, 2, P], 1 + r)
+            for x in range(2):
+                nc.tensor.transpose(turned[:, x, :], parts[r][:, x * P : (x + 1) * P], ident[:])
+            for x in range(2):
+                weighted[r, x] = keep.tile([P, P], F32, name=f"weighted{r}{x}", align_bytes=64)
+                nc.scalar.activation(weighted[r, x][:], turned[:, x, :], COPY, scale=gate_cols[r][:, x : x + 1])
+        for x in range(2):
+            for r in range(TOP - 1):
+                nc.tensor.matmul(
+                    backs[0][:, x * P : (x + 1) * P], weighted[r, x][:], ident[:], start=r == 0, stop=r == TOP - 2, is_transpose=True
+                )
+        for half, cols in list(enumerate(halves))[1:]:
             sums = [b_bank([P, P], 2 * half + x) for x in range(2)]
             for r in range(TOP - 1):
                 gather_part(r, cols)

@@ -34,21 +34,21 @@ GATHER_AFTER = {1: 4, 2: 5, 4: 6, 5: 7}
 WARM_UPS = 2
 
 KB = 1024
-AT_X_RAW = (0, 4 * KB, 35 * KB, 12 * KB)
-AT_X_BF = (8 * KB, 16 * KB)
+AT_X_RAW = (12 * KB, 8 * KB, 4 * KB, 35 * KB)
+AT_X_BF = (0, 16 * KB)
 AT_SHIFTED = 36 * KB
 AT_FIRST_WORDS = {
     (0, 0): 62 * KB,
-    (1, 0): 4 * KB,
+    (1, 0): 4 * KB + 64,
     (0, 1): 34 * KB,
     (1, 1): 38 * KB,
 }
 AT_EARLY_BYTES = 44 * KB
-AT_EARLY_SHIFTED = 6 * KB
-AT_W3_FIRST_SCALES = 0
+AT_EARLY_SHIFTED = 11 * KB
+AT_W3_FIRST_SCALES = KB + 64
 AT_EXPERT_2 = 56 * KB + 256
 AT_EXPERT_3 = 62 * KB
-AT_LATE_SCALES = (12 * KB, 4 * KB)
+AT_LATE_SCALES = (12 * KB, 4 * KB + 64)
 AT_FIRST_CODES = {(0, 0): 56 * KB, (0, 1): 48 * KB, (1, 0): 42 * KB, (1, 1): 16 * KB}
 AT_CODES = (17 * KB, 48 * KB + 512, 19 * KB)
 AT_BYTES = (45 * KB, 46 * KB, 48 * KB, 46 * KB)
@@ -199,14 +199,14 @@ def tile_moe_tk_glu_sigmoid_kernel(
         quantize_tokens(0)
         quantize_tokens(1)
         gather_early_bytes()
-        load_first_words(1, 0)
-        load_scales(1, 0, EARLY, placed([P, EARLY * PASSES * H], U8, "w3_first_scales", AT_W3_FIRST_SCALES)[:])
         gather_first_codes(0, 0)
         gather_first_codes(0, 1)
         quantize_tokens(2)
+        load_first_words(1, 0)
+        load_scales(1, 0, EARLY, placed([P, EARLY * PASSES * H], U8, "w3_first_scales", AT_W3_FIRST_SCALES)[:])
+        quantize_tokens(3)
         load_first_words(0, 1)
         load_first_words(1, 1)
-        quantize_tokens(3)
         shifted = placed([P, SLOTS], U8, "shifted", AT_SHIFTED)
         gather_bytes(0)
         gather_first_codes(1, 0)
@@ -234,14 +234,29 @@ def tile_moe_tk_glu_sigmoid_kernel(
                 stop=not opens,
             )
 
-        def activate(e, st, banks):
+        def sigmoid(bank):
             sig = work.tile([P, 2, P, 2], F32, name="sig", align_bytes=64)
-            nc.scalar.activation(sig[:], banks[0][:].rearrange("s (p u d) -> s u p d", u=2, d=2), SIGMOID)
+            nc.scalar.activation(sig[:], bank[:].rearrange("s (p u d) -> s u p d", u=2, d=2), SIGMOID)
+            return sig
+
+        def product(e, st, bank, sig):
             h = work.tile([P, 2, P, 2], BF16, name="h", align_bytes=64, bufs=6)
-            nc.vector.tensor_tensor(h[:], banks[1][:].rearrange("s (p u d) -> s u p d", u=2, d=2), sig[:], MULT)
+            nc.vector.tensor_tensor(h[:], bank[:].rearrange("s (p u d) -> s u p d", u=2, d=2), sig[:], MULT)
             h_tiles[e, st] = h
 
         banks = {}
+
+        def first_expert():
+            for st in range(2):
+                banks[0, st] = (a_bank([P, H], st), b_bank([P, H], st))
+            for s in range(PASSES):
+                for st in range(2):
+                    multiply_1(0, st, 0, s, banks[0, st][0], s == 0)
+            sigs = [sigmoid(banks[0, st][0]) for st in range(2)]
+            for st in range(2):
+                for s in range(PASSES):
+                    multiply_1(0, st, 1, s, banks[0, st][1], s == 0)
+                product(0, st, banks[0, st][1], sigs[st])
 
         def open_sums(e):
             for st in range(2):
@@ -257,8 +272,8 @@ def tile_moe_tk_glu_sigmoid_kernel(
                 for m in range(2):
                     if e >= 2:
                         multiply_1(e, st, m, 1, banks[e, st][m], True)
-                    multiply_1(e, st, m, 1 if e == 0 else 0, banks[e, st][m], False)
-                activate(e, st, banks[e, st])
+                    multiply_1(e, st, m, 0, banks[e, st][m], False)
+                product(e, st, banks[e, st][1], sigmoid(banks[e, st][0]))
 
         def turn(e, tiles, count, h_bf):
             n = len(tiles) * P
@@ -327,9 +342,8 @@ def tile_moe_tk_glu_sigmoid_kernel(
                 start=True,
                 stop=True,
             )
-        open_sums(0)
+        first_expert()
         load_weights(2, 3, "expert_2", AT_EXPERT_2)
-        first_layer(0)
         gather_expert(2)
         gather_expert(3)
         open_sums(1)
@@ -359,14 +373,8 @@ def tile_moe_tk_glu_sigmoid_kernel(
             if e == 3:
                 load_weights(6, 8, "experts_6_7", AT_EXPERTS_6_7)
             if e == 5:
-                last_gate = placed([P, T], F32, "last_gate", AT_GATES)
-                nc.sync.dma_start(last_gate[:], gate[TOP - 1])
-                gates = placed([P, TOP - 1, T // 2], F32, "gates", AT_GATES + 2 * KB)
-                nc.sync.dma_start(gates[:], gate[: TOP - 1, :, T // 2 :].rearrange("r p t -> p r t"))
-                gate_cols = [placed([P, 2], F32, f"gate_cols{r}", AT_GATES + 6 * KB + 64 * r) for r in range(TOP - 1)]
-                with nc.allow_non_contiguous_dma(reason="one gate a partition"):
-                    for r in range(TOP - 1):
-                        nc.sync.dma_start(gate_cols[r][:], gate[r, 0, : T // 2].rearrange("(x p) -> p x", p=P))
+                gates = placed([P, TOP, T], F32, "gates", AT_GATES)
+                nc.sync.dma_start(gates[:], gate.rearrange("r p t -> p r t"))
 
         last_hidden = turn_and_quantize(LAST, (0,), 2 * LAST + 2)
         y_before = b_bank([P, C + P], 2 * LAST - 1)
@@ -378,48 +386,59 @@ def tile_moe_tk_glu_sigmoid_kernel(
         multiply_2(LAST, y_last[:], *last_hidden)
         nc.scalar.copy(y_t[:, LAST * C + P :], y_last[:])
 
-        parts = [keep.tile([P, T], F32, name=f"part{r}", align_bytes=64) for r in range(TOP)]
         halves = (slice(0, T // 2), slice(T // 2, T))
 
         def picked(r, cols):
             return y_t[:].indirect(pos_t[r][:, cols.start // 16 : cols.stop // 16])
 
-        def gather_part(r, cols):
-            weights = last_gate[:, cols] if r == TOP - 1 else gates[:, r, :]
-            nc.vector.tensor_tensor(parts[r][:, cols], picked(r, cols), weights, MULT)
+        def part(name):
+            return keep.tile([P, T // 2], F32, name=name, align_bytes=64)
 
-        backs = [a_bank([P, T // 2], 0)]
-        weighted = {}
-        for r in range(TOP - 1):
-            nc.vector.tensor_copy(parts[r][:, halves[0]], picked(r, halves[0]))
-            turned = a_bank([P, 2, P], 1 + r)
-            for x in range(2):
-                nc.tensor.transpose(turned[:, x, :], parts[r][:, x * P : (x + 1) * P], ident[:])
-            for x in range(2):
-                weighted[r, x] = keep.tile([P, P], F32, name=f"weighted{r}{x}", align_bytes=64)
-                nc.scalar.activation(weighted[r, x][:], turned[:, x, :], COPY, scale=gate_cols[r][:, x : x + 1])
-        for x in range(2):
-            for r in range(TOP - 1):
-                nc.tensor.matmul(
-                    backs[0][:, x * P : (x + 1) * P], weighted[r, x][:], ident[:], start=r == 0, stop=r == TOP - 2, is_transpose=True
-                )
-        for half, cols in list(enumerate(halves))[1:]:
-            sums = [b_bank([P, P], 2 * half + x) for x in range(2)]
-            for r in range(TOP - 1):
-                gather_part(r, cols)
+        sums = [b_bank([P, 2, P], half) for half in range(2)]
+        products = {}
+
+        def add_up(half, r):
+            if r < TOP - 1:
                 for x in range(2):
-                    first = cols.start + x * P
                     nc.tensor.matmul(
-                        sums[x][:], parts[r][:, first : first + P], ident[:], start=r == 0, stop=r == TOP - 2, is_transpose=True
+                        sums[half][:, x, :],
+                        products[half, r][:, x * P : (x + 1) * P],
+                        ident[:],
+                        start=r == 0 and x == 0,
+                        stop=r == TOP - 2 and x == 1,
+                        is_transpose=True,
                     )
+
+        def fused(half, r, name):
+            products[half, r] = part(name)
+            nc.vector.tensor_tensor(products[half, r][:], picked(r, halves[half]), gates[:, r, halves[half]], MULT)
+            add_up(half, r)
+
+        def weigh(r):
+            products[1, r] = part(f"weighted{r}")
+            nc.vector.tensor_tensor(products[1, r][:], plain[r][:], gates[:, r, halves[1]], MULT)
+            add_up(1, r)
+
+        def turn_back(half):
+            by_token = work.tile([P, 2, P], F32, name="by_token", align_bytes=64)
+            nc.scalar.copy(by_token[:], sums[half][:])
             back = a_bank([P, T // 2], half)
             for x in range(2):
-                by_token = work.tile([P, P], F32, name="by_token", align_bytes=64)
-                nc.scalar.copy(by_token[:], sums[x][:])
-                nc.tensor.transpose(back[:, x * P : (x + 1) * P], by_token[:], ident[:])
-            backs.append(back)
-        for cols in halves:
-            gather_part(TOP - 1, cols)
-        for back, cols in zip(backs, halves):
-            nc.vector.tensor_tensor(out_t[:, cols], back[:], parts[TOP - 1][:, cols], ADD)
+                nc.tensor.transpose(back[:, x * P : (x + 1) * P], by_token[:, x, :], ident[:])
+            return back
+
+        plain = [part(f"plain{r}") for r in range(TOP - 1)]
+        for r in range(TOP - 1):
+            nc.scalar.activation(plain[r][:], picked(r, halves[1]), COPY)
+        fused(0, 0, "fused0")
+        fused(0, 1, "fused1")
+        weigh(0)
+        weigh(1)
+        fused(0, 2, "plain0")
+        weigh(2)
+        backs = [turn_back(half) for half in range(2)]
+        fused(0, 3, "plain1")
+        fused(1, 3, "plain2")
+        for half, cols in enumerate(halves):
+            nc.vector.tensor_tensor(out_t[:, cols], backs[half][:], products[half, TOP - 1][:], ADD)
             nc.sync.dma_start(out[:, cols], out_t[:, cols])

@@ -31,7 +31,6 @@ A_BANKS = 3
 B_BANKS = 4
 CODES_PLACE = {2: 2, 3: 0, 4: 1, 5: 2, 6: 1, 7: 2}
 GATHER_AFTER = {1: 4, 2: 5, 4: 6, 5: 7}
-WARM_UPS = 2
 
 KB = 1024
 AT_X_RAW = (12 * KB, 8 * KB, 4 * KB, 35 * KB)
@@ -331,17 +330,6 @@ def tile_moe_tk_glu_sigmoid_kernel(
                 multiply_2(e + x, y_bank[:, x * C : (x + 1) * C], *hidden[e + x])
             engine_copy(y_t[:, e * C : (e + 2) * C], y_bank[:])
 
-        warm = psum.tile([P, H], F32, name="y_bank")
-        for x in range(WARM_UPS):
-            nc.tensor.matmul_mx(
-                out=warm[:],
-                lhsT=slot_codes[0, 0, 0].bitcast(FP8X4),
-                lhsT_scale=w_scales[0, 0][:, 1, :P],
-                rhs=w_words[0, 0, 1].bitcast(FP4X4),
-                rhs_scale=w_scales[0, 0][:, 1, :],
-                start=True,
-                stop=True,
-            )
         first_expert()
         load_weights(2, 3, "expert_2", AT_EXPERT_2)
         gather_expert(2)

@@ -24,7 +24,7 @@ LAST = E - 1
 FLOPS = 2 * SLOTS * (2 * K * H + H * N)
 
 X_PIECES = ((0, 0, T // 2), (0, T // 2, T), (1, 0, T // 2), (1, T // 2, T))
-VECTOR_CAST = (176, 176, 0, 192)
+VECTOR_CAST = (176, 176, 0, 96)
 EARLY = 3
 SHIFT_ROWS = ((0, 64), (64, 4), (96, 4))
 A_BANKS = 3
@@ -92,9 +92,6 @@ def tile_moe_tk_glu_sigmoid_kernel(
         nc.sync.dma_start(offs_t[:], offs)
         for r, src in enumerate((pos1, pos2, pos3, pos4)):
             nc.sync.dma_start(pos_t[r][:], src)
-        load_tokens(2)
-        load_tokens(3)
-
         w_scales = {}
         w_words = {}
 
@@ -128,10 +125,14 @@ def tile_moe_tk_glu_sigmoid_kernel(
 
         first_scales = keep.tile([P, EARLY * PASSES * H], U8, name="first_scales", align_bytes=64)
         nc.vector.memset(first_scales[:].bitcast(I32), 0)
+        load_tokens(2)
+        load_tokens(3)
         load_first_words(0, 0)
         load_scales(0, 0, EARLY, first_scales[:])
 
         nc.vector.memset(x_bytes[:].bitcast(I32), 0)
+        upper = keep.tile([P, C], U8, name="early_upper", align_bytes=64)
+        nc.vector.memset(upper[:].bitcast(I32), 0)
         make_identity(nc, ident[:])
 
         def cast(i, a, b, engine_copy):
@@ -166,7 +167,9 @@ def tile_moe_tk_glu_sigmoid_kernel(
             early = placed([P, C], U8, "early_bytes", AT_EARLY_BYTES)
             nc.vector.tensor_copy(early[:], x_bytes[:].indirect(entries(0, C)))
             moved = placed([P, C], U8, "early_shifted", AT_EARLY_SHIFTED)
-            shift(moved[:], early[:])
+            nc.vector.tensor_copy(upper[0:64].bitcast(I32), early[64:P].bitcast(I32))
+            nc.sync.dma_start(moved[0:64].bitcast(I32), early[4:68].bitcast(I32))
+            nc.sync.dma_start(moved[64:P].bitcast(I32), upper[4:68].bitcast(I32))
             slot_bytes[0, 0] = moved[:]
 
         def gather_bytes(e0):
@@ -342,7 +345,7 @@ def tile_moe_tk_glu_sigmoid_kernel(
         for e in range(1, E):
             first_layer(e)
             if e == LAST:
-                second_layer_pair(e - 3, nc.vector.tensor_copy)
+                second_layer_pair(e - 3, nc.scalar.copy)
                 hidden[e - 1] = turn_and_quantize(e - 1, (0, 1), 2 * e)
             elif e % 2 == 0:
                 if e >= 4:
@@ -382,51 +385,53 @@ def tile_moe_tk_glu_sigmoid_kernel(
         def part(name):
             return keep.tile([P, T // 2], F32, name=name, align_bytes=64)
 
-        sums = [b_bank([P, 2, P], half) for half in range(2)]
-        products = {}
-
-        def add_up(half, r):
-            if r < TOP - 1:
-                for x in range(2):
-                    nc.tensor.matmul(
-                        sums[half][:, x, :],
-                        products[half, r][:, x * P : (x + 1) * P],
-                        ident[:],
-                        start=r == 0 and x == 0,
-                        stop=r == TOP - 2 and x == 1,
-                        is_transpose=True,
-                    )
-
-        def fused(half, r, name):
-            products[half, r] = part(name)
-            nc.vector.tensor_tensor(products[half, r][:], picked(r, halves[half]), gates[:, r, halves[half]], MULT)
-            add_up(half, r)
-
-        def weigh(r):
-            products[1, r] = part(f"weighted{r}")
-            nc.vector.tensor_tensor(products[1, r][:], plain[r][:], gates[:, r, halves[1]], MULT)
-            add_up(1, r)
-
-        def turn_back(half):
-            by_token = work.tile([P, 2, P], F32, name="by_token", align_bytes=64)
-            nc.scalar.copy(by_token[:], sums[half][:])
-            back = a_bank([P, T // 2], half)
+        def fused(r):
+            values = part(f"fused{r}")
+            nc.vector.tensor_tensor(values[:], picked(r, halves[0]), gates[:, r, halves[0]], MULT)
             for x in range(2):
-                nc.tensor.transpose(back[:, x * P : (x + 1) * P], by_token[:, x, :], ident[:])
-            return back
+                nc.tensor.matmul(
+                    summed[:, x, :],
+                    values[:, x * P : (x + 1) * P],
+                    ident[:],
+                    start=r == 0 and x == 0,
+                    stop=r == TOP - 2 and x == 1,
+                    is_transpose=True,
+                )
 
-        plain = [part(f"plain{r}") for r in range(TOP - 1)]
+        def fetch(half, r):
+            plain[half, r] = part(f"plain{r}")
+            nc.scalar.activation(plain[half, r][:], picked(r, halves[half]), COPY)
+
+        def weigh(half, r):
+            weighed[half, r] = part(f"weighed{half}{r}")
+            nc.vector.tensor_tensor(weighed[half, r][:], plain[half, r][:], gates[:, r, halves[half]], MULT)
+
+        def add(target, first, second):
+            nc.vector.tensor_tensor(target, first, second, ADD)
+
+        summed = b_bank([P, 2, P], 0)
+        plain = {}
+        weighed = {}
+        for r in range(TOP):
+            fetch(1, r)
         for r in range(TOP - 1):
-            nc.scalar.activation(plain[r][:], picked(r, halves[1]), COPY)
-        fused(0, 0, "fused0")
-        fused(0, 1, "fused1")
-        weigh(0)
-        weigh(1)
-        fused(0, 2, "plain0")
-        weigh(2)
-        backs = [turn_back(half) for half in range(2)]
-        fused(0, 3, "plain1")
-        fused(1, 3, "plain2")
-        for half, cols in enumerate(halves):
-            nc.vector.tensor_tensor(out_t[:, cols], backs[half][:], products[half, TOP - 1][:], ADD)
-            nc.sync.dma_start(out[:, cols], out_t[:, cols])
+            fused(r)
+        by_token = work.tile([P, 2, P], F32, name="by_token", align_bytes=64)
+        nc.scalar.copy(by_token[:], summed[:])
+        back = a_bank([P, T // 2], 0)
+        for x in range(2):
+            nc.tensor.transpose(back[:, x * P : (x + 1) * P], by_token[:, x, :], ident[:])
+        weigh(1, 0)
+        weigh(1, 1)
+        fourth = part("plain0")
+        nc.vector.tensor_tensor(fourth[:], picked(TOP - 1, halves[0]), gates[:, TOP - 1, halves[0]], MULT)
+        weigh(1, 2)
+        two = part("two")
+        add(two[:], weighed[1, 0][:], weighed[1, 1][:])
+        weigh(1, TOP - 1)
+        three = part("three")
+        add(three[:], two[:], weighed[1, 2][:])
+        add(out_t[:, halves[0]], back[:], fourth[:])
+        nc.sync.dma_start(out[:, halves[0]], out_t[:, halves[0]])
+        add(out_t[:, halves[1]], three[:], weighed[1, TOP - 1][:])
+        nc.sync.dma_start(out[:, halves[1]], out_t[:, halves[1]])

@@ -27,10 +27,13 @@ X_PIECES = ((0, 0, T // 2), (0, T // 2, T), (1, 0, T // 2), (1, T // 2, T))
 VECTOR_CAST = (176, 176, 0, 96)
 EARLY = 3
 SHIFT_ROWS = ((0, 64), (64, 4), (96, 4))
+WARM_UPS = 2
+OPENED_FIRST = (1, 4, 6)
+BANK = 2048
 A_BANKS = 3
 B_BANKS = 4
-CODES_PLACE = {2: 2, 3: 0, 4: 1, 5: 2, 6: 1, 7: 2}
-GATHER_AFTER = {1: 4, 2: 5, 4: 6, 5: 7}
+CODES_PLACE = {2: 2, 3: 0, 4: 1, 5: 2, 6: 0, 7: 2}
+GATHER_AFTER = {1: 4, 2: 5, 3: 6, 5: 7}
 
 KB = 1024
 AT_X_RAW = (12 * KB, 8 * KB, 4 * KB, 35 * KB)
@@ -51,7 +54,8 @@ AT_LATE_SCALES = (12 * KB, 4 * KB + 64)
 AT_FIRST_CODES = {(0, 0): 56 * KB, (0, 1): 48 * KB, (1, 0): 42 * KB, (1, 1): 16 * KB}
 AT_CODES = (17 * KB, 48 * KB + 512, 19 * KB)
 AT_BYTES = (45 * KB, 46 * KB, 48 * KB, 46 * KB)
-AT_EXPERTS_4_5 = 28 * KB
+AT_H_CODES = {0: 48 * KB + 512, 2: 26 * KB, 4: 19 * KB}
+AT_EXPERTS_4_5 = 26 * KB
 AT_W2_SCALES = 38 * KB
 AT_W2 = 39 * KB
 AT_EXPERTS_6_7 = 62 * KB
@@ -117,11 +121,11 @@ def tile_moe_tk_glu_sigmoid_kernel(
         def load_first_words(m, e):
             load_words(m, e, e + 1, placed([P, PASSES * 2 * H], U8, f"first_words{m}{e}", AT_FIRST_WORDS[m, e])[:])
 
-        def load_weights(e0, e1, name, offset):
+        def load_weights(e0, e1, name, offset, before=0):
             size = (e1 - e0) * PASSES * 2 * H
-            room = placed([P, 2 * size], U8, name, offset)
+            room = placed([P, before + 2 * size], U8, name, offset)
             for m in range(2):
-                load_words(m, e0, e1, room[:, m * size : (m + 1) * size])
+                load_words(m, e0, e1, room[:, before + m * size : before + (m + 1) * size])
 
         first_scales = keep.tile([P, EARLY * PASSES * H], U8, name="first_scales", align_bytes=64)
         nc.vector.memset(first_scales[:].bitcast(I32), 0)
@@ -171,6 +175,7 @@ def tile_moe_tk_glu_sigmoid_kernel(
             nc.sync.dma_start(moved[0:64].bitcast(I32), early[4:68].bitcast(I32))
             nc.sync.dma_start(moved[64:P].bitcast(I32), upper[4:68].bitcast(I32))
             slot_bytes[0, 0] = moved[:]
+            slot_bytes["early"] = early[:]
 
         def gather_bytes(e0):
             both = placed([P, 2 * C], U8, f"slot_bytes{e0}", AT_BYTES[e0 // 2])
@@ -195,8 +200,8 @@ def tile_moe_tk_glu_sigmoid_kernel(
 
         def gather_expert(e):
             codes = expert_codes(e)
-            gather_codes(1, e, codes[:, C:])
-            gather_codes(0, e, codes[:, :C])
+            for s in (0, 1) if e % 2 else (1, 0):
+                gather_codes(s, e, codes[:, s * C : (s + 1) * C])
 
         quantize_tokens(0)
         quantize_tokens(1)
@@ -217,13 +222,19 @@ def tile_moe_tk_glu_sigmoid_kernel(
 
         h_tiles = {}
 
+        uses = []
+
+        def bank_tile(shape, number):
+            uses.append(number)
+            return psum.tile(shape, F32, name=f"bank{len(uses)}", offset=number * BANK)
+
         def a_bank(shape, count):
             if count == A_BANKS:
-                return psum.tile(shape, F32, name="y_bank")
-            return psum.tile(shape, F32, name=f"bank_a{(count - (count > A_BANKS)) % A_BANKS}")
+                return bank_tile(shape, A_BANKS + B_BANKS)
+            return bank_tile(shape, (count - (count > A_BANKS)) % A_BANKS)
 
         def b_bank(shape, count):
-            return psum.tile(shape, F32, name=f"bank_b{count % B_BANKS}")
+            return bank_tile(shape, A_BANKS + count % B_BANKS)
 
         def multiply_1(e, st, m, s, bank, opens):
             nc.tensor.matmul_mx(
@@ -249,6 +260,17 @@ def tile_moe_tk_glu_sigmoid_kernel(
         banks = {}
 
         def first_expert():
+            idle = b_bank([P, H], B_BANKS - 1)
+            for st in range(WARM_UPS):
+                nc.tensor.matmul_mx(
+                    out=idle[:],
+                    lhsT=slot_codes[0, 0, 0].bitcast(FP8X4),
+                    lhsT_scale=slot_bytes["early"][:, :P],
+                    rhs=w_words[0, 0, 0].bitcast(FP4X4),
+                    rhs_scale=w_scales[0, 0][:, 0, :],
+                    start=True,
+                    stop=True,
+                )
             for st in range(2):
                 banks[0, st] = (a_bank([P, H], st), b_bank([P, H], st))
             for s in range(PASSES):
@@ -265,17 +287,23 @@ def tile_moe_tk_glu_sigmoid_kernel(
                 banks[e, st] = (a_bank([P, H], 2 * e + st), b_bank([P, H], 2 * e + st))
             for m in range(2):
                 for st in range(2):
-                    multiply_1(e, st, m, e, banks[e, st][m], True)
+                    multiply_1(e, st, m, 1, banks[e, st][m], True)
 
         def first_layer(e):
+            opened = e in OPENED_FIRST
+            first = 1 if opened or e % 2 == 0 else 0
+            if opened and e > 1:
+                open_sums(e)
             for st in range(2):
-                if e >= 2:
+                if not opened and e >= 2:
                     banks[e, st] = (a_bank([P, H], 2 * e + st), b_bank([P, H], 2 * e + st))
                 for m in range(2):
-                    if e >= 2:
-                        multiply_1(e, st, m, 1, banks[e, st][m], True)
-                    multiply_1(e, st, m, 0, banks[e, st][m], False)
+                    if not opened and e >= 2:
+                        multiply_1(e, st, m, first, banks[e, st][m], True)
+                    multiply_1(e, st, m, 1 - first, banks[e, st][m], False)
                 product(e, st, banks[e, st][1], sigmoid(banks[e, st][0]))
+                if (e, st) == (LAST, 0):
+                    second_layer_pair(2, nc.scalar.copy)
 
         def turn(e, tiles, count, h_bf):
             n = len(tiles) * P
@@ -286,9 +314,12 @@ def tile_moe_tk_glu_sigmoid_kernel(
                     nc.tensor.transpose(turned[:, u, x * P : (x + 1) * P], words[:, u * P : (u + 1) * P], ident[:])
             nc.scalar.copy(h_bf.bitcast(F32).rearrange("p (r u) -> p r u", u=2), turned[:].rearrange("p u r -> p r u"))
 
-        def quantize_hidden(h_bf):
+        def quantize_hidden(h_bf, e=None):
             n = h_bf.shape[1] // 4
-            h_codes = work.tile([P, n], U32, name="h_codes", align_bytes=64)
+            if e is None:
+                h_codes = work.tile([P, n], U32, name="h_codes", align_bytes=64)
+            else:
+                h_codes = placed([P, n], U32, f"h_codes{e}", AT_H_CODES[e])
             h_bytes = work.tile([P, n], U8, name="h_bytes", align_bytes=64)
             nc.vector.quantize_mx(out=h_codes[:].bitcast(FP8X4), scales=h_bytes[:], in_=h_bf[:])
             return h_codes[:], h_bytes[:]
@@ -300,11 +331,16 @@ def tile_moe_tk_glu_sigmoid_kernel(
 
         hidden = {}
 
-        def turn_and_quantize_pair(e):
+        turned_pairs = {}
+
+        def turn_pair(e):
             h_bf = work.tile([P, 8 * C], BF16, name="h_bf", align_bytes=64)
             for x in range(2):
                 turn(e + x, (0, 1), 2 * (e + 2) + x, h_bf[:, 4 * C * x : 4 * C * (x + 1)])
-            h_codes, h_bytes = quantize_hidden(h_bf)
+            turned_pairs[e] = h_bf
+
+        def quantize_pair(e):
+            h_codes, h_bytes = quantize_hidden(turned_pairs[e], e)
             for x in range(2):
                 hidden[e + x] = (h_codes[:, x * C : (x + 1) * C], h_bytes[:, x * C : (x + 1) * C])
 
@@ -328,7 +364,7 @@ def tile_moe_tk_glu_sigmoid_kernel(
             )
 
         def second_layer_pair(e, engine_copy):
-            y_bank = psum.tile([P, 2 * C], F32, name="y_bank")
+            y_bank = a_bank([P, 2 * C], 2 * LAST if e == 2 else A_BANKS)
             for x in range(2):
                 multiply_2(e + x, y_bank[:, x * C : (x + 1) * C], *hidden[e + x])
             engine_copy(y_t[:, e * C : (e + 2) * C], y_bank[:])
@@ -345,24 +381,26 @@ def tile_moe_tk_glu_sigmoid_kernel(
         for e in range(1, E):
             first_layer(e)
             if e == LAST:
-                second_layer_pair(e - 3, nc.scalar.copy)
+                quantize_pair(e - 3)
                 hidden[e - 1] = turn_and_quantize(e - 1, (0, 1), 2 * e)
             elif e % 2 == 0:
-                if e >= 4:
-                    second_layer_pair(e - 4, nc.scalar.copy)
-                if e >= 2:
-                    turn_and_quantize_pair(e - 2)
+                if e == 4:
+                    quantize_pair(0)
+                if e == 6:
+                    second_layer_pair(0, nc.scalar.copy)
+                turn_pair(e - 2)
             if e == 1:
                 gather_bytes(4)
             if e == 3:
+                load_weights(6, 8, "experts_6_7", AT_EXPERTS_6_7)
                 gather_bytes(6)
             if e in GATHER_AFTER:
                 gather_expert(GATHER_AFTER[e])
+            if e == 5:
+                quantize_pair(2)
             if e == 1:
-                load_weights(4, 6, "experts_4_5", AT_EXPERTS_4_5)
+                load_weights(4, 6, "experts_4_5", AT_EXPERTS_4_5, before=2 * KB)
                 load_w2()
-            if e == 3:
-                load_weights(6, 8, "experts_6_7", AT_EXPERTS_6_7)
             if e == 5:
                 gates = placed([P, TOP, T], F32, "gates", AT_GATES)
                 nc.sync.dma_start(gates[:], gate.rearrange("r p t -> p r t"))
@@ -373,6 +411,7 @@ def tile_moe_tk_glu_sigmoid_kernel(
         multiply_2(LAST, y_before[:, C:], *last_hidden)
         nc.vector.tensor_copy(y_t[:, (LAST - 1) * C : LAST * C + P], y_before[:])
         last_hidden = turn_and_quantize(LAST, (1,), 2 * LAST + 1)
+        second_layer_pair(LAST - 3, nc.scalar.copy)
         y_last = b_bank([P, P], 2 * LAST - 2)
         multiply_2(LAST, y_last[:], *last_hidden)
         nc.scalar.copy(y_t[:, LAST * C + P :], y_last[:])

@@ -25,7 +25,7 @@ FLOPS = 2 * SLOTS * (2 * K * H + H * N)
 
 X_PIECES = ((0, 0, T // 2), (0, T // 2, T), (1, 0, T // 2), (1, T // 2, T))
 VECTOR_CAST = (176, 176, 0, 96)
-EARLY = 3
+EARLY = 4
 SHIFT_ROWS = ((0, 64), (64, 4), (96, 4))
 WARM_UPS = 2
 OPENED_FIRST = (1, 4, 6)
@@ -47,7 +47,7 @@ AT_FIRST_WORDS = {
 }
 AT_EARLY_BYTES = 44 * KB
 AT_EARLY_SHIFTED = 11 * KB
-AT_W3_FIRST_SCALES = KB + 64
+AT_W3_FIRST_SCALES = 64
 AT_EXPERT_2 = 56 * KB + 256
 AT_EXPERT_3 = 62 * KB
 AT_LATE_SCALES = (12 * KB, 4 * KB + 64)

@@ -54,12 +54,13 @@ AT_LATE_SCALES = (12 * KB, 4 * KB + 64)
 AT_FIRST_CODES = {(0, 0): 56 * KB, (0, 1): 48 * KB, (1, 0): 42 * KB, (1, 1): 16 * KB}
 AT_CODES = (17 * KB, 48 * KB + 512, 19 * KB)
 AT_BYTES = (45 * KB, 46 * KB, 48 * KB, 46 * KB)
-AT_H_CODES = {0: 48 * KB + 512, 2: 26 * KB, 4: 19 * KB}
-AT_EXPERTS_4_5 = 26 * KB
-AT_W2_SCALES = 38 * KB
-AT_W2 = 39 * KB
+AT_H_CODES = {0: 48 * KB + 512, 2: 58 * KB + 512, 4: 19 * KB}
+AT_EXPERT_5 = 56 * KB + 256
+AT_EXPERT_4 = 32 * KB
+AT_W2_SCALES = 32 * KB
+AT_W2 = 33 * KB
 AT_EXPERTS_6_7 = 62 * KB
-AT_GATES = 28 * KB
+AT_GATES = 50 * KB + 512
 
 
 def tile_moe_tk_glu_sigmoid_kernel(
@@ -121,11 +122,11 @@ def tile_moe_tk_glu_sigmoid_kernel(
         def load_first_words(m, e):
             load_words(m, e, e + 1, placed([P, PASSES * 2 * H], U8, f"first_words{m}{e}", AT_FIRST_WORDS[m, e])[:])
 
-        def load_weights(e0, e1, name, offset, before=0):
+        def load_weights(e0, e1, name, offset):
             size = (e1 - e0) * PASSES * 2 * H
-            room = placed([P, before + 2 * size], U8, name, offset)
+            room = placed([P, 2 * size], U8, name, offset)
             for m in range(2):
-                load_words(m, e0, e1, room[:, before + m * size : before + (m + 1) * size])
+                load_words(m, e0, e1, room[:, m * size : (m + 1) * size])
 
         first_scales = keep.tile([P, EARLY * PASSES * H], U8, name="first_scales", align_bytes=64)
         nc.vector.memset(first_scales[:].bitcast(I32), 0)
@@ -399,7 +400,10 @@ def tile_moe_tk_glu_sigmoid_kernel(
             if e == 5:
                 quantize_pair(2)
             if e == 1:
-                load_weights(4, 6, "experts_4_5", AT_EXPERTS_4_5, before=2 * KB)
+                load_weights(4, 5, "expert_4", AT_EXPERT_4)
+            if e == 2:
+                load_weights(5, 6, "expert_5", AT_EXPERT_5)
+            if e == 4:
                 load_w2()
             if e == 5:
                 gates = placed([P, TOP, T], F32, "gates", AT_GATES)

@@ -303,8 +303,6 @@ def tile_moe_tk_glu_sigmoid_kernel(
                         multiply_1(e, st, m, first, banks[e, st][m], True)
                     multiply_1(e, st, m, 1 - first, banks[e, st][m], False)
                 product(e, st, banks[e, st][1], sigmoid(banks[e, st][0]))
-                if (e, st) == (LAST, 0):
-                    second_layer_pair(2, nc.scalar.copy)
 
         def turn(e, tiles, count, h_bf):
             n = len(tiles) * P
@@ -365,7 +363,7 @@ def tile_moe_tk_glu_sigmoid_kernel(
             )
 
         def second_layer_pair(e, engine_copy):
-            y_bank = a_bank([P, 2 * C], 2 * LAST if e == 2 else A_BANKS)
+            y_bank = b_bank([P, 2 * C], 2 * LAST) if e == 2 else a_bank([P, 2 * C], A_BANKS)
             for x in range(2):
                 multiply_2(e + x, y_bank[:, x * C : (x + 1) * C], *hidden[e + x])
             engine_copy(y_t[:, e * C : (e + 2) * C], y_bank[:])
@@ -383,7 +381,6 @@ def tile_moe_tk_glu_sigmoid_kernel(
             first_layer(e)
             if e == LAST:
                 quantize_pair(e - 3)
-                hidden[e - 1] = turn_and_quantize(e - 1, (0, 1), 2 * e)
             elif e % 2 == 0:
                 if e == 4:
                     quantize_pair(0)
@@ -409,10 +406,14 @@ def tile_moe_tk_glu_sigmoid_kernel(
                 gates = placed([P, TOP, T], F32, "gates", AT_GATES)
                 nc.sync.dma_start(gates[:], gate.rearrange("r p t -> p r t"))
 
-        last_hidden = turn_and_quantize(LAST, (0,), 2 * LAST + 2)
+        three_bf = work.tile([P, 4 * (C + P)], BF16, name="h_bf", align_bytes=64)
+        turn(LAST - 1, (0, 1), 2 * LAST, three_bf[:, : 4 * C])
+        turn(LAST, (0,), 2 * LAST + 2, three_bf[:, 4 * C :])
+        h_codes, h_bytes = quantize_hidden(three_bf)
+        second_layer_pair(2, nc.scalar.copy)
         y_before = b_bank([P, C + P], 2 * LAST - 1)
-        multiply_2(LAST - 1, y_before[:, 0:C], *hidden[LAST - 1])
-        multiply_2(LAST, y_before[:, C:], *last_hidden)
+        multiply_2(LAST - 1, y_before[:, 0:C], h_codes[:, :C], h_bytes[:, :C])
+        multiply_2(LAST, y_before[:, C:], h_codes[:, C:], h_bytes[:, C:])
         nc.vector.tensor_copy(y_t[:, (LAST - 1) * C : LAST * C + P], y_before[:])
         last_hidden = turn_and_quantize(LAST, (1,), 2 * LAST + 1)
         second_layer_pair(LAST - 3, nc.scalar.copy)

@@ -27,7 +27,6 @@ X_PIECES = ((0, 0, T // 2), (0, T // 2, T), (1, 0, T // 2), (1, T // 2, T))
 VECTOR_CAST = (176, 176, 0, 96)
 EARLY = 4
 SHIFT_ROWS = ((0, 64), (64, 4), (96, 4))
-WARM_UPS = 2
 OPENED_FIRST = (1, 4, 6)
 BANK = 2048
 A_BANKS = 3
@@ -50,11 +49,11 @@ AT_EARLY_SHIFTED = 11 * KB
 AT_W3_FIRST_SCALES = 64
 AT_EXPERT_2 = 56 * KB + 256
 AT_EXPERT_3 = 62 * KB
-AT_LATE_SCALES = (12 * KB, 4 * KB + 64)
+AT_LATE_SCALES = (12 * KB + 256, 4 * KB + 64)
 AT_FIRST_CODES = {(0, 0): 56 * KB, (0, 1): 48 * KB, (1, 0): 42 * KB, (1, 1): 16 * KB}
 AT_CODES = (17 * KB, 48 * KB + 512, 19 * KB)
 AT_BYTES = (45 * KB, 46 * KB, 48 * KB, 46 * KB)
-AT_H_CODES = {0: 48 * KB + 512, 2: 58 * KB + 512, 4: 19 * KB}
+AT_H_CODES = {0: 48 * KB + 512, 2: 58 * KB + 512, 4: 72 * KB}
 AT_EXPERT_5 = 56 * KB + 256
 AT_EXPERT_4 = 32 * KB
 AT_W2_SCALES = 32 * KB
@@ -176,7 +175,6 @@ def tile_moe_tk_glu_sigmoid_kernel(
             nc.sync.dma_start(moved[0:64].bitcast(I32), early[4:68].bitcast(I32))
             nc.sync.dma_start(moved[64:P].bitcast(I32), upper[4:68].bitcast(I32))
             slot_bytes[0, 0] = moved[:]
-            slot_bytes["early"] = early[:]
 
         def gather_bytes(e0):
             both = placed([P, 2 * C], U8, f"slot_bytes{e0}", AT_BYTES[e0 // 2])
@@ -261,17 +259,6 @@ def tile_moe_tk_glu_sigmoid_kernel(
         banks = {}
 
         def first_expert():
-            idle = b_bank([P, H], B_BANKS - 1)
-            for st in range(WARM_UPS):
-                nc.tensor.matmul_mx(
-                    out=idle[:],
-                    lhsT=slot_codes[0, 0, 0].bitcast(FP8X4),
-                    lhsT_scale=slot_bytes["early"][:, :P],
-                    rhs=w_words[0, 0, 0].bitcast(FP4X4),
-                    rhs_scale=w_scales[0, 0][:, 0, :],
-                    start=True,
-                    stop=True,
-                )
             for st in range(2):
                 banks[0, st] = (a_bank([P, H], st), b_bank([P, H], st))
             for s in range(PASSES):
@@ -363,7 +350,7 @@ def tile_moe_tk_glu_sigmoid_kernel(
             )
 
         def second_layer_pair(e, engine_copy):
-            y_bank = b_bank([P, 2 * C], 2 * LAST) if e == 2 else a_bank([P, 2 * C], A_BANKS)
+            y_bank = b_bank([P, 2 * C], 2 * LAST) if e == 2 else a_bank([P, 2 * C], 2 * LAST if e else A_BANKS)
             for x in range(2):
                 multiply_2(e + x, y_bank[:, x * C : (x + 1) * C], *hidden[e + x])
             engine_copy(y_t[:, e * C : (e + 2) * C], y_bank[:])
@@ -379,14 +366,14 @@ def tile_moe_tk_glu_sigmoid_kernel(
             load_scales(m, EARLY, E, room[:])
         for e in range(1, E):
             first_layer(e)
-            if e == LAST:
-                quantize_pair(e - 3)
-            elif e % 2 == 0:
+            if e % 2 == 0:
                 if e == 4:
                     quantize_pair(0)
                 if e == 6:
                     second_layer_pair(0, nc.scalar.copy)
                 turn_pair(e - 2)
+                if e == 6:
+                    quantize_pair(4)
             if e == 1:
                 gather_bytes(4)
             if e == 3:

@@ -31,8 +31,7 @@ OPENED_FIRST = (1, 4, 6)
 BANK = 2048
 A_BANKS = 3
 B_BANKS = 4
-CODES_PLACE = {2: 2, 3: 0, 4: 1, 5: 2, 6: 0, 7: 2}
-GATHER_AFTER = {1: 4, 2: 5, 3: 6, 5: 7}
+GATHERED_BEHIND = {e: e - 3 if e < LAST else e - 2 for e in range(4, E)}
 
 KB = 1024
 AT_X_RAW = (12 * KB, 8 * KB, 4 * KB, 35 * KB)
@@ -47,19 +46,19 @@ AT_FIRST_WORDS = {
 AT_EARLY_BYTES = 44 * KB
 AT_EARLY_SHIFTED = 11 * KB
 AT_W3_FIRST_SCALES = 64
-AT_EXPERT_2 = 56 * KB + 256
-AT_EXPERT_3 = 62 * KB
 AT_LATE_SCALES = (12 * KB + 256, 4 * KB + 64)
 AT_FIRST_CODES = {(0, 0): 56 * KB, (0, 1): 48 * KB, (1, 0): 42 * KB, (1, 1): 16 * KB}
-AT_CODES = (17 * KB, 48 * KB + 512, 19 * KB)
+AT_CODES = {2: 19 * KB, 3: 17 * KB, 4: 48 * KB + 512, 5: 19 * KB, 6: 17 * KB, 7: 19 * KB}
 AT_BYTES = (45 * KB, 46 * KB, 48 * KB, 46 * KB)
-AT_H_CODES = {0: 48 * KB + 512, 2: 58 * KB + 512, 4: 72 * KB}
-AT_EXPERT_5 = 56 * KB + 256
+AT_EXPERT_2 = 62 * KB
+AT_EXPERT_3 = 56 * KB + 256
 AT_EXPERT_4 = 32 * KB
-AT_W2_SCALES = 32 * KB
-AT_W2 = 33 * KB
-AT_EXPERTS_6_7 = 62 * KB
-AT_GATES = 50 * KB + 512
+AT_EXPERT_5 = AT_EXPERT_2
+AT_EXPERTS_6_7 = AT_EXPERT_3 - 4 * KB
+AT_W2_SCALES = AT_EXPERT_4
+AT_W2 = AT_EXPERT_4 + KB
+AT_GATES = 65 * KB + 768
+AT_H_CODES = {0: AT_CODES[4], 2: 60 * KB + 256, 4: 80 * KB}
 
 
 def tile_moe_tk_glu_sigmoid_kernel(
@@ -194,11 +193,8 @@ def tile_moe_tk_glu_sigmoid_kernel(
         def gather_first_codes(s, e):
             gather_codes(s, e, placed([P, C], U32, f"first_codes{s}{e}", AT_FIRST_CODES[s, e])[:])
 
-        def expert_codes(e):
-            return placed([P, PASSES * C], U32, f"slot_codes{e}", AT_CODES[CODES_PLACE[e]])
-
         def gather_expert(e):
-            codes = expert_codes(e)
+            codes = placed([P, PASSES * C], U32, f"slot_codes{e}", AT_CODES[e])
             for s in (0, 1) if e % 2 else (1, 0):
                 gather_codes(s, e, codes[:, s * C : (s + 1) * C])
 
@@ -220,7 +216,6 @@ def tile_moe_tk_glu_sigmoid_kernel(
         gather_first_codes(1, 1)
 
         h_tiles = {}
-
         uses = []
 
         def bank_tile(shape, number):
@@ -316,7 +311,6 @@ def tile_moe_tk_glu_sigmoid_kernel(
             return quantize_hidden(h_bf)
 
         hidden = {}
-
         turned_pairs = {}
 
         def turn_pair(e):
@@ -349,11 +343,10 @@ def tile_moe_tk_glu_sigmoid_kernel(
                 stop=True,
             )
 
-        def second_layer_pair(e, engine_copy):
-            y_bank = b_bank([P, 2 * C], 2 * LAST) if e == 2 else a_bank([P, 2 * C], 2 * LAST if e else A_BANKS)
+        def second_layer_pair(e, y_bank):
             for x in range(2):
                 multiply_2(e + x, y_bank[:, x * C : (x + 1) * C], *hidden[e + x])
-            engine_copy(y_t[:, e * C : (e + 2) * C], y_bank[:])
+            nc.scalar.copy(y_t[:, e * C : (e + 2) * C], y_bank[:])
 
         first_expert()
         load_weights(2, 3, "expert_2", AT_EXPERT_2)
@@ -370,7 +363,7 @@ def tile_moe_tk_glu_sigmoid_kernel(
                 if e == 4:
                     quantize_pair(0)
                 if e == 6:
-                    second_layer_pair(0, nc.scalar.copy)
+                    second_layer_pair(0, a_bank([P, 2 * C], A_BANKS))
                 turn_pair(e - 2)
                 if e == 6:
                     quantize_pair(4)
@@ -379,8 +372,9 @@ def tile_moe_tk_glu_sigmoid_kernel(
             if e == 3:
                 load_weights(6, 8, "experts_6_7", AT_EXPERTS_6_7)
                 gather_bytes(6)
-            if e in GATHER_AFTER:
-                gather_expert(GATHER_AFTER[e])
+            for later, behind in GATHERED_BEHIND.items():
+                if behind == e:
+                    gather_expert(later)
             if e == 5:
                 quantize_pair(2)
             if e == 1:
@@ -397,13 +391,13 @@ def tile_moe_tk_glu_sigmoid_kernel(
         turn(LAST - 1, (0, 1), 2 * LAST, three_bf[:, : 4 * C])
         turn(LAST, (0,), 2 * LAST + 2, three_bf[:, 4 * C :])
         h_codes, h_bytes = quantize_hidden(three_bf)
-        second_layer_pair(2, nc.scalar.copy)
+        second_layer_pair(2, b_bank([P, 2 * C], 2 * LAST))
         y_before = b_bank([P, C + P], 2 * LAST - 1)
         multiply_2(LAST - 1, y_before[:, 0:C], h_codes[:, :C], h_bytes[:, :C])
         multiply_2(LAST, y_before[:, C:], h_codes[:, C:], h_bytes[:, C:])
         nc.vector.tensor_copy(y_t[:, (LAST - 1) * C : LAST * C + P], y_before[:])
         last_hidden = turn_and_quantize(LAST, (1,), 2 * LAST + 1)
-        second_layer_pair(LAST - 3, nc.scalar.copy)
+        second_layer_pair(4, a_bank([P, 2 * C], 2 * LAST))
         y_last = b_bank([P, P], 2 * LAST - 2)
         multiply_2(LAST, y_last[:], *last_hidden)
         nc.scalar.copy(y_t[:, LAST * C + P :], y_last[:])
@@ -429,13 +423,13 @@ def tile_moe_tk_glu_sigmoid_kernel(
                     is_transpose=True,
                 )
 
-        def fetch(half, r):
-            plain[half, r] = part(f"plain{r}")
-            nc.scalar.activation(plain[half, r][:], picked(r, halves[half]), COPY)
+        def fetch(r):
+            plain[r] = part(f"plain{r}")
+            nc.scalar.activation(plain[r][:], picked(r, halves[1]), COPY)
 
-        def weigh(half, r):
-            weighed[half, r] = part(f"weighed{half}{r}")
-            nc.vector.tensor_tensor(weighed[half, r][:], plain[half, r][:], gates[:, r, halves[half]], MULT)
+        def weigh(r):
+            weighed[r] = part(f"weighed{r}")
+            nc.vector.tensor_tensor(weighed[r][:], plain[r][:], gates[:, r, halves[1]], MULT)
 
         def add(target, first, second):
             nc.vector.tensor_tensor(target, first, second, ADD)
@@ -444,7 +438,7 @@ def tile_moe_tk_glu_sigmoid_kernel(
         plain = {}
         weighed = {}
         for r in range(TOP):
-            fetch(1, r)
+            fetch(r)
         for r in range(TOP - 1):
             fused(r)
         by_token = work.tile([P, 2, P], F32, name="by_token", align_bytes=64)
@@ -452,17 +446,17 @@ def tile_moe_tk_glu_sigmoid_kernel(
         back = a_bank([P, T // 2], 0)
         for x in range(2):
             nc.tensor.transpose(back[:, x * P : (x + 1) * P], by_token[:, x, :], ident[:])
-        weigh(1, 0)
-        weigh(1, 1)
+        weigh(0)
+        weigh(1)
         fourth = part("plain0")
         nc.vector.tensor_tensor(fourth[:], picked(TOP - 1, halves[0]), gates[:, TOP - 1, halves[0]], MULT)
-        weigh(1, 2)
+        weigh(2)
         two = part("two")
-        add(two[:], weighed[1, 0][:], weighed[1, 1][:])
-        weigh(1, TOP - 1)
+        add(two[:], weighed[0][:], weighed[1][:])
+        weigh(TOP - 1)
         three = part("three")
-        add(three[:], two[:], weighed[1, 2][:])
+        add(three[:], two[:], weighed[2][:])
         add(out_t[:, halves[0]], back[:], fourth[:])
         nc.sync.dma_start(out[:, halves[0]], out_t[:, halves[0]])
-        add(out_t[:, halves[1]], three[:], weighed[1, TOP - 1][:])
+        add(out_t[:, halves[1]], three[:], weighed[TOP - 1][:])
         nc.sync.dma_start(out[:, halves[1]], out_t[:, halves[1]])

from contextlib import ExitStack

import concourse.mybir as mybir
from concourse.masks import make_identity

F32 = mybir.dt.float32
BF16 = mybir.dt.bfloat16
I32 = mybir.dt.int32
U32 = mybir.dt.uint32
U16 = mybir.dt.uint16
U8 = mybir.dt.uint8
FP8X4 = mybir.dt.float8_e4m3fn_x4
FP4X4 = mybir.dt.float4_e2m1fn_x4
COPY = mybir.ActivationFunctionType.Copy
SIGMOID = mybir.ActivationFunctionType.Sigmoid
MULT = mybir.AluOpType.mult
ADD = mybir.AluOpType.add

P = 128
K, T, E, C, H, N, TOP = 1024, 512, 8, 256, 512, 128, 4
SLOTS = E * C
PASSES = K // 512
LAST = E - 1
FLOPS = 2 * SLOTS * (2 * K * H + H * N)

X_PIECES = ((0, 0, T // 2), (0, T // 2, T), (1, 0, T // 2), (1, T // 2, T))
VECTOR_CAST = (176, 176, 0, 96)
EARLY = 4
SHIFT_ROWS = ((0, 64), (64, 4), (96, 4))
OPENED_FIRST = (1, 4, 6)
BANK = 2048
A_BANKS = 3
B_BANKS = 4
GATHERED_BEHIND = {e: e - 3 if e < LAST else e - 2 for e in range(4, E)}

KB = 1024
AT_X_RAW = (12 * KB, 8 * KB, 4 * KB, 35 * KB)
AT_X_BF = (0, 16 * KB)
AT_SHIFTED = 36 * KB
AT_FIRST_WORDS = {
    (0, 0): 62 * KB,
    (1, 0): 4 * KB + 64,
    (0, 1): 34 * KB,
    (1, 1): 38 * KB,
}
AT_EARLY_BYTES = 44 * KB
AT_EARLY_SHIFTED = 11 * KB
AT_W3_FIRST_SCALES = 64
AT_LATE_SCALES = (12 * KB + 256, 4 * KB + 64)
AT_FIRST_CODES = {(0, 0): 56 * KB, (0, 1): 48 * KB, (1, 0): 42 * KB, (1, 1): 16 * KB}
AT_CODES = {2: 19 * KB, 3: 17 * KB, 4: 48 * KB + 512, 5: 19 * KB, 6: 17 * KB, 7: 19 * KB}
AT_BYTES = (45 * KB, 46 * KB, 48 * KB, 46 * KB)
AT_EXPERT_2 = 62 * KB
AT_EXPERT_3 = 56 * KB + 256
AT_EXPERT_4 = 32 * KB
AT_EXPERT_5 = AT_EXPERT_2
AT_EXPERTS_6_7 = AT_EXPERT_3 - 4 * KB
AT_W2_SCALES = AT_EXPERT_4
AT_W2 = AT_EXPERT_4 + KB
AT_GATES = 65 * KB + 768
AT_H_CODES = {0: AT_CODES[4], 2: 60 * KB + 256, 4: 80 * KB}


def tile_moe_tk_glu_sigmoid_kernel(
    tc, xT, w1_words, w1_scales, w3_words, w3_scales, w2_words, w2_scales, gate, offs, pos1, pos2, pos3, pos4, out
):
    nc = tc.nc
    with ExitStack() as ctx:
        lists = ctx.enter_context(tc.tile_pool(name="lists", bufs=1))
        places = ctx.enter_context(tc.tile_pool(name="places", bufs=1))
        keep = ctx.enter_context(tc.tile_pool(name="keep", bufs=1))
        work = ctx.enter_context(tc.tile_pool(name="work", bufs=4))
        psum = ctx.enter_context(tc.psum_pool(name="psum", bufs=1))

        def placed(shape, dtype, name, offset):
            return places.tile(shape, dtype, name=name, align_bytes=64, offset=offset)

        offs_t = lists.tile([P, SLOTS // 16], U16, name="offs_t")
        pos_t = [lists.tile([P, T // 16], U16, name=f"pos{r}_t") for r in range(TOP)]

        x_raw = [placed([P, 4, T // 2], F32, f"x_raw{i}", AT_X_RAW[i]) for i in range(len(X_PIECES))]
        x_bf = [placed([P, T, 4], BF16, f"x_bf{s}", AT_X_BF[s]) for s in range(PASSES)]
        x_codes = [keep.tile([P, T], U32, name=f"x_codes{s}", align_bytes=64) for s in range(PASSES)]
        x_bytes = keep.tile([P, 2 * T], U8, name="x_bytes", align_bytes=64)
        y_t = keep.tile([P, SLOTS], F32, name="y_t", align_bytes=64)
        out_t = keep.tile([P, T], F32, name="out_t", align_bytes=64)
        ident = keep.tile([P, P], F32, name="ident", align_bytes=64)

        def load_tokens(i):
            s, a, b = X_PIECES[i]
            nc.sync.dma_start(x_raw[i][:], xT[512 * s : 512 * (s + 1), a:b].rearrange("(p j) w -> p j w", j=4))

        load_tokens(0)
        load_tokens(1)
        nc.sync.dma_start(offs_t[:], offs)
        for r, src in enumerate((pos1, pos2, pos3, pos4)):
            nc.sync.dma_start(pos_t[r][:], src)
        w_scales = {}
        w_words = {}

        def load_scale_rows(plane, rows):
            for r in range(4):
                nc.sync.dma_start(plane[r:P:32], rows[r:16:4])

        def load_scales(m, e0, e1, room):
            planes = room.rearrange("p (g i) -> p g i", i=H)
            rows = (w1_scales, w3_scales)[m].bitcast(I32).rearrange("e s q i -> q (e s) i")
            load_scale_rows(planes.bitcast(I32), rows[:, e0 * PASSES : e1 * PASSES, :])
            for e in range(e0, e1):
                w_scales[m, e] = planes[:, (e - e0) * PASSES : (e - e0 + 1) * PASSES, :]

        def load_words(m, e0, e1, room):
            words = room.rearrange("p (g c) -> p g c", c=2 * H)
            src = (w1_words, w3_words)[m].bitcast(I32)[e0:e1].rearrange("e s p c -> p (e s) c")
            nc.sync.dma_start(words.bitcast(I32), src)
            for e in range(e0, e1):
                for s in range(PASSES):
                    w_words[m, e, s] = words[:, (e - e0) * PASSES + s, :]

        def load_first_words(m, e):
            load_words(m, e, e + 1, placed([P, PASSES * 2 * H], U8, f"first_words{m}{e}", AT_FIRST_WORDS[m, e])[:])

        def load_weights(e0, e1, name, offset):
            size = (e1 - e0) * PASSES * 2 * H
            room = placed([P, 2 * size], U8, name, offset)
            for m in range(2):
                load_words(m, e0, e1, room[:, m * size : (m + 1) * size])

        first_scales = keep.tile([P, EARLY * PASSES * H], U8, name="first_scales", align_bytes=64)
        nc.vector.memset(first_scales[:].bitcast(I32), 0)
        load_tokens(2)
        load_tokens(3)
        load_first_words(0, 0)
        load_scales(0, 0, EARLY, first_scales[:])

        nc.vector.memset(x_bytes[:].bitcast(I32), 0)
        upper = keep.tile([P, C], U8, name="early_upper", align_bytes=64)
        nc.vector.memset(upper[:].bitcast(I32), 0)
        make_identity(nc, ident[:])

        def cast(i, a, b, engine_copy):
            s, first = X_PIECES[i][0:2]
            engine_copy(
                x_bf[s][:, first + a : first + b, :].rearrange("p (c i) j -> p c j i", i=4),
                x_raw[i][:, :, a:b].rearrange("p j (c i) -> p c j i", i=4),
            )

        def quantize_tokens(i):
            s, a, b = X_PIECES[i]
            cast(i, VECTOR_CAST[i], b - a, nc.scalar.copy)
            if VECTOR_CAST[i]:
                cast(i, 0, VECTOR_CAST[i], nc.vector.tensor_copy)
            nc.vector.quantize_mx(
                out=x_codes[s][:, a:b].bitcast(FP8X4),
                scales=x_bytes[4 * (1 - s) : P, a:b],
                in_=x_bf[s][:, a:b].rearrange("p w j -> p (w j)"),
            )

        slot_codes = {}
        slot_bytes = {}

        def entries(first, count):
            return offs_t[:, first // 16 : (first + count) // 16]

        def shift(target, source):
            for row, rows in SHIFT_ROWS:
                nc.sync.dma_start(target[row : row + rows].bitcast(I32), source[row + 4 : row + 4 + rows].bitcast(I32))

        def gather_early_bytes():
            early = placed([P, C], U8, "early_bytes", AT_EARLY_BYTES)
            nc.vector.tensor_copy(early[:], x_bytes[:].indirect(entries(0, C)))
            moved = placed([P, C], U8, "early_shifted", AT_EARLY_SHIFTED)
            nc.vector.tensor_copy(upper[0:64].bitcast(I32), early[64:P].bitcast(I32))
            nc.sync.dma_start(moved[0:64].bitcast(I32), early[4:68].bitcast(I32))
            nc.sync.dma_start(moved[64:P].bitcast(I32), upper[4:68].bitcast(I32))
            slot_bytes[0, 0] = moved[:]

        def gather_bytes(e0):
            both = placed([P, 2 * C], U8, f"slot_bytes{e0}", AT_BYTES[e0 // 2])
            nc.vector.tensor_copy(both[:], x_bytes[:].indirect(entries(e0 * C, 2 * C)))
            skip = 1 if e0 == 0 else 0
            shift(shifted[:, (e0 + skip) * C : (e0 + 2) * C], both[:, skip * C :])
            for x in range(2):
                if x >= skip:
                    slot_bytes[0, e0 + x] = shifted[:, (e0 + x) * C : (e0 + x + 1) * C]
                slot_bytes[1, e0 + x] = both[:, x * C : (x + 1) * C]

        def gather_codes(s, e, codes):
            nc.vector.tensor_copy(codes, x_codes[s][:].indirect(entries(e * C, C)))
            for st in range(2):
                slot_codes[s, e, st] = codes[:, st * P : (st + 1) * P]

        def gather_first_codes(s, e):
            gather_codes(s, e, placed([P, C], U32, f"first_codes{s}{e}", AT_FIRST_CODES[s, e])[:])

        def gather_expert(e):
            codes = placed([P, PASSES * C], U32, f"slot_codes{e}", AT_CODES[e])
            for s in (0, 1) if e % 2 else (1, 0):
                gather_codes(s, e, codes[:, s * C : (s + 1) * C])

        quantize_tokens(0)
        quantize_tokens(1)
        gather_early_bytes()
        gather_first_codes(0, 0)
        gather_first_codes(0, 1)
        quantize_tokens(2)
        load_first_words(1, 0)
        load_scales(1, 0, EARLY, placed([P, EARLY * PASSES * H], U8, "w3_first_scales", AT_W3_FIRST_SCALES)[:])
        quantize_tokens(3)
        load_first_words(0, 1)
        load_first_words(1, 1)
        shifted = placed([P, SLOTS], U8, "shifted", AT_SHIFTED)
        gather_bytes(0)
        gather_first_codes(1, 0)
        gather_bytes(2)
        gather_first_codes(1, 1)

        h_tiles = {}
        uses = []

        def bank_tile(shape, number):
            uses.append(number)
            return psum.tile(shape, F32, name=f"bank{len(uses)}", offset=number * BANK)

        def a_bank(shape, count):
            if count == A_BANKS:
                return bank_tile(shape, A_BANKS + B_BANKS)
            return bank_tile(shape, (count - (count > A_BANKS)) % A_BANKS)

        def b_bank(shape, count):
            return bank_tile(shape, A_BANKS + count % B_BANKS)

        def multiply_1(e, st, m, s, bank, opens):
            nc.tensor.matmul_mx(
                out=bank[:],
                lhsT=slot_codes[s, e, st].bitcast(FP8X4),
                lhsT_scale=slot_bytes[s, e][:, st * P : (st + 1) * P],
                rhs=w_words[m, e, s].bitcast(FP4X4),
                rhs_scale=w_scales[m, e][:, s, :],
                start=opens,
                stop=not opens,
            )

        def sigmoid(bank):
            sig = work.tile([P, 2, P, 2], F32, name="sig", align_bytes=64)
            nc.scalar.activation(sig[:], bank[:].rearrange("s (p u d) -> s u p d", u=2, d=2), SIGMOID)
            return sig

        def product(e, st, bank, sig):
            h = work.tile([P, 2, P, 2], BF16, name="h", align_bytes=64, bufs=6)
            nc.vector.tensor_tensor(h[:], bank[:].rearrange("s (p u d) -> s u p d", u=2, d=2), sig[:], MULT)
            h_tiles[e, st] = h

        banks = {}

        def first_expert():
            for st in range(2):
                banks[0, st] = (a_bank([P, H], st), b_bank([P, H], st))
            for s in range(PASSES):
                for st in range(2):
                    multiply_1(0, st, 0, s, banks[0, st][0], s == 0)
            sigs = [sigmoid(banks[0, st][0]) for st in range(2)]
            for st in range(2):
                for s in range(PASSES):
                    multiply_1(0, st, 1, s, banks[0, st][1], s == 0)
                product(0, st, banks[0, st][1], sigs[st])

        def open_sums(e):
            for st in range(2):
                banks[e, st] = (a_bank([P, H], 2 * e + st), b_bank([P, H], 2 * e + st))
            for m in range(2):
                for st in range(2):
                    multiply_1(e, st, m, 1, banks[e, st][m], True)

        def first_layer(e):
            opened = e in OPENED_FIRST
            first = 1 if opened or e % 2 == 0 else 0
            if opened and e > 1:
                open_sums(e)
            for st in range(2):
                if not opened and e >= 2:
                    banks[e, st] = (a_bank([P, H], 2 * e + st), b_bank([P, H], 2 * e + st))
                for m in range(2):
                    if not opened and e >= 2:
                        multiply_1(e, st, m, first, banks[e, st][m], True)
                    multiply_1(e, st, m, 1 - first, banks[e, st][m], False)
                product(e, st, banks[e, st][1], sigmoid(banks[e, st][0]))

        def turn(e, tiles, count, h_bf):
            n = len(tiles) * P
            turned = a_bank([P, 2, n], count)
            for x, st in enumerate(tiles):
                words = h_tiles[e, st][:].rearrange("s u p d -> s (u p d)").bitcast(F32)
                for u in range(2):
                    nc.tensor.transpose(turned[:, u, x * P : (x + 1) * P], words[:, u * P : (u + 1) * P], ident[:])
            nc.scalar.copy(h_bf.bitcast(F32).rearrange("p (r u) -> p r u", u=2), turned[:].rearrange("p u r -> p r u"))

        def quantize_hidden(h_bf, e=None):
            n = h_bf.shape[1] // 4
            if e is None:
                h_codes = work.tile([P, n], U32, name="h_codes", align_bytes=64)
            else:
                h_codes = placed([P, n], U32, f"h_codes{e}", AT_H_CODES[e])
            h_bytes = work.tile([P, n], U8, name="h_bytes", align_bytes=64)
            nc.vector.quantize_mx(out=h_codes[:].bitcast(FP8X4), scales=h_bytes[:], in_=h_bf[:])
            return h_codes[:], h_bytes[:]

        def turn_and_quantize(e, tiles, count):
            h_bf = work.tile([P, 4 * P * len(tiles)], BF16, name="h_bf", align_bytes=64)
            turn(e, tiles, count, h_bf[:])
            return quantize_hidden(h_bf)

        hidden = {}
        turned_pairs = {}

        def turn_pair(e):
            h_bf = work.tile([P, 8 * C], BF16, name="h_bf", align_bytes=64)
            for x in range(2):
                turn(e + x, (0, 1), 2 * (e + 2) + x, h_bf[:, 4 * C * x : 4 * C * (x + 1)])
            turned_pairs[e] = h_bf

        def quantize_pair(e):
            h_codes, h_bytes = quantize_hidden(turned_pairs[e], e)
            for x in range(2):
                hidden[e + x] = (h_codes[:, x * C : (x + 1) * C], h_bytes[:, x * C : (x + 1) * C])

        w2 = {}

        def load_w2():
            w2["scales"] = placed([P, E, N], U8, "w2_planes", AT_W2_SCALES)[:]
            w2["words"] = placed([P, E, 2 * N], U8, "w2_codes", AT_W2)[:]
            load_scale_rows(w2["scales"].bitcast(I32), w2_scales.bitcast(I32).rearrange("e s q i -> q (e s) i"))
            nc.sync.dma_start(w2["words"].bitcast(I32), w2_words.bitcast(I32).rearrange("e s p c -> p (e s) c"))

        def multiply_2(e, target, h_codes, h_bytes):
            nc.tensor.matmul_mx(
                out=target,
                lhsT=w2["words"][:, e, :].bitcast(FP4X4),
                lhsT_scale=w2["scales"][:, e, :],
                rhs=h_codes.bitcast(FP8X4),
                rhs_scale=h_bytes,
                start=True,
                stop=True,
            )

        def second_layer_pair(e, y_bank):
            for x in range(2):
                multiply_2(e + x, y_bank[:, x * C : (x + 1) * C], *hidden[e + x])
            nc.scalar.copy(y_t[:, e * C : (e + 2) * C], y_bank[:])

        first_expert()
        load_weights(2, 3, "expert_2", AT_EXPERT_2)
        gather_expert(2)
        gather_expert(3)
        open_sums(1)
        load_weights(3, 4, "expert_3", AT_EXPERT_3)
        for m in range(2):
            room = placed([P, (E - EARLY) * PASSES * H], U8, f"late_scales{m}", AT_LATE_SCALES[m])
            load_scales(m, EARLY, E, room[:])
        for e in range(1, E):
            first_layer(e)
            if e % 2 == 0:
                if e == 4:
                    quantize_pair(0)
                if e == 6:
                    second_layer_pair(0, a_bank([P, 2 * C], A_BANKS))
                turn_pair(e - 2)
                if e == 6:
                    quantize_pair(4)
            if e == 1:
                gather_bytes(4)
            if e == 3:
                load_weights(6, 8, "experts_6_7", AT_EXPERTS_6_7)
                gather_bytes(6)
            for later, behind in GATHERED_BEHIND.items():
                if behind == e:
                    gather_expert(later)
            if e == 5:
                quantize_pair(2)
            if e == 1:
                load_weights(4, 5, "expert_4", AT_EXPERT_4)
            if e == 2:
                load_weights(5, 6, "expert_5", AT_EXPERT_5)
            if e == 4:
                load_w2()
            if e == 5:
                gates = placed([P, TOP, T], F32, "gates", AT_GATES)
                nc.sync.dma_start(gates[:], gate.rearrange("r p t -> p r t"))

        three_bf = work.tile([P, 4 * (C + P)], BF16, name="h_bf", align_bytes=64)
        turn(LAST - 1, (0, 1), 2 * LAST, three_bf[:, : 4 * C])
        turn(LAST, (0,), 2 * LAST + 2, three_bf[:, 4 * C :])
        h_codes, h_bytes = quantize_hidden(three_bf)
        second_layer_pair(2, b_bank([P, 2 * C], 2 * LAST))
        y_before = b_bank([P, C + P], 2 * LAST - 1)
        multiply_2(LAST - 1, y_before[:, 0:C], h_codes[:, :C], h_bytes[:, :C])
        multiply_2(LAST, y_before[:, C:], h_codes[:, C:], h_bytes[:, C:])
        nc.vector.tensor_copy(y_t[:, (LAST - 1) * C : LAST * C + P], y_before[:])
        last_hidden = turn_and_quantize(LAST, (1,), 2 * LAST + 1)
        second_layer_pair(4, a_bank([P, 2 * C], 2 * LAST))
        y_last = b_bank([P, P], 2 * LAST - 2)
        multiply_2(LAST, y_last[:], *last_hidden)
        nc.scalar.copy(y_t[:, LAST * C + P :], y_last[:])

        halves = (slice(0, T // 2), slice(T // 2, T))

        def picked(r, cols):
            return y_t[:].indirect(pos_t[r][:, cols.start // 16 : cols.stop // 16])

        def part(name):
            return keep.tile([P, T // 2], F32, name=name, align_bytes=64)

        def fused(r):
            values = part(f"fused{r}")
            nc.vector.tensor_tensor(values[:], picked(r, halves[0]), gates[:, r, halves[0]], MULT)
            for x in range(2):
                nc.tensor.matmul(
                    summed[:, x, :],
                    values[:, x * P : (x + 1) * P],
                    ident[:],
                    start=r == 0 and x == 0,
                    stop=r == TOP - 2 and x == 1,
                    is_transpose=True,
                )

        def fetch(r):
            plain[r] = part(f"plain{r}")
            nc.scalar.activation(plain[r][:], picked(r, halves[1]), COPY)

        def weigh(r):
            weighed[r] = part(f"weighed{r}")
            nc.vector.tensor_tensor(weighed[r][:], plain[r][:], gates[:, r, halves[1]], MULT)

        def add(target, first, second):
            nc.vector.tensor_tensor(target, first, second, ADD)

        summed = b_bank([P, 2, P], 0)
        plain = {}
        weighed = {}
        for r in range(TOP):
            fetch(r)
        for r in range(TOP - 1):
            fused(r)
        by_token = work.tile([P, 2, P], F32, name="by_token", align_bytes=64)
        nc.scalar.copy(by_token[:], summed[:])
        back = a_bank([P, T // 2], 0)
        for x in range(2):
            nc.tensor.transpose(back[:, x * P : (x + 1) * P], by_token[:, x, :], ident[:])
        weigh(0)
        weigh(1)
        fourth = part("plain0")
        nc.vector.tensor_tensor(fourth[:], picked(TOP - 1, halves[0]), gates[:, TOP - 1, halves[0]], MULT)
        weigh(2)
        two = part("two")
        add(two[:], weighed[0][:], weighed[1][:])
        weigh(TOP - 1)
        three = part("three")
        add(three[:], two[:], weighed[2][:])
        add(out_t[:, halves[0]], back[:], fourth[:])
        nc.sync.dma_start(out[:, halves[0]], out_t[:, halves[0]])
        add(out_t[:, halves[1]], three[:], weighed[TOP - 1][:])
        nc.sync.dma_start(out[:, halves[1]], out_t[:, halves[1]])
